import numpy as np, ml_dtypes
CORES = [40,41,42,43,44,45,46,47]
N = 8
BF = ml_dtypes.bfloat16
def gentries(a):
    return np.ascontiguousarray(a.reshape(8, 16, -1).transpose(0, 2, 1)).reshape(8, -1)
def gtable(e):
    e = np.asarray(e); return np.ascontiguousarray(e.reshape(8, -1, 16).transpose(0, 2, 1)).reshape(128, -1).astype(np.int32)
V, XW, L, RO, CAP, TH, EPS, LIM = 1536, 4096, 64, 6, 160, 72, 28, 15
def of(rng, lev, want):
    out = np.zeros(want.shape, np.int64)
    for q in range(N):
        for g in range(8):
            o = np.argsort(lev[q, g], kind="stable"); st = np.searchsorted(lev[q, g][o], np.arange(7))
            a, b = st[want[q, g]], st[want[q, g] + 1]
            out[q, g] = o[a + ((b - a) * rng.random(want[q, g].shape)).astype(np.int64)]
    return out
def parts(rng):
    lev = rng.integers(0, 5, (N, 8, XW)); lev = np.where(rng.random((N, 8, XW)) < rng.choice(np.array([0.1, 0.2, 0.35]), (N, 8, 1)), 5, lev)
    like = np.minimum(3 * lev[:, :, None, :] + rng.integers(0, 3, (N, 8, 16, 1)) + (rng.random((N, 8, 16, XW)) * rng.integers(1, 5, (N, 8, 1, XW))).astype(np.int64), 15)
    x = np.where(lev[:, :, None, :] == 5, rng.integers(0, 16, (N, 8, 16, XW)), like)
    own = lev[:, :, :V]; keep = rng.random((N, 8, V, 8)) < rng.choice(np.array([0.4, 0.75, 0.95]), (N, 8, V, 1))
    s = of(rng, own, np.where(keep, own[..., None], rng.integers(0, 6, (N, 8, V, 8))))
    p = np.where(rng.random((N, 8, V, 1)) < 0.12, of(rng, lev, np.zeros((N, 8, V, 8), np.int64)), rng.integers(0, XW, (N, 8, V, 8)))
    e = np.ascontiguousarray(np.concatenate([p, s], axis=3).transpose(0, 1, 3, 2))
    v = rng.integers(0, V, (N, 8, L)); v = np.where(rng.random((N, 8, L)) < 0.2, np.take_along_axis(v, rng.integers(0, L, (N, 8, L)), 2), v)
    return e, x, v, rng.integers(0, 256, (N, 8, 16))
def pack(e, x, v, w):
    return {"e0": np.ascontiguousarray(e).reshape(N, 128, V).astype(np.int32), "x0": np.ascontiguousarray(x).reshape(N, 128, XW).astype(np.float32).astype(BF),
            "v0": np.stack([gtable(a) for a in v]), "wt": np.ascontiguousarray(w).reshape(N, 128, 1).astype(np.int32)}
def node(e, v, p, s):
    e[:8, v] = p; e[8:, v] = s
def place(w, c):
    u = int(np.add.reduce(w * c)) & (XW - 1)
    return ((u * u >> 5) + u) & (XW - 1)
def total(rng, s):
    o = np.full(16, s >> 4); o[rng.permutation(16)[:s & 15]] += 1; a = rng.permutation(16)
    for i in range(8):
        m = int(rng.integers(0, min(int(o[a[2 * i]]), 15 - int(o[a[2 * i + 1]])) + 1)); o[a[2 * i]] -= m; o[a[2 * i + 1]] += m
    return o
def away(rng, c, d):
    o = c.copy()
    for r in rng.permutation(16):
        k = int(c[r]); s = min(d, max(k, 15 - k)); o[r] = k + s if 15 - k >= k else k - s; d -= s
    return o
def fan(rng, e, nd, n, pr, far, fit):
    for i in range(7):
        s = np.full(8, fit); s[rng.permutation(8)[:n // 7 + int(i < n % 7)]] = far; node(e, nd[i], pr, s)
def setup_inputs(rng):
    return pack(*parts(rng))
def setup_inputs_corners(rng):
    e, x, v, w = parts(rng); w = np.maximum(w, 1); goal = (CAP, CAP + 1, CAP - 1, 0, 8 * L, 1, CAP, 8)
    for q in range(N):
        for g in range(8):
            eg, xg, wg = e[q, g], x[q, g], w[q, g]
            a1, a0 = total(rng, TH), total(rng, TH - 1); ha = place(wg, a1)
            for i in range(64):
                m1 = total(rng, TH + 40); hm = place(wg, m1)
                if hm != ha: break
            c = rng.permutation(V); c = c[(c != ha) & (c != hm)]
            cb, ca, cz, cm, cp, cf, cx = c[:7]
            xg[:, ha] = away(rng, a1, EPS + 1); xg[:, hm] = away(rng, m1, EPS)
            xg[:, cb] = 15; xg[:, ca] = a1; xg[:, cz] = a0; xg[:, cm] = m1
            xg[:, cp] = total(rng, 120); xg[:, cf] = away(rng, xg[:, cp], EPS); xg[:, cx] = away(rng, xg[:, cp], EPS + 1)
            nd = rng.permutation(V)
            for k in range(9):
                node(eg, nd[k], np.where(rng.permutation(8) < k, ca, rng.choice(np.array([cm, cz]), 8)), rng.integers(0, V, 8))
            node(eg, nd[9], cz, rng.integers(0, V, 8)); node(eg, nd[10], cm, cp)
            fan(rng, eg, nd[11:18], LIM, cm, cx, cf); fan(rng, eg, nd[18:25], LIM + 1, cm, cx, cf)
            at = nd[25:25 + L]; n = goal[(q + g) % 8]
            kind = rng.choice(np.array([0, 9, 10, 11]), L); kind[:n // 8] = 8
            if n % 8: kind[n // 8] = n % 8
            kind = rng.permutation(kind)
            for l in range(L):
                k = int(kind[l])
                s = np.full(8, nd[k]) if k < 10 else np.concatenate([nd[10:11], nd[11:18] if k == 10 else nd[18:25]])
                node(eg, at[l], cb, s)
            v[q, g] = at
    return pack(e, x, v, w)
def setup_inputs_crowd(rng):
    e, x, v, w = parts(rng); w = np.maximum(w, 1); w[2, 4] = 0
    for q in range(N):
        for g in range(8):
            eg, xg, wg = e[q, g], x[q, g], w[q, g]
            h = place(wg, np.full(16, 15)); c = XW // 4 + rng.permutation(V - XW // 4); c = c[c != h]
            cb, cp, cq = c[:3]; dd = c[3:11]; na, nb, nc, turn, hold = c[11:16]; lo = rng.integers(0, 4, 16)
            xg[:, h] = 0; xg[:, cb] = 15; xg[:, cp] = lo; xg[:, dd] = lo[:, None]; xg[:, cq] = rng.integers(12, 16, 16)
            node(eg, na, cb, dd); node(eg, nb, cb, cq); node(eg, nc, cb, c[16:24])
            node(eg, turn, cb, np.array([na] + 7 * [nb])); node(eg, hold, cb, nc)
            node(eg, dd[0], cb, cp); fan(rng, eg, dd[1:], LIM + 7, cb, cq, cp)
            o = np.full(L, hold); any2 = rng.integers(0, V, 2); k = (q + g) % 6
            if q < 2:
                o[:] = turn
                if q == 1 and g == 7: o[L - 1] = hold
            elif k == 1: o[L - 1] = turn
            elif k == 2: o[rng.integers(0, L)] = any2[0]
            elif k == 3: o = rng.choice(np.array([turn, hold, any2[0], any2[1]]), L)
            elif k == 4: o[:] = any2[0]
            elif k == 5: o[:] = any2[0]; o[0] = any2[1]
            v[q, g] = o
    return pack(e, x, v, w)
def tips(rng, n, shape, a, b):
    r = rng.random(shape)
    return np.where(r < a, 0, np.where(r < a + b, n - 1, rng.integers(0, n, shape)))
def setup_inputs_ends(rng):
    pops = np.array([0, 4, 7, 10, 13, 16]); lev = rng.integers(0, 6, (N, 8, XW)); row = np.argsort(rng.random((N, 8, 16)), axis=-1)
    lev[..., 0] = np.where(np.arange(8) % 2 == 0, 4, 1); lev[..., V - 1] = 2; lev[..., XW - 1] = 5
    flip = (rng.random((N, 8, 1, XW)) < 0.5) & (np.arange(16)[:, None] == rng.integers(0, 16, (N, 8, 1, XW))); flip[..., [0, V - 1, XW - 1]] = False
    x = 15 * ((row[..., None] < pops[lev][:, :, None, :]) ^ flip).astype(np.int64)
    e = np.concatenate([tips(rng, XW, (N, 8, 8, V), 0.45, 0.45), tips(rng, V, (N, 8, 8, V), 0.45, 0.35)], axis=2)
    v = tips(rng, V, (N, 8, L), 0.35, 0.45); w = 255 * rng.integers(0, 2, (N, 8, 16)); w[:, 7] = 255
    for q in range(N):
        node(e[q, 7], V - 1, XW - 1, 0); node(e[q, 7], 0, XW - 1, np.array([V - 1, 0] * 4)); v[q, 7] = V - 1
        x[q, 7, :, place(w[q, 7], np.full(16, 15))] = 0
        node(e[q, 6], V - 2, XW - 1, np.array([V - 3] + [V - 4] * 7)); node(e[q, 6], V - 3, XW - 1, 0); node(e[q, 6], V - 4, XW - 1, V - 1)
        v[q, 6, 0] = V - 2; v[q, 6, L - 2:] = V - 2
    return pack(e, x, v, w)
def setup_inputs_quiet(rng):
    e, x, v, w = parts(rng); w = np.maximum(w, 1)
    for q in range(N):
        few = rng.permutation(8 * L).reshape(8, L) < 7 + 8 * int(rng.integers(0, L))
        for g in range(8):
            eg, xg = e[q, g], x[q, g]
            for i in range(64):
                h = place(w[q, g], np.full(16, 15))
                if h >= XW // 4: break
                w[q, g] = rng.integers(1, 256, 16)
            c = XW // 4 + rng.permutation(V - XW // 4); c = c[c != h]
            cb, cz = c[:2]; xg[:, h] = 0; xg[:, cb] = 15; xg[:, cz] = 0
            if q % 2 == 0:
                z, asks, mids = c[2:10], c[10:18], c[18:26]; y1, y2, y3, ask0, mid0, ask4 = c[26:32]
                for k in range(8):
                    node(eg, z[k], cz, rng.choice(z, 8)); node(eg, asks[k], cb, mids[k]); node(eg, mids[k], cb, np.roll(z, k))
                node(eg, ask0, cb, mid0); node(eg, mid0, cb, y1); node(eg, y1, cz, y2); node(eg, y2, cz, y3); node(eg, y3, cz, ask4); node(eg, ask4, cb, mids[0])
                v[q, g] = asks[rng.integers(0, 8, L)]; v[q, g, int(rng.integers(1, CAP // 8))] = ask0
            else:
                cp, cq, na, nb, turn, first, idle = c[2:9]; dd = c[9:17]; lo = rng.integers(0, 4, 16)
                xg[:, cp] = lo; xg[:, dd] = lo[:, None]; xg[:, na] = lo; xg[:, nb] = lo; xg[:, cq] = rng.integers(12, 16, 16)
                node(eg, na, cb, dd); node(eg, nb, cb, cq); node(eg, dd[0], cb, cp); fan(rng, eg, dd[1:], LIM + 7, cb, cq, cp)
                node(eg, turn, cb, np.array([nb] + 7 * [na])); node(eg, first, cb, np.array([turn] + 7 * [nb])); node(eg, idle, cz, turn)
                v[q, g] = np.where(few[g], first, idle)
    return pack(e, x, v, w)
def setup_inputs_spread(rng):
    full = rng.random((N, 8, 1, XW)) < rng.choice(np.array([0.3, 0.6, 1.0]), (N, 8, 1, 1))
    x = np.minimum((rng.random((N, 8, 16, XW)) * np.where(full, 16, rng.integers(1, 17, (N, 8, 1, XW)))).astype(np.int64), 15)
    s = np.minimum((V * rng.random((N, 8, 8, V)) ** rng.choice(np.array([1.0, 2.0]), (N, 8, 1, 1))).astype(np.int64), V - 1)
    e = np.concatenate([rng.integers(0, XW, (N, 8, 8, V)), s], axis=2)
    v = np.minimum((V * rng.random((N, 8, L)) ** rng.choice(np.array([1.0, 3.0]), (N, 8, 1))).astype(np.int64), V - 1)
    w = np.minimum(np.exp2(8 * rng.random((N, 8, 16))).astype(np.int64) - 1, 255)
    return pack(e, x, v, w)
def check_inputs(d):
    bad = []
    for k, lo, hi in (("e0", 0, XW - 1), ("x0", 0, 15), ("v0", 0, V - 1), ("wt", 0, 255)):
        a = np.asarray(d[k]).astype(np.float64)
        if not np.all((a >= lo) & (a <= hi)): bad.append("range of " + k)
    if np.max(np.asarray(d["e0"]).reshape(-1, 16, V)[:, 8:]) >= V: bad.append("range of the subs in e0")
    a = np.asarray(d["x0"]).astype(np.float32)
    if np.any(a != np.floor(a)): bad.append("whole numbers in x0")
    return bad
def reference(e0, x0, v0, wt):
    M = 8 * N
    E = np.ascontiguousarray(e0.reshape(M, 16, V).transpose(0, 2, 1)).astype(np.int64)
    X = np.ascontiguousarray(x0.astype(np.float32).reshape(M, 16, XW).transpose(0, 2, 1)).astype(np.int32)
    v = np.stack([gentries(a) for a in v0]).reshape(M, L).astype(np.int64); w = wt.reshape(M, 1, 1, 16).astype(np.int32)
    k = np.arange(M); k1, k2, k3 = k[:, None], k[:, None, None], k[:, None, None, None]
    A = np.zeros((M, 1), np.int64); lower = np.arange(L)[None, :] < np.arange(L)[:, None]
    for t in range(RO):
        c = E[k1, v]; p, s = c[..., :8], c[..., 8:]
        c = E[k2, s]; pp, ss = c[..., :8], c[..., 8:]
        m = np.minimum(X[k2, p][:, :, :, None, :], X[k3, pp])
        alive = np.add.reduce(m, axis=4) >= TH
        full = np.any(alive, axis=2); first = np.argmax(alive, axis=2)
        sub = np.take_along_axis(ss, first[:, :, None, :], 2)[:, :, 0]
        far = np.add.reduce(np.abs(X[k3, ss] - X[k2, sub][:, :, None]), axis=4) > EPS
        pi = np.max(np.where((alive & ~far)[..., None], m, 0), axis=2)
        stand = np.add.reduce((alive & far).astype(np.int64), axis=(2, 3)) <= LIM + (A & 7)
        u = np.add.reduce(w * pi, axis=3).astype(np.int64) & (XW - 1); h = ((u * u >> 5) + u) & (XW - 1)
        known = np.add.reduce(np.abs(X[k2, h] - pi), axis=3) <= EPS
        new = XW // 4 * (t & 3) + np.arange(8 * L).reshape(L, 8); name = np.where(known, h, new)
        ask = stand[:, :, None] & full & ~known
        one = ask.reshape(M, 8 * L).astype(np.int64); before = (np.add.accumulate(one, axis=1) - one).reshape(M, L, 8)
        k4 = (k // 8 + 1 + t % (N - 1)) % N * 8 + k % 8
        got = X[k4[:, None, None], h]
        val = np.where((ask & (before < CAP))[..., None], (pi + got) >> 1, pi)
        best = np.argmax(np.where(full, np.add.reduce(pi, axis=3), -1), axis=2)
        go = np.where(stand & np.any(full, axis=2), np.take_along_axis(sub, best[..., None], 2)[..., 0], s[:, :, t])
        lead = stand & ~np.any((v[:, :, None] == v[:, None, :]) & stand[:, None, :] & lower, axis=2)
        pair = np.concatenate([np.where(full, name, p), np.where(full, sub, s)], axis=2)
        a, l = np.nonzero(lead); E[a, v[a, l]] = pair[a, l]
        a, l, j = np.nonzero(ask); X[a, new[l, j]] = val[a, l, j]
        A = np.repeat(np.add.reduce((~stand).reshape(N, 8 * L).astype(np.int64), axis=1), 8)[:, None]; v = go
    return {"ye": np.ascontiguousarray(E.transpose(0, 2, 1)).reshape(N, 128, V).astype(np.float32),
            "yx": np.ascontiguousarray(X.transpose(0, 2, 1)).reshape(N, 128, XW).astype(np.float32).astype(BF),
            "yv": np.stack([gtable(a) for a in v.reshape(N, 8, L)]).astype(np.float32)}

@@ -1,0 +1,825 @@
+import numpy as np
+from concourse.mybir import AluOpType, ActivationFunctionType
+import comms_topo
+
+ALU = AluOpType
+ACT = ActivationFunctionType
+NR, V_N, XW, RO = 8, 1536, 4096, 6
+TH4 = 72 * 4096
+C0 = TH4 - 2048
+PAR = {
+    "L": [0, 8, 32],
+    "X": [0, 8, 16, 24, 32],
+    "XE": ["VVV", "VVG", "VGG", "VGG"],
+    "M": [0, 4, 8, 12, 16, 20, 24, 28, 32],
+    "N": [0, 4, 8, 12, 16, 20, 24, 28, 32],
+    "A": [0, 8, 16, 24, 32],
+    "B": [0, 8, 16, 24, 32],
+    "BE": "SVVV",
+    "T": [0, 32],
+    "old": "D", "spp": True, "rec": "S", "k1": "S", "NE": "SSSSSSSS", "pre": True, "uso": False, "dd": 16,
+    "bias": {0: -800, 1: -800, 7: 4000, 8: 4000, 9: 4000, 10: 4000, 18: 4000, 21: 4000, 24: -800, 25: -4800, 26: -800, 27: -1600, 28: -800, 29: -800, 30: -800, 31: -800, 33: -300, 34: 800, 35: 4800, 36: 800, 37: 800, 45: -800, 46: -800, 47: -4800, 48: -4800, 49: -4800, 50: -800, 51: 4000, 53: -4000, 54: -3200, 56: 4000, 57: 3200, 58: -800, 59: -4000, 71: 4000, 72: 4000, 74: -2000, 75: -2800, 76: 1200, 77: -2800, 78: -4000, 80: 3700, 81: -300, 83: 800, 84: 800, 85: 800, 86: 800, 87: 800, 88: 800, 89: 800, 90: 800, 93: 800, 94: 800, 95: -4000, 96: -4000, 97: -4000, 98: -4000, 105: -300, 108: -300, 109: -4300, 110: 4000, 111: -300, 119: 4000, 120: 4000, 121: -800, 122: 3200, 124: 800, 128: -300, 129: -300, 130: -300, 131: -300, 132: -300, 143: -300, 144: -600, 145: -300, 146: -300, 147: -300, 159: -2000, 160: -2000, 161: -2000, 162: -2000, 164: 2000, 165: 2000, 166: 4000, 167: 4000, 169: 800, 170: 800, 171: 800, 172: 800, 175: -800, 176: -4800, 177: -800, 178: -800, 179: 800, 180: 800, 181: 800, 182: 800, 184: 4000, 186: -800, 187: -4800, 188: -4000, 189: -4000, 190: -4000, 192: 4000, 193: -6000, 194: -2000, 195: -2000, 196: -4000, 201: -800, 202: -800, 1020: -2000, 1021: 2000, 1024: -2000, 1025: -2000, 1026: -2000, 1027: -2000, 1034: 500, 1035: 800, 1036: 4800, 1037: 800, 1041: 2000, 1045: 2000, 1046: 2000, 1051: -4000, 1053: -300, 1055: -2000, 1056: -2000, 1057: -2000, 1058: -2000, 1059: 7700, 1060: 4000, 1061: 4000, 1062: 4000, 1063: -2000, 1064: -2000, 1065: -1200, 1066: -2000, 1072: 2000},
+}
+PAR["bias"].update({8: 0, 40: 2000, 41: 2000, 49: -5100, 50: -1100, 51: 3700, 52: -300, 69: 4000, 70: 4000, 71: 6000, 81: -4300, 82: -4000, 100: -2000, 101: -6000, 135: -300, 136: -300, 137: -300, 138: -300, 178: -2800, 179: -3200, 180: 4800, 1026: 2000, 1027: 2000, 1028: 4000, 1029: 4000, 1030: -300, 1031: -300, 1036: 6800, 1037: 2800, 1038: 2000, 1039: 2000, 1045: 4800, 1046: 2800, 1047: 4800, 1048: 800, 1072: 0})
+PAR.update({"X": [0, 8, 20, 32], "XE": ["VVVVVVSG", "VVVVGGGG", "GGGGGGGG"]})
+PAR["bias"] = {3: -300, 4: -300, 5: -300, 6: -300, 7: 2000, 8: 2000, 9: 2000, 10: 2000, 14: 300, 15: -1700, 16: 4300, 18: 3700, 19: 4000, 20: 4000, 21: 4000, 24: -1600, 25: -1600, 26: 3200, 27: 3200, 28: -2000, 30: -800, 31: -800, 37: 4000, 39: -4000, 40: -4000, 41: -4000, 46: -4000, 47: -4000, 48: -4000, 50: 2000, 51: -6300, 52: -6300, 53: -6300, 54: -4300, 56: 4000, 57: 4000, 58: 5200, 59: 5200, 60: 1200, 61: 2000, 65: -4000, 66: -800, 68: 800, 69: 800, 70: 800, 71: 800, 75: -2000, 76: -1200, 77: 800, 78: -3200, 79: 800, 80: 800, 81: 800, 83: 2000, 84: 2000, 85: 2000, 86: 2000, 93: -600, 94: -300, 98: 4000, 102: 800, 103: 800, 104: 800, 109: -300, 111: 800, 116: 800, 117: 800, 118: -300, 120: -500, 121: -500, 122: 300, 125: -800, 126: 300, 128: -300, 129: 1600, 130: 800, 145: -2000, 147: 2000, 152: 4000, 153: 2000, 154: 2000, 155: 2000, 156: 2000, 160: 2000, 161: 2000, 162: 2000, 163: 2000, 189: -4000, 190: -4800, 191: -4500, 192: 300, 193: -3700, 194: 300, 211: -300, 212: -300, 213: -300, 214: -300, 217: -800, 218: -800, 219: -800, 220: -800, 1007: -6000, 1008: -2000, 1009: -2000, 1010: -2000, 1048: 3200, 1049: 4000, 1050: 4000, 1051: 4000, 1053: 4000, 1054: 8000, 1055: 8000, 1056: 6000, 1057: 8000, 1058: 4000, 1060: 2000, 1061: 2000, 1062: 2000, 1063: 2000}
+SAME_WAR = True
+KEYS = []
+
+
+def cuts(k):
+    return list(zip(PAR[k][:-1], PAR[k][1:]))
+
+SCRATCH = {
+    "X": ("sbuf", [128, XW], "bfloat16"), "XR": ("sbuf", [128, RO * XW], "bfloat16"),
+    "Ei": ("sbuf", [128, V_N], "int32"), "E": ("sbuf", [128, V_N + 64], "float32"),
+    "vi": ("sbuf", [128, 4], "int32"), "wi": ("sbuf", [128, 1], "int32"),
+    "vL": ("sbuf", [128, 8], "uint16"), "v128": ("sbuf", [128, 8], "float32"),
+    "c1h": ("sbuf", [128, 64], "float16"), "c1f": ("sbuf", [128, 64], "float32"),
+    "L1": ("sbuf", [128, 64], "uint16"), "pC": ("sbuf", [128, 32], "float32"), "sC": ("sbuf", [128, 32], "float32"),
+    "Xp": ("sbuf", [128, 512], "bfloat16"), "c2h": ("sbuf", [128, 512], "float16"),
+    "c128": ("sbuf", [128, 512], "bfloat16"),
+    "L2": ("sbuf", [128, 512], "uint16"), "Spp": ("sbuf", [128, 256], "float32"),
+    "dS": ("sbuf", [128, 32], "float16"),
+    "Xpb": ("sbuf", [128, XW], "bfloat16"), "m": ("sbuf", [128, XW], "bfloat16"),
+    "Gs": ("sbuf", [128, XW], "bfloat16"), "absd": ("sbuf", [128, XW], "bfloat16"),
+    "Fb": ("sbuf", [128, XW], "bfloat16"), "SO": ("sbuf", [128, XW], "bfloat16"),
+    "dead": ("sbuf", [128, 256], "bfloat16"), "lo": ("sbuf", [128, 256], "float32"),
+    "st": ("sbuf", [128, 256], "float32"), "subl": ("sbuf", [128, 32], "uint16"),
+    "nXs": ("sbuf", [128, 512], "bfloat16"), "ok": ("sbuf", [128, 256], "bfloat16"),
+    "I16": ("sbuf", [128, 128], "float16"), "n16": ("sbuf", [128, 32], "float16"),
+    "Z": ("sbuf", [128, 3 * 1536], "bfloat16"), "ns": ("sbuf", [128, 32], "bfloat16"),
+    "ha": ("sbuf", [128, 192], "int32"), "hl": ("sbuf", [128, 32], "uint16"),
+    "dd": ("sbuf", [128, 512], "bfloat16"), "ad": ("sbuf", [128, 512], "bfloat16"), "sm": ("sbuf", [128, 512], "bfloat16"),
+    "tf": ("sbuf", [128, 512], "float32"), "ask": ("sbuf", [128, 32], "bfloat16"), "cum": ("sbuf", [128, 32], "bfloat16"),
+    "idx": ("sbuf", [128, 32], "uint16"), "pr": ("sbuf", [128, 64], "float32"),
+    "U": ("sbuf", [128, 64], "float32"), "AB": ("sbuf", [128, 256], "float32"), "fm": ("sbuf", [128, 256], "float32"),
+    "lf": ("sbuf", [128, 16], "float32"), "off": ("sbuf", [128, 4], "uint16"),
+    "gi": ("sbuf", [128, 16], "int32"), "af": ("sbuf", [128, 40], "float32"), "thr": ("sbuf", [128, 2], "float32"),
+    "yvs": ("sbuf", [128, 8], "float32"),
+    "pi": ("sbuf", [128, 8], "int32"), "col": ("sbuf", [128, 32], "float32"),
+    "D1": ("sbuf", [128, 144], "float32"), "D16": ("sbuf", [128, 128], "float32"), "D8": ("sbuf", [128, 128], "float32"),
+    "cc": ("sbuf", [128, 64], "float32"), "lq": ("sbuf", [128, 64], "float32"),
+    "I": ("sbuf", [128, 128], "bfloat16"), "In": ("sbuf", [128, 128], "bfloat16"),
+    "W4": ("sbuf", [128, 144], "bfloat16"), "Wn": ("sbuf", [128, 144], "bfloat16"), "Ww": ("sbuf", [128, 144], "bfloat16"),
+    "Lo16": ("sbuf", [128, 144], "float16"), "Hi16": ("sbuf", [128, 144], "float16"),
+    "Lo32": ("sbuf", [128, 144], "float32"), "Hi32": ("sbuf", [128, 144], "float32"),
+    "RP": ("sbuf", [128, 144], "float16"), "RS": ("sbuf", [128, 144], "float16"),
+    "G0": ("sbuf", [128, 144], "float32"), "G1": ("sbuf", [128, 144], "float32"),
+    "P0": ("sbuf", [128, 144], "float32"), "P1": ("sbuf", [128, 144], "float32"),
+    "B16": ("sbuf", [128, 128], "bfloat16"), "B8": ("sbuf", [128, 128], "bfloat16"),
+    "TL": ("sbuf", [128, 128], "bfloat16"), "TL0": ("sbuf", [128, 128], "bfloat16"),
+    "Sel": ("sbuf", [128, 2048], "bfloat16"), "rs8": ("sbuf", [128, 2048], "bfloat16"),
+    "rsB": ("sbuf", [128, 256], "float32"), "c89": ("sbuf", [128, 128], "bfloat16"), "one": ("sbuf", [128, 128], "bfloat16"),
+    "IO": ("sbuf", [128, V_N], "float32"), "nC": ("sbuf", [128, 128], "float32"), "nC0": ("sbuf", [128, 128], "float32"),
+    "RL": ("sbuf", [128, 32], "uint16"), "lL": ("sbuf", [128, 32], "float32"), "mk": ("sbuf", [128, 16], "float32"),
+    "wb": ("sbuf", [128, 2], "bfloat16"),
+    "b0": ("psum", [128, 4, 8, 16], "float32"), "b1": ("psum", [128, 4, 8, 16], "float32"),
+    "b2": ("psum", [128, 512], "float32"), "b3": ("psum", [128, 512], "float32"),
+    "b4": ("psum", [128, 512], "float32"), "b5": ("psum", [128, 512], "float32"),
+    "b6": ("psum", [128, 512], "float32"), "b7": ("psum", [128, 64, 8], "float32"),
+}
+SEMAPHORES = (["cz", "ca", "cv", "cs", "cp", "cg", "ld0", "ld1", "ld2", "ld3", "st0", "st1", "st2", "st3", "st4"]
+              + ["snt%d" % t for t in range(RO)] + ["arr%d" % t for t in range(RO)])
+COUNTER = {"V": "cv", "S": "cs", "P": "cp", "G": "cg"}
+TWO = ("bfloat16", "float16", "uint16")
+CM = {"v0": 64, "s0": 80, "g0": 200, "gat": 1.5, "sca": 3.8, "pe": 0.5, "pe0": 0, "x": 110, "same": 60, "tt": 2.0}
+S_ = slice
+
+
+def R(name, a=None, b=None, s=None):
+    return (name, (S_(a, b, s),))
+
+
+def IND(name, a, b, lst):
+    return ("ind", R(name, a, b), lst)
+
+
+def cols(ref):
+    shape = SCRATCH[ref[0]][1][1:]
+    return np.arange(int(np.prod(shape))).reshape(shape)[ref[1]].ravel()
+
+
+def dtp(ref):
+    return SCRATCH[ref[1][0] if ref[0] == "ind" else ref[0]][2]
+
+
+def is_ref(x):
+    return isinstance(x, tuple)
+
+
+def ap(T, x):
+    if not is_ref(x):
+        return x
+    if x[0] == "ind":
+        return ap(T, x[1]).indirect(ap(T, x[2]))
+    return T[x[0]][(S_(None),) + x[1]]
+
+
+def count(ref):
+    return 16 * len(cols(ref[2])) if ref[0] == "ind" else len(cols(ref))
+
+
+def build():
+    ops = []
+    hist = {}
+    bank = {}
+
+    def add(eng, cost, emit, rd, wr, sig=None, lat=0, ext=()):
+        me = len(ops)
+        deps = {}
+        reads, writes = [], []
+        for r in rd:
+            if is_ref(r):
+                reads += [r[1], r[2]] if r[0] == "ind" else [r]
+        for w in wr:
+            if w[0] == "ind":
+                writes.append(w[1])
+                reads.append(w[2])
+            else:
+                writes.append(w)
+        for kind, refs in (("r", reads), ("w", writes)):
+            for r in refs:
+                name = r[0]
+                if SCRATCH[name][0] == "psum":
+                    last = bank.setdefault(name, {})
+                    for e, o in last.items():
+                        if o != me and (e != eng or eng == "P"):
+                            deps[o] = deps.get(o, False) or e != eng
+                    if eng in last and last[eng] != me and eng != "P":
+                        deps.setdefault(last[eng], False)
+                    last[eng] = me
+                    continue
+                mask = np.zeros(int(np.prod(SCRATCH[name][1][1:])), bool)
+                mask[cols(r)] = True
+                keep = []
+                for o, k, mk in hist.setdefault(name, []):
+                    hit = o != me and (k == "w" or kind == "w") and bool(np.any(mk & mask))
+                    if hit:
+                        deps[o] = deps.get(o, False) or (k == "w" and kind == "r") or SAME_WAR
+                    if not (kind == "w" and o != me and not np.any(mk & ~mask)):
+                        keep.append((o, k, mk))
+                keep.append((me, kind, mask))
+                hist[name] = keep
+        ops.append({"eng": eng, "cost": cost, "emit": emit, "deps": deps, "sig": sig, "lat": lat, "ext": ext})
+        return me
+
+    def vcost(out, ins):
+        n = count(ins[0])
+        if ins[0][0] == "ind":
+            return CM["v0"] + CM["gat"] * n
+        if out[0] == "ind":
+            return CM["v0"] + CM["sca"] * n
+        return CM["v0"] + n * (0.5 if all(dtp(x) in TWO for x in [out] + ins) else 1.0)
+
+    def ts(out, a, s1, op0, s2=None, op1=None):
+        def emit(g, T):
+            if op1 is None:
+                return [g.vector.tensor_scalar(ap(T, out), ap(T, a), ap(T, s1), None, op0)]
+            return [g.vector.tensor_scalar(ap(T, out), ap(T, a), ap(T, s1), ap(T, s2), op0, op1)]
+        return add("V", vcost(out, [a]), emit, [a, s1, s2], [out])
+
+    def tt(out, a, b, op, ext=()):
+        c = vcost(out, [a, b])
+        if a[0] != "ind":
+            c = CM["v0"] + count(a) * (1.0 if "psum" in (SCRATCH[a[0]][0], SCRATCH[b[0]][0]) else CM["tt"])
+        return add("V", c, lambda g, T: [g.vector.tensor_tensor(ap(T, out), ap(T, a), ap(T, b), op)], [a, b], [out], ext=ext)
+
+    def cp(out, a):
+        return add("V", vcost(out, [a]), lambda g, T: [g.vector.tensor_copy(ap(T, out), ap(T, a))], [a], [out])
+
+    def scan(out, a, b, op0, op1, first=0.0):
+        return add("V", vcost(out, [a, b]),
+                   lambda g, T: [g.vector.tensor_tensor_scan(ap(T, out), ap(T, a), ap(T, b), ap(T, first), op0, op1)],
+                   [a, b, first], [out])
+
+    def mset(out, val):
+        return add("V", vcost(out, [out]), lambda g, T: [g.vector.memset(ap(T, out), val)], [], [out])
+
+    def act(out, a, func, bias=0.0, scale=1.0, acc=None):
+        def emit(g, T):
+            if acc is not None:
+                return [g.scalar.activation(ap(T, out), ap(T, a), func, bias=ap(T, bias), scale=scale, accum_out=ap(T, acc))]
+            return [g.scalar.activation(ap(T, out), ap(T, a), func, bias=ap(T, bias), scale=ap(T, scale))]
+        c = CM["s0"] + count(a) * (CM["gat"] if a[0] == "ind" else 1.0) + (25 if acc else 0)
+        return add("S", c, emit, [a, bias, scale], [out] + ([acc] if acc else []))
+
+    def mm(seq):
+        def emit(g, T):
+            res = []
+            for o, l, r, a, b in seq:
+                i = g.tensor.matmul(ap(T, o), ap(T, l), ap(T, r), a, b)
+                if b or (o, l, r, a, b) == seq[-1]:
+                    res.append(i)
+            return res
+        c = sum(CM["pe0"] + CM["pe"] * max(64, count(r)) * (4 if dtp(r) == "float32" else 1) for o, l, r, a, b in seq)
+        me = add("P", c, emit, [x for q in seq for x in q[1:3]], [q[0] for q in seq])
+        ops[me]["incs"] = sum(1 for q in seq if q[4] or q == seq[-1])
+        return me
+
+    def grp(out, pairs, start=True, stop=True):
+        return [(out, l, r, start and n == 0, stop and n == len(pairs) - 1) for n, (l, r) in enumerate(pairs)]
+
+    def iota(out, pattern, base, cm):
+        def emit(g, T):
+            if dtp(out) == "int32":
+                return [g.iota(ap(T, out), pattern, base, cm)]
+            return [g.iota(ap(T, out), pattern, base, cm, allow_small_or_imprecise_dtypes=True)]
+        return add("G", 160 + 2 * count(out), emit, [], [out])
+
+    def gcopy(out, a):
+        n = count(a)
+        return add("G", CM["g0"] + 2 * n,
+                   lambda g, T: [g.affine_select(ap(T, out), ap(T, a), [[0, n]], ALU.is_gt, 0.0, 1, 0)], [a], [out])
+
+    def dma(eng, sem, emit, rd, wr, nbytes):
+        return add(eng, 60, emit, rd, wr, sig=(sem, 16), lat=2000 + nbytes / 250.0)
+
+    def c_(n):
+        return R("col", n, n + 1)
+
+    dma("Y", "ld0", lambda g, T: [g.sync.dma_start(T.vi[:], T.v0[:])], [], [R("vi")], 2048)
+    dma("Y", "ld1", lambda g, T: [g.sync.dma_start(T.Ei[:], T.e0[:])], [], [R("Ei")], 786432)
+    dma("Y", "ld2", lambda g, T: [g.sync.dma_start(T.X[:], T.x0[:])], [], [R("X")], 1835008)
+    dma("Y", "ld3", lambda g, T: [g.sync.dma_start(T.wi[:], T.wt[:])], [], [R("wi")], 512)
+
+    iota(R("pi", 0, 1), [[0, 1]], 0, 1)
+    iota(R("D1"), [[1, 144]], 0, -1)
+    iota(R("D16"), [[16, 8], [0, 16]], 0, -1)
+    iota(R("cc"), [[1, 64]], 0, 0)
+    iota(R("D8"), [[8, 16], [0, 8]], 0, -1)
+    for n, k in ((1, 15), (2, 7), (3, 8), (4, 16)):
+        ts(R("pi", n, n + 1), R("pi", 0, 1), k, ALU.bitwise_and)
+    cp(R("col", 0, 4), R("pi", 1, 5))
+    r_, j_, hi_, kk_ = c_(0), c_(1), c_(2), c_(3)
+    ts(c_(4), hi_, 125.0, ALU.mult, 8.0, ALU.add)
+    ts(c_(5), hi_, -125.0, ALU.mult, 1008.0, ALU.add)
+    ts(c_(6), j_, -3.0, ALU.mult, c_(4), ALU.add)
+    ts(c_(7), j_, -3.0, ALU.mult, c_(5), ALU.add)
+    ts(R("RS"), R("D1"), 1.0, ALU.add, c_(7), ALU.is_equal)
+    ts(R("RP"), R("D1"), -7.0, ALU.add, c_(6), ALU.is_equal)
+    ts(R("Lo16"), R("D1"), c_(4), ALU.is_equal)
+    ts(R("Hi16"), R("D1"), c_(5), ALU.is_equal)
+    ts(c_(8), r_, -1.0, ALU.mult, 16.0, ALU.add)
+    ts(R("W4"), R("D1"), c_(8), ALU.is_equal, 4096.0, ALU.mult)
+    act(R("Wn"), R("W4"), ACT.Identity, scale=-1.0 / 131072)
+    cp(c_(9), R("wi"))
+    ts(R("Ww"), R("D1"), c_(8), ALU.is_equal, c_(9), ALU.mult)
+    ts(R("I"), R("D1", 0, 128), 0.0, ALU.is_equal)
+    act(R("In"), R("I"), ACT.Identity, scale=-512.0)
+    ts(R("Lo32"), R("D1"), c_(4), ALU.is_equal)
+    ts(R("Hi32"), R("D1"), c_(5), ALU.is_equal)
+    ts(c_(10), kk_, 100.0, ALU.mult, 16.0, ALU.add)
+    ts(c_(11), kk_, -100.0, ALU.mult, 1600.0, ALU.add)
+    ts(R("G0"), R("D1"), c_(10), ALU.is_equal)
+    ts(R("G1"), R("D1"), c_(11), ALU.is_equal)
+    ts(R("B16"), R("D16"), r_, ALU.add, 0.0, ALU.is_equal)
+    ts(R("B8"), R("D8"), j_, ALU.add, 0.0, ALU.is_equal)
+    ts(R("TL0"), R("D1", 0, 128), 0.0, ALU.is_lt, -1.0, ALU.mult)
+    tt(R("TL"), R("TL0"), R("B16"), ALU.mult)
+    mset(R("Fb", 0, 2048), 128.0)
+    add("G", CM["g0"] + 4096, lambda g, T: [g.affine_select(T.Sel[:], T.Fb[:, 0:2048], [[1, 16], [16, 8], [0, 16]],
+                                                            ALU.is_equal, 0.0, 0, -1)], [R("Fb", 0, 2048)], [R("Sel")])
+    mset(R("rs8"), 1.0)
+    mset(R("rs8", 0, None, 8), 0.0)
+    mset(R("c89"), 28.5 / 32)
+    mset(R("c128"), 128.0)
+    mset(R("one"), 1.0)
+    mset(R("thr", 0, 1), 49.0)
+    mset(R("E", V_N, V_N + 64), 0.0)
+    iota(R("IO"), [[128, V_N]], 0, 0)
+    iota(R("lq"), [[1, 2], [2, 32]], 0, 0)
+    iota(R("nC0"), [[1024, 4], [16, 32]], 0, 0)
+    act(R("nC"), R("nC0"), ACT.Identity, bias=r_)
+    ts(R("n16"), R("nC", 0, 32), 512.0, ALU.add)
+    cp(R("I16"), R("I"))
+    mset(R("Z", 0, 1536 * len(cuts("T"))), 0.0)
+    iota(R("lL", 16, 20), [[1, 2], [32, 2]], 0, 0)
+    ts(R("lL", 0, 4), R("cc", 0, 64, 16), r_, ALU.add)
+    ts(R("lL", 4, 8), R("lL", 16, 20), r_, ALU.add, r_, ALU.add)
+    ts(R("lL", 8, 16), R("lL", 0, 8), float(V_N), ALU.add, 128.0, ALU.mult)
+    for K in sorted(set(b - a for a, b in cuts("B"))):
+        n = 12 + K // 8
+        ts(c_(n), r_, 8.0 * K, ALU.mult, 7.0, ALU.add)
+        ts(R("RL", K, 2 * K), R("cc", 0, K), 8.0, ALU.mult, c_(n), ALU.add)
+    ts(c_(17), j_, -2048.0, ALU.mult, float(8 * 2048 - C0), ALU.add)
+    ts(R("mk", 0, 8), R("cc", 0, 8), j_, ALU.is_equal)
+    ts(R("mk", 8, 16), R("cc", 0, 8), j_, ALU.is_equal, float(-C0), ALU.mult)
+    ts(R("lL", 24, 32), R("lL", 0, 8), float(2 ** 18), ALU.mult)
+    cp(R("wb", 0, 1), R("wi"))
+    mm(grp(R("b3", 0, 1), [(R("B16"), R("wb", 0, 1))]))
+    ts(c_(18), R("b3", 0, 1), 128.0, ALU.mult)
+    ts(c_(19), j_, c_(4), ALU.add, -7.0, ALU.add)
+    ts(c_(20), j_, c_(5), ALU.add, -15.0, ALU.add)
+    cp(R("vL", 0, 4), R("vi"))
+    ts(R("v128", 0, 4), R("vi"), 128.0, ALU.mult)
+    gcopy(R("E", 0, V_N), R("Ei"))
+
+    def W(name, o):
+        return R(name, o, o + 128)
+    lolo, lohi, hilo, hihi = (8, "Lo"), (0, "Lo"), (16, "Hi"), (8, "Hi")
+
+    def sh(which, bits):
+        return W(which[1] + bits, which[0])
+
+    def send(t):
+        def emit(g, T):
+            return [("send", t)]
+        return add("G", 1000 if t else 3000, emit, [R("X")], [], sig=("snt%d" % t, 16), lat=14000)
+
+    f = {}
+    names = ["SF", "thK", "hp", "d1", "nh", "ds", "ix", "k1", "Rk", "k2", "FB", "key", "tr", "M", "d2", "t"]
+    for n, k in enumerate(names):
+        f[k] = R("tf", 32 * n, 32 * n + 32)
+
+    for t in range(RO):
+        last = t == RO - 1
+        nat = t == 0
+        vo = 4 * (t % 2)
+        vn = 4 - vo
+        vl = R("vL", vo, vo + 4)
+        EW = "Ei" if nat else "E"
+        reg = 1024 * (t % 4)
+        sent = send(t)
+        ops[sent]["round"] = t
+
+        def half(name, h):
+            return R(name, h, 64, 2) if nat else R(name, 32 * h, 32 * h + 32)
+        ts(R("c1h"), IND(EW, 0, V_N, vl), -2048.0, ALU.add)
+        mm(grp(R("b6", 0, 32), [(W("RS", 1 - h), half("c1h", h)) for h in (0, 1)])
+           + grp(R("b6", 32, 64), [(W("RP", 1 - h), half("c1h", h)) for h in (0, 1)]))
+        ts(R("L1"), R("b6", 0, 64), 2048.0, ALU.add)
+        mm(grp(R("b2", 0, 32), [(sh(lolo, "16"), half("c1h", 0)), (sh(lohi, "16"), half("c1h", 1))])
+           + grp(R("b2", 32, 64), [(sh(hilo, "16"), half("c1h", 0)), (sh(hihi, "16"), half("c1h", 1))]))
+        act(R("pC"), R("b2", 0, 32), ACT.Identity, bias=2048.0)
+        act(R("sC"), R("b2", 32, 64), ACT.Identity, bias=float(TH4))
+        where = {}
+        for c, (k0, k1) in enumerate(cuts("L")):
+            K = k1 - k0
+            ks = S_(k0, k1)
+            ts(R("c2h", 16 * k0, 16 * k1), IND(EW, 0, V_N, R("L1", k0, k1)), -2048.0, ALU.add)
+            ev, od = R("c2h", 16 * k0, 16 * k1, 2), R("c2h", 16 * k0 + 1, 16 * k1, 2)
+            mm(grp(("b7", (ks, S_(None))), [(sh(hilo, "16"), ev), (sh(hihi, "16"), od)]))
+            mm(grp(R("b4", 8 * k0, 8 * k1), [(sh(lolo, "16"), ev), (sh(lohi, "16"), od)]))
+            ts(R("L2", 16 * k0 + 8 * K, 16 * k0 + 15 * K), ("b7", (ks, S_(0, 7))), 2048.0, ALU.add)
+            ts(R("L2", 16 * k0, 16 * k0 + 8 * K), R("b4", 8 * k0, 8 * k1), 2048.0, ALU.add)
+            if PAR["spp"] or k1 == 32:
+                e = k0 if PAR["spp"] else 0
+                act(R("Spp", 8 * e, 8 * k1), ("b7", (S_(e, k1), S_(None))), ACT.Identity, bias=float(TH4))
+            for k in range(k0, k1):
+                where[k] = (16 * k0 + 8 * (k - k0), 16 * k0 + 8 * K + 7 * (k - k0))
+        for c, (k0, k1) in enumerate(cuts("X")):
+            act(R("Xp", 16 * k0, 16 * k1), IND("X", 0, XW, R("L1", 32 + k0, 32 + k1)), ACT.Identity)
+            for j, e in enumerate(PAR["XE"][c]):
+                dst, src = R("Xpb", 128 * k0 + j, 128 * k1, 8), R("Xp", 16 * k0, 16 * k1)
+                if e == "S":
+                    act(dst, src, ACT.Identity)
+                else:
+                    (gcopy if e == "G" else cp)(dst, src)
+        tt(R("U"), IND("IO", 0, V_N, vl), R("cc" if nat else "lq"), ALU.add)
+        for c in range(4):
+            act(R("AB", 64 * c, 64 * c + 64), R("U"), ACT.Abs, bias=R("v128", vo + c, vo + c + 1), scale=-1.0)
+        lo_ = 0 if nat else 4
+        for c in range(4):
+            act(R("fm", 64 * c, 64 * c + 64), R("AB", 64 * c, 64 * c + 64), ACT.Relu,
+                bias=R("lL", 24 + lo_ + c, 25 + lo_ + c), scale=-float(2 ** 18), acc=R("lf", c, c + 1))
+        tt(R("lf", 4, 8), R("lf", 0, 4), R("lL", 8 + lo_, 12 + lo_), ALU.min)
+        tt(R("lf", 8, 12), R("lf", 4, 8), R("v128", vo, vo + 4), ALU.max)
+        ts(R("off"), R("lf", 8, 12), 1.0 / 128, ALU.mult)
+        act(f["FB"], R("sC"), ACT.Identity, bias=R("mk", 8 + t, 9 + t), scale=R("mk", t, t + 1))
+        for a, b in cuts("M"):
+            o = where[a][0]
+            tt(R("m", 128 * a, 128 * b), IND("X", 0, XW, R("L2", o, o + 8 * (b - a))),
+               R("Xpb", 128 * a, 128 * b), ALU.min)
+        for c, (a, b) in enumerate(cuts("N")):
+            o = where[a][1]
+            src = IND("X", 0, XW, R("L2", o, o + 7 * (b - a)))
+            if PAR["NE"][c] == "S":
+                act(R("Gs", 112 * a, 112 * b), src, ACT.Identity)
+            else:
+                cp(R("Gs", 112 * a, 112 * b), src)
+        for c, (k0, k1) in enumerate(cuts("A")):
+            zm = R(("b5", "b6")[c % 2], 8 * k0, 8 * k1)
+            mm(grp(zm, [(W("W4", 16 - x), R("m", 128 * k0 + x, 128 * k1, 16)) for x in range(16)]))
+            ts(R("dead", 8 * k0, 8 * k1), zm, float(TH4), ALU.is_lt)
+            tt(R("lo", 8 * k0, 8 * k1), zm, R("Spp", 8 * k0, 8 * k1), ALU.min)
+            scan(R("st", 8 * k0, 8 * k1), R("dead", 8 * k0, 8 * k1), R("lo", 8 * k0, 8 * k1), ALU.mult, ALU.max)
+            ts(R("subl", k0, k1), R("st", 8 * k0 + 7, 8 * k1, 8), float(-C0), ALU.add, 0.0, ALU.max)
+            act(R("nXs", 16 * k0, 16 * k1), IND("X", 0, XW, R("subl", k0, k1)), ACT.Identity, scale=-1.0)
+        nd = [0, 0]
+
+        def h_(n, a=0, b=32):
+            return R("ha", 32 * n + a, 32 * n + b)
+
+        def f_(n, a, b):
+            return R("tf", f[n][1][0].start + a, f[n][1][0].start + b)
+
+        def names_records(p, a, b):
+            zb, n = 1536 * p, b - a
+            pi_ = R("Z", zb + 16 * a, zb + 16 * b)
+            mm(grp(R("b5", a, b), [(R("B8"), R(q, 8 * a + i, 8 * b, 8)) for q in ("dead", "ok") for i in range(8)]))
+            ts(R("ns", a, b), R("b5", a, b), R("thr", t % 2, t % 2 + 1), ALU.is_lt, -float(2 ** 24), ALU.mult)
+            ts(h_(0, a, b), R("b4", a, b), c_(18), ALU.subtract)
+            ts(h_(1, a, b), h_(0, a, b), XW - 1, ALU.bitwise_and)
+            tt(h_(2, a, b), h_(1, a, b), h_(1, a, b), ALU.mult)
+            ts(h_(3, a, b), h_(2, a, b), 5, ALU.arith_shift_right)
+            tt(h_(4, a, b), h_(3, a, b), h_(1, a, b), ALU.add)
+            ts(h_(5, a, b), h_(4, a, b), XW - 1, ALU.bitwise_and)
+            cp(R("hl", a, b), h_(5, a, b))
+            mm(grp(R("b5", 32 + a, 32 + b), [(R("I"), R("ns", a, b))]
+                   + [(W("W4", 16 - x), R("Z", zb + 16 * a + x, zb + 16 * b, 16)) for x in range(16)]))
+            ts(f_("thK", a, b), R("b5", 32 + a, 32 + b), float(2 ** 23), ALU.is_lt, -1000.0, ALU.mult)
+            if b == 32:
+                ts(f["SF"], R("b5", 32, 64), float(2 ** 23), ALU.is_ge)
+                if PAR["k1"] == "V":
+                    ts(f["k1"], R("b5", 32, 64), -float(2 ** 23), ALU.add, 4.0, ALU.mult)
+                else:
+                    act(f["k1"], R("b5", 32, 64), ACT.Identity, bias=-float(2 ** 25), scale=4.0)
+            for u, v in ((a, b),) if n <= PAR["dd"] else ((a, (a + b) // 2), ((a + b) // 2, b)):
+                tt(R("dd", 16 * u, 16 * v), IND("X", 0, XW, R("hl", u, v)), R("Z", zb + 16 * u, zb + 16 * v), ALU.subtract)
+                act(R("ad", 16 * u, 16 * v), R("dd", 16 * u, 16 * v), ACT.Abs, bias=128.0)
+            mm(grp(R("b6", 64 + a, 64 + b), [(R("I"), R("c89", 0, n))]
+                   + [(W("Wn", 16 - x), R("ad", 16 * a + x, 16 * b, 16)) for x in range(16)]))
+            tt(R("ask", a, b), R("b6", 64 + a, 64 + b), f_("thK", a, b), ALU.is_lt)
+            old, was = R("Z", zb + 512 + 16 * a, zb + 512 + 16 * b), R("X", reg + 16 * a, reg + 16 * b)
+            if PAR["old"] == "S":
+                act(old, was, ACT.Identity, bias=128.0)
+            else:
+                add("Y", 60, lambda g, T: [g.sync.dma_start(ap(T, old), ap(T, was))], [was], [old],
+                    sig=("cz", 16 * (t + 1)), lat=3000)
+                add("G", 1000, lambda g, T: [g.dma_start(ap(T, old), T.c128[:], accum_op=ALU.add)], [old, R("c128")], [old],
+                    sig=("ca", 16 * (t + 1)), lat=3000)
+            got, avg = IND("XR", XW * t, XW * (t + 1), R("hl", a, b)), R("Z", zb + 1024 + 16 * a, zb + 1024 + 16 * b)
+            if PAR["rec"] == "V":
+                tt(R("sm", 16 * a, 16 * b), got, pi_, ALU.add, ext=[("arr%d" % t, 16)])
+                act(avg, R("sm", 16 * a, 16 * b), ACT.Identity, bias=63.75, scale=0.5)
+            else:
+                me = ops[act(R("sm", 16 * a, 16 * b), got, ACT.Identity)]
+                me["ext"] = [("arr%d" % t, 16)]
+                me["deps"][sent] = True
+                mm(grp(R("b3", 0, 16 * n), [(R("I"), pi_), (R("I"), R("sm", 16 * a, 16 * b))]))
+                act(avg, R("b3", 0, 16 * n), ACT.Identity, bias=63.75, scale=0.5)
+            scan(R("cum", a, b), R("one", 0, n), R("ask", a, b), ALU.mult, ALU.add, R("cum", a - 1, a) if a else 0.0)
+            ak = R("ask", a, b)
+            mm(grp(R("b5", 64 + a, 64 + b), [(R("TL"), ak), (R("In"), ak), (R("B16"), R("cum", a, b))])
+               + grp(R("b5", 96 + a, 96 + b), [(R("I16"), R("n16", a, b)), (R("In"), ak)]))
+            ts(f_("t", a, b), R("b5", 64 + a, 64 + b), -351.0, ALU.is_lt, 1024.0, ALU.mult)
+            tt(f_("ix", a, b), R("b5", 96 + a, 96 + b), f_("t", a, b), ALU.add)
+            cp(R("idx", a, b), f_("ix", a, b))
+
+        for c, (k0, k1) in enumerate(cuts("B")):
+            K = k1 - k0
+            part = [p for p, (a, b) in enumerate(cuts("T")) if a <= k0 < b][0]
+            for a in range(k0, k1, 4):
+                bk = "b%d" % (nd[0] % 2)
+                nd[0] += 1
+                whole = (bk, (S_(None), S_(0, 7), S_(None)))
+                mm([(whole, R("I"), R("Gs", 112 * a, 112 * a + 448), True, False)])
+                mm([((bk, (S_(None), i, S_(None))), R("I"), R("nXs", 16 * a, 16 * a + 64), False, i == 6) for i in range(7)])
+                act(R("absd", 112 * a, 112 * a + 448), whole, ACT.Abs)
+            zd = ("b7", (S_(k0, k1), S_(None)))
+            mm([(zd, R("I"), R("c89", 0, 8 * K), True, False)]
+               + [(("b7", (S_(k0, k1), S_(0, 7))), W("Wn", 16 - x), R("absd", 112 * k0 + x, 112 * k1, 16), False, x == 15)
+                  for x in range(16)])
+            tt(R("ok", 8 * k0, 8 * k1), zd, R("dead", 8 * k0, 8 * k1), ALU.is_gt)
+            per = 64 // K
+            for x0 in range(0, 16, per):
+                bk = "b%d" % (2 + nd[1] % 2)
+                nd[1] += 1
+                xs = range(x0, x0 + per)
+                one = [(R(bk, 8 * K * (x - x0), 8 * K * (x - x0 + 1)), R("I"), R("m", 128 * k0 + x, 128 * k1, 16)) for x in xs]
+                two = [(R(bk, 8 * K * (x - x0), 8 * K * (x - x0 + 1)), W("Sel", 128 * x), R("ok", 8 * k0, 8 * k1)) for x in xs]
+                if PAR["pre"]:
+                    mm([q + (q is one[0], False) for q in one])
+                    mm([q + (False, q is two[-1]) for q in two])
+                else:
+                    mm([q for u, v in zip(one, two) for q in (u + (True, False), v + (False, True))])
+                o = 128 * k0 + 8 * K * x0
+                if PAR["BE"][c] == "S":
+                    act(R("Fb", o, o + 512), R(bk), ACT.Identity)
+                    if (x0 // per) % 2 == 0 and x0 + per < 16:
+                        continue
+                    xs = range(max(x0 - per, 0), x0 + per)
+                    o = 128 * k0 + 8 * K * xs[0]
+                    w = 8 * K * len(xs)
+                    scan(R("SO", o, o + w), R("rs8", 0, w), R("Fb", o, o + w), ALU.mult, ALU.max)
+                else:
+                    scan(R("SO", o, o + 512), R("rs8", 0, 512), R(bk), ALU.mult, ALU.max)
+                if k1 == 32 or PAR["uso"]:
+                    mm([(R("b4", k0, k1), W("Ww", 16 - x), R("SO", 128 * k0 + 8 * K * x + 7, 128 * k0 + 8 * K * (x + 1), 8),
+                         x == 0, x == 15) for x in xs])
+            zb = 1536 * part
+            act(R("Z", zb + 16 * k0, zb + 16 * k1), IND("SO", 128 * k0, 128 * k1, R("RL", K, 2 * K)), ACT.Identity)
+            a, b = cuts("T")[part]
+            if not PAR["uso"]:
+                e = min(b, PAR["B"][-2])
+                if k1 == e:
+                    mm(grp(R("b4", a, e), [(W("Ww", 16 - x), R("Z", zb + 16 * a + x, zb + 16 * e, 16)) for x in range(16)]))
+            if k1 == b:
+                names_records(part, a, b)
+        sub = R("st", 7, 256, 8)
+        tt(f["ds"], sub, R("sC"), ALU.subtract)
+        act(f["Rk"], sub, ACT.Identity, bias=c_(17))
+        tt(f["hp"], h_(5), R("pC"), ALU.subtract)
+        tt(f["nh"], R("nC", 32 * (t % 4), 32 * (t % 4) + 32), h_(5), ALU.subtract)
+        tt(f["d1"], f["hp"], f["SF"], ALU.mult)
+        tt(R("dS"), f["ds"], f["SF"], ALU.mult)
+        tt(f["k2"], f["k1"], f["Rk"], ALU.add)
+        tt(f["key"], f["k2"], f["FB"], ALU.max)
+        add("V", CM["v0"] + 32, lambda g, T: [g.vector.transpose(ap(T, f["tr"]), ap(T, f["key"]))], [f["key"]], [f["tr"]])
+        scan(f["M"], R("rs8", 0, 32), f["tr"], ALU.mult, ALU.max)
+        mo = f["M"][1][0].start
+        seq = []
+        for kk in (0, 1):
+            seq += grp(R("b2", kk, 4, 2), [(W("G%d" % kk, 16 - 16 * gp), R("tf", mo + 16 * gp + 7, mo + 16 * gp + 16, 8)) for gp in (0, 1)])
+        mm(seq)
+        cp(R("gi", 0, 4), R("b2", 0, 4))
+        ts(R("gi", 4, 8), R("gi", 0, 4), 2047, ALU.bitwise_and)
+        if not last:
+            cp(R("vL", vn, vn + 4), R("gi", 4, 8))
+            ts(R("v128", vn, vn + 4), R("gi", 4, 8), 128.0, ALU.mult)
+            mm(grp(R("b3", 0, 32), [(R("one"), R("ns"))]))
+            act(R("af", 0, 32), R("b3", 0, 32), ACT.Identity, scale=-1.0 / 2 ** 27, acc=R("af", 32, 33))
+            cp(R("gi", 8, 9), R("af", 32, 33))
+            ts(R("gi", 9, 10), R("gi", 8, 9), 7, ALU.bitwise_and)
+            ts(R("thr", 1 - t % 2, 2 - t % 2), R("gi", 9, 10), -1.0, ALU.mult, 49.0, ALU.add)
+        else:
+            ts(R("P0"), R("D1"), c_(19), ALU.is_equal)
+            ts(R("P1"), R("D1"), c_(20), ALU.is_equal)
+            cp(R("yvs", 0, 4), R("gi", 4, 8))
+            seq = []
+            for b in (0, 1):
+                seq += grp(R("b3", b, 4, 2), [(W("P%d" % b, 1 - h), R("yvs", 2 * h, 2 * h + 2)) for h in (0, 1)])
+            mm(seq)
+            act(R("yvs", 4, 8), R("b3", 0, 4), ACT.Identity)
+            dma("Y", "st0", lambda g, T: [g.sync.dma_start(T.yv[:], T.yvs[:, 4:8])], [R("yvs", 4, 8)], [], 2048)
+        pair = R("b4", 0, 64)
+        mm([(pair, R("I16"), R("c1h"), True, False)]
+           + [(half("b4", h), sh((lohi, hihi)[h], "16"), R("dS"), False, False) for h in (0, 1)])
+        mm([(half("b4", h), sh((lolo, hilo)[h], "32"), f["d1"], False, False) for h in (0, 1)])
+        tt(f["d2"], R("ask"), f["nh"], ALU.mult)
+        mm([(half("b4", h), sh((lolo, hilo)[h], "32"), f["d2"], False, h == 1) for h in (0, 1)])
+        ts(R("pr"), pair, 2048.0, ALU.add)
+        cp(IND("E", 0, V_N + 64, R("off")), R("pr"))
+        if last:
+            dma("Y", "st1", lambda g, T: [g.sync.dma_start(T.ye[:], T.E[:, 0:V_N])], [R("E", 0, V_N)], [], 786432)
+        for p, (a, b) in enumerate(cuts("T")):
+            act(R("X", reg + 16 * a, reg + 16 * b), IND("Z", 1536 * p, 1536 * (p + 1), R("idx", a, b)), ACT.Identity, bias=-128.0)
+        if t == RO - 2:
+            nx = 1024 * ((t + 1) % 4)
+            dma("Y", "st2", lambda g, T, nx=nx: [g.sync.dma_start(T.yx[:, 0:nx], T.X[:, 0:nx])], [R("X", 0, nx)], [], 262144)
+            dma("Y", "st3", lambda g, T, nx=nx: [g.sync.dma_start(T.yx[:, nx + 512:XW], T.X[:, nx + 512:XW])],
+                [R("X", nx + 512, XW)], [], 655360)
+        if last:
+            dma("S", "st4", lambda g, T, reg=reg: [g.scalar.dma_start(T.yx[:, reg:reg + 512], T.X[:, reg:reg + 512])],
+                [R("X", reg, reg + 512)], [], 131072)
+    return ops
+
+
+def schedule(ops):
+    n = len(ops)
+    succ = [[] for _ in range(n)]
+    for i, o in enumerate(ops):
+        for d in o["deps"]:
+            succ[d].append(i)
+
+    def gap(d, i):
+        if ops[d]["sig"] is not None:
+            return ops[d]["lat"]
+        if ops[d]["eng"] != ops[i]["eng"]:
+            return CM["x"]
+        return CM["same"] if ops[i]["deps"][d] else 0
+    bl = [0.0] * n
+    for i in range(n - 1, -1, -1):
+        bl[i] = ops[i]["cost"] + max([gap(i, s) + bl[s] for s in succ[i]] + [ops[i]["lat"]])
+    first = -1000
+    for i, o in enumerate(ops):
+        first = i if "round" in o else first
+        o["pos"] = i - first
+        bl[i] += PAR["bias"].get(i - first, 0) + (1e6 * (4 - i) if i < 4 else 0)
+    left = [len(o["deps"]) for o in ops]
+    ready = [0.0] * n
+    pool = {e: [] for e in "VSPGY"}
+    for i in range(n):
+        if left[i] == 0:
+            pool[ops[i]["eng"]].append(i)
+    free = {e: 0.0 for e in pool}
+    order, end = [], [0.0] * n
+    while len(order) < n:
+        best = None
+        for e in pool:
+            if pool[e]:
+                at = max(free[e], min(ready[i] for i in pool[e]))
+                if best is None or at < best[0]:
+                    best = (at, e)
+        at, e = best
+        now = [i for i in pool[e] if ready[i] <= at]
+        i = max(now, key=lambda q: bl[q])
+        soon = [q for q in pool[e] if at < ready[q] < at + min(0.5 * ops[i]["cost"], 250) and bl[q] > bl[i] + ops[i]["cost"]]
+        if soon:
+            i = max(soon, key=lambda q: bl[q])
+            at = ready[i]
+        pool[e].remove(i)
+        end[i] = at + ops[i]["cost"]
+        free[e] = end[i]
+        ops[i]["at"] = at
+        order.append(i)
+        for s in succ[i]:
+            ready[s] = max(ready[s], end[i] + gap(i, s))
+            left[s] -= 1
+            if left[s] == 0:
+                pool[ops[s]["eng"]].append(s)
+    return order
+
+
+def by_keys(ops, keys):
+    n = len(ops)
+    place, succ, left = [0] * n, [[] for _ in range(n)], [len(o["deps"]) for o in ops]
+    t, first = -1, 0
+    for i, o in enumerate(ops):
+        if "round" in o:
+            t, first = o["round"], i
+        tab = keys[0] if t < 0 else keys[1] if t == 0 else keys[3] if t == RO - 1 else keys[2]
+        place[i] = tab[min(i - first, len(tab) - 1)] + (keys[4] + keys[5] * t if t > 0 else 0)
+        o["at"] = place[i]
+        for d in o["deps"]:
+            succ[d].append(i)
+    pool = [i for i in range(n) if left[i] == 0]
+    order = []
+    while pool:
+        i = min(pool, key=lambda q: (place[q], q))
+        pool.remove(i)
+        order.append(i)
+        for s in succ[i]:
+            left[s] -= 1
+            if left[s] == 0:
+                pool.append(s)
+    return order
+
+
+def links(ops, cm):
+    return [[(d, ops[d]["lat"] if ops[d]["sig"] is not None else cm["x"] if ops[d]["eng"] != o["eng"] else cm["same"] if raw else 0)
+             for d, raw in o["deps"].items()] for o in ops]
+
+
+def place(seq, before, cost, eng, start):
+    end = [0.0] * len(cost)
+    busy = {e: [] for e in "VSPGY"}
+    for i in seq:
+        at = start[i]
+        for d, g in before[i]:
+            if end[d] + g > at:
+                at = end[d] + g
+        row = busy[eng[i]]
+        n = len(row)
+        while n > 0 and row[n - 1][1] > at:
+            n -= 1
+        while n < len(row) and row[n][0] < at + cost[i]:
+            at = max(at, row[n][1])
+            n += 1
+        row.insert(n, (at, at + cost[i]))
+        end[i] = at + cost[i]
+    return end
+
+
+def length(order, before, ops):
+    free = {e: 0.0 for e in "VSPGY"}
+    end = [0.0] * len(ops)
+    last = 0.0
+    for i in order:
+        o = ops[i]
+        at = free[o["eng"]]
+        for d, g in before[i]:
+            if end[d] + g > at:
+                at = end[d] + g
+        end[i] = free[o["eng"]] = at + o["cost"]
+        last = max(last, end[i] + o["lat"])
+    return last
+
+
+def improve(ops, tries, seed=1):
+    base = dict(CM)
+    views = []
+    for w, m in VIEWS:
+        CM.update(m)
+        o = build()
+        views.append((w, links(o, CM), o))
+        CM.update(base)
+    n = len(ops)
+    cost, eng, lat = [o["cost"] for o in ops], [o["eng"] for o in ops], [o["lat"] for o in ops]
+    before = links(ops, CM)
+    for i in (1, 2, 3):
+        before[i].append((i - 1, 0))
+    after = [[] for _ in range(n)]
+    for i in range(n):
+        for d, g in before[i]:
+            after[d].append((i, g))
+    rng = np.random.RandomState(seed)
+    best = schedule(ops)
+    key = [o["at"] for o in ops]
+    top = sum(w * length(best, b, o) for w, b, o in views)
+    now = top
+    for it in range(tries):
+        shake = rng.normal(0, (30, 120, 400)[it % 3], n) * (rng.rand(n) < 0.3)
+        k = [key[i] + shake[i] for i in range(n)]
+        for i in range(n):
+            for d, g in before[i]:
+                if k[i] <= k[d]:
+                    k[i] = k[d] + 1e-3
+        end = place(sorted(range(n), key=lambda q: k[q]), before, cost, eng, [0.0] * n)
+        end = place(sorted(range(n), key=lambda q: -end[q]), after, cost, eng, lat)
+        end = place(sorted(range(n), key=lambda q: -end[q]), before, cost, eng, [0.0] * n)
+        order = sorted(range(n), key=lambda q: (end[q] - cost[q], q))
+        v = sum(w * length(order, b, o) for w, b, o in views)
+        if v < now + 150:
+            now, key = v, [end[q] - cost[q] for q in range(n)]
+            if v < top:
+                top, best = v, order
+                for q in range(n):
+                    ops[q]["at"] = key[q]
+    return best
+
+
+VIEWS = [(0.45, {}), (0.25, {"pe": 0.7, "gat": 1.3}), (0.3, {"x": 200, "same": 120, "gat": 1.7})]
+TRIES = 300
+
+
+def plan():
+    ops = build()
+    order = schedule(ops)
+    cnt = {e: 0 for e in COUNTER}
+    known = {e: {} for e in "VSPGY"}
+    seen = {}
+    for i in order:
+        o = ops[i]
+        e = o["eng"]
+        need = {}
+        for d, raw in o["deps"].items():
+            p = ops[d]
+            if p["sig"] is None and p["eng"] == e and not raw:
+                continue
+            s, v = p["done"]
+            if v > need.get(s, (0, None))[0]:
+                need[s] = (v, d)
+        waits = []
+        for s, (v, d) in sorted(need.items(), key=lambda q: -ops[q[1][1]]["at"]):
+            if known[e].get(s, 0) < v:
+                waits.append((s, v))
+                for s2, v2 in ops[d]["vc"].items():
+                    known[e][s2] = max(known[e].get(s2, 0), v2)
+        waits += list(o["ext"])
+        for s, v in waits:
+            seen[s] = max(seen.get(s, 0), v)
+        o["waits"] = waits
+        if o["sig"] is None:
+            cnt[e] += o.get("incs", 1)
+            o["done"] = (COUNTER[e], cnt[e])
+        else:
+            o["done"] = o["sig"]
+        o["vc"] = dict(known[e])
+        o["vc"][o["done"][0]] = o["done"][1]
+    final = {}
+    for o in ops:
+        s, v = o["done"]
+        final[s] = max(final.get(s, 0), v)
+    tail = [(s, v) for s, v in final.items() if seen.get(s, 0) < v]
+    return ops, order, tail
+
+
+PLAN = []
+
+
+def rank_program(g, core, T, topo):
+    rank = T.rank_of(core)
+    if rank is None:
+        return
+    if not PLAN:
+        PLAN.append(plan())
+    ops, order, tail = PLAN[0]
+    queue = {"V": g.vector, "S": g.scalar, "P": g.tensor, "G": g, "Y": g.sync}
+    for i in order:
+        o = ops[i]
+        for s, v in o["waits"]:
+            queue[o["eng"]].wait_ge(T.sem[s], v * wide(s, core, T, topo))
+        for ins in o["emit"](g, T):
+            if isinstance(ins, tuple):
+                t = ins[1]
+                dst = T.cores[(rank - 1 - t % (NR - 1)) % NR]
+                rid, pid, _ = topo.addr(dst)
+                g.remote_dma(T.XR[:, XW * t:XW * (t + 1)], T.X[:], T.sem["arr%d" % t], T.sem["snt%d" % t],
+                             pid, rid, topo.mask(core, dst))
+            else:
+                ins.then_inc(T.sem[o["done"][0]], 1 if o["sig"] is None else 16)
+    for s, v in tail:
+        g.wait_ge(T.sem[s], v * wide(s, core, T, topo))
+
+
+def wide(s, core, T, topo):
+    if s[:3] not in ("snt", "arr"):
+        return 1
+    t = int(s[3:])
+    rank = T.rank_of(core)
+    step = 1 + t % (NR - 1)
+    if s[:3] == "snt":
+        return len(topo.engines(core, T.cores[(rank - step) % NR])) // 16
+    return len(topo.engines(T.cores[(rank + step) % NR], core)) // 16

@@ -23,6 +23,11 @@ PAR = {
 PAR["bias"].update({8: 0, 40: 2000, 41: 2000, 49: -5100, 50: -1100, 51: 3700, 52: -300, 69: 4000, 70: 4000, 71: 6000, 81: -4300, 82: -4000, 100: -2000, 101: -6000, 135: -300, 136: -300, 137: -300, 138: -300, 178: -2800, 179: -3200, 180: 4800, 1026: 2000, 1027: 2000, 1028: 4000, 1029: 4000, 1030: -300, 1031: -300, 1036: 6800, 1037: 2800, 1038: 2000, 1039: 2000, 1045: 4800, 1046: 2800, 1047: 4800, 1048: 800, 1072: 0})
 PAR.update({"X": [0, 8, 20, 32], "XE": ["VVVVVVSG", "VVVVGGGG", "GGGGGGGG"]})
 PAR["bias"] = {3: -300, 4: -300, 5: -300, 6: -300, 7: 2000, 8: 2000, 9: 2000, 10: 2000, 14: 300, 15: -1700, 16: 4300, 18: 3700, 19: 4000, 20: 4000, 21: 4000, 24: -1600, 25: -1600, 26: 3200, 27: 3200, 28: -2000, 30: -800, 31: -800, 37: 4000, 39: -4000, 40: -4000, 41: -4000, 46: -4000, 47: -4000, 48: -4000, 50: 2000, 51: -6300, 52: -6300, 53: -6300, 54: -4300, 56: 4000, 57: 4000, 58: 5200, 59: 5200, 60: 1200, 61: 2000, 65: -4000, 66: -800, 68: 800, 69: 800, 70: 800, 71: 800, 75: -2000, 76: -1200, 77: 800, 78: -3200, 79: 800, 80: 800, 81: 800, 83: 2000, 84: 2000, 85: 2000, 86: 2000, 93: -600, 94: -300, 98: 4000, 102: 800, 103: 800, 104: 800, 109: -300, 111: 800, 116: 800, 117: 800, 118: -300, 120: -500, 121: -500, 122: 300, 125: -800, 126: 300, 128: -300, 129: 1600, 130: 800, 145: -2000, 147: 2000, 152: 4000, 153: 2000, 154: 2000, 155: 2000, 156: 2000, 160: 2000, 161: 2000, 162: 2000, 163: 2000, 189: -4000, 190: -4800, 191: -4500, 192: 300, 193: -3700, 194: 300, 211: -300, 212: -300, 213: -300, 214: -300, 217: -800, 218: -800, 219: -800, 220: -800, 1007: -6000, 1008: -2000, 1009: -2000, 1010: -2000, 1048: 3200, 1049: 4000, 1050: 4000, 1051: 4000, 1053: 4000, 1054: 8000, 1055: 8000, 1056: 6000, 1057: 8000, 1058: 4000, 1060: 2000, 1061: 2000, 1062: 2000, 1063: 2000}
+PAR["XE"] = ["VVVVVVSS", "VVVVVVVV", "VVVVVVVV"]
+SHIFT = ('0 0 0 -3 -3 -3 -3 20 20 0 20 0 0 0 3 -17 83 40 37 40 40 40 0 0 -36 -28 32 32 -20 0 -8 -8 -20 0 0 0 0 40 0 -40 -60 -60 -12 -12 8 8 -40 -40 -40 0 20 -63 -63 -63 -43 0 40 40 52 52 12 20 0 0 0 -80 -48 -20 8 8 8 8 0 0 0 -20 28 48 0 48 -32 -32 -40 -20 20 20 20 0 0 0 0 -20 -20 -6 -3 0 0 0 40 0 0 8 -32 -32 8 0 0 0 0 -3 0 28 0 0 0 0 8 8 5 8 -5 -5 3 0 0 -8 3 0 -3 16 8 0 0 0 0 0 0 0 0 0 0 0 0 0 0 -17 0 20 0 0 0 0 0 20 20 20 20 0 0 0 20 20 0 0 -20 -20 0 0 0 0 0 0 0 0 40 40 40 40 0 0 0 0 0 0 0 0 0 0 12 -28 -28 -25 3 -37 6 3 0 0 0 0 0 0 0 0 0 0 0 0 0 0 0 -3 -3 -3 -3 0 0 -8 -8 -8 -8', '0 0 0 0 0 0 0 -60 -20 -60 -60 -40 -40 0 0 0 0 0 0 0 8 8 8 8 0 -40 0 0 0 0 0 0 0 20 20 20 20 0 -40 -40 0 0 40 20 20 20 -60 0 32 40 40 40 0 40 80 80 60 80 40 0 20 20 20 20 0 -40 -40 0 0 0 -40 -40')
+PAR["XE"] = ["VVVVVVSS", "VVVVVVGG", "VVGGGGGG"]
+SHIFT = ('0 -3 17 11 33 44 13 28 28 -58 -23 0 81 -52 38 -17 3 2 -14 100 28 0 68 6 -45 0 83 40 8 27 -216 -115 23 6 12 8 70 116 0 -38 20 -126 0 -72 -20 -7 5 -3 -68 -75 -47 -82 45 -20 -72 -23 0 136 3 113 119 34 32 0 -16 -35 -57 44 -8 -43 -31 -33 -88 43 104 -9 -37 107 -54 71 -3 -1 39 8 40 86 23 72 -2 -56 -31 -32 91 28 -1 0 -11 115 -40 51 99 40 -17 -8 32 0 -7 16 -114 -22 2 44 16 -28 43 -42 0 31 -3 -43 0 -37 -110 0 27 -9 -169 45 29 -29 -11 115 12 -88 3 0 55 -110 -93 -59 -25 -230 -36 20 21 -38 26 -20 59 -52 -35 0 0 -9 51 117 48 77 140 37 -60 -12 -29 8 41 0 25 11 2 4 -32 -2 -39 -165 -43 20 20 43 83 3 0 -3 20 -107 -8 -8 -131 -114 -35 -3 6 -3 -75 19 -3 -1 -72 -9 0 -142 -40 -54 -7 -56 52 8 -23 -40 25 28 -55 -47 0 -37 0 25 36 160 -46 0 -20 -20 20 84 56', '-23 25 160 0 137 177 0 -60 11 0 -54 -17 -32 -60 -8 -24 -64 -68 -32 0 49 -15 -32 -75 45 8 8 25 -40 83 52 18 -53 -77 0 0 23 7 0 -29 2 -11 0 32 40 -20 -20 0 -20 0 60 40 0 30 149 45 17 77 -20 -28 12 23 40 -52 -48 -111 0 0 66 -3 -80 -20 -49 -17 -17')
+PAR["bias"] = {n + 1000 * q: 100 * int(v) for q in (0, 1) for n, v in enumerate(SHIFT[q].split())}
 SAME_WAR = True
 KEYS = []
 
@@ -83,7 +88,7 @@ SEMAPHORES = (["cz", "ca", "cv", "cs", "cp", "cg", "ld0", "ld1", "ld2", "ld3", "
               + ["snt%d" % t for t in range(RO)] + ["arr%d" % t for t in range(RO)])
 COUNTER = {"V": "cv", "S": "cs", "P": "cp", "G": "cg"}
 TWO = ("bfloat16", "float16", "uint16")
-CM = {"v0": 64, "s0": 80, "g0": 200, "gat": 1.5, "sca": 3.8, "pe": 0.5, "pe0": 0, "x": 110, "same": 60, "tt": 2.0}
+CM = {"v0": 64, "s0": 80, "g0": 200, "gat": 1.6, "sca": 3.8, "pe": 0.55, "pe0": 0, "x": 200, "same": 170, "tt": 2.0}
 S_ = slice
 
 
@@ -325,7 +330,7 @@ def build():
     def send(t):
         def emit(g, T):
             return [("send", t)]
-        return add("G", 1000 if t else 3000, emit, [R("X")], [], sig=("snt%d" % t, 16), lat=14000)
+        return add("G", 2200 if t else 4000, emit, [R("X")], [], sig=("snt%d" % t, 16), lat=11000)
 
     f = {}
     names = ["SF", "thK", "hp", "d1", "nh", "ds", "ix", "k1", "Rk", "k2", "FB", "key", "tr", "M", "d2", "t"]
@@ -421,10 +426,10 @@ def build():
             ts(R("ns", a, b), R("b5", a, b), R("thr", t % 2, t % 2 + 1), ALU.is_lt, -float(2 ** 24), ALU.mult)
             ts(h_(0, a, b), R("b4", a, b), c_(18), ALU.subtract)
             ts(h_(1, a, b), h_(0, a, b), XW - 1, ALU.bitwise_and)
-            tt(h_(2, a, b), h_(1, a, b), h_(1, a, b), ALU.mult)
-            ts(h_(3, a, b), h_(2, a, b), 5, ALU.arith_shift_right)
-            tt(h_(4, a, b), h_(3, a, b), h_(1, a, b), ALU.add)
-            ts(h_(5, a, b), h_(4, a, b), XW - 1, ALU.bitwise_and)
+            ts(h_(2, a, b), h_(1, a, b), -4064.0, ALU.add)
+            ts(h_(3, a, b), h_(1, a, b), 4096.0, ALU.add)
+            tt(h_(4, a, b), h_(3, a, b), h_(2, a, b), ALU.mult)
+            ts(h_(5, a, b), h_(4, a, b), 5, ALU.arith_shift_right, XW - 1, ALU.bitwise_and)
             cp(R("hl", a, b), h_(5, a, b))
             mm(grp(R("b5", 32 + a, 32 + b), [(R("I"), R("ns", a, b))]
                    + [(W("W4", 16 - x), R("Z", zb + 16 * a + x, zb + 16 * b, 16)) for x in range(16)]))
@@ -447,16 +452,17 @@ def build():
             else:
                 add("Y", 60, lambda g, T: [g.sync.dma_start(ap(T, old), ap(T, was))], [was], [old],
                     sig=("cz", 16 * (t + 1)), lat=3000)
-                add("G", 1000, lambda g, T: [g.dma_start(ap(T, old), T.c128[:], accum_op=ALU.add)], [old, R("c128")], [old],
+                add("G", 1800, lambda g, T: [g.dma_start(ap(T, old), T.c128[:], accum_op=ALU.add)], [old, R("c128")], [old],
                     sig=("ca", 16 * (t + 1)), lat=3000)
             got, avg = IND("XR", XW * t, XW * (t + 1), R("hl", a, b)), R("Z", zb + 1024 + 16 * a, zb + 1024 + 16 * b)
             if PAR["rec"] == "V":
                 tt(R("sm", 16 * a, 16 * b), got, pi_, ALU.add, ext=[("arr%d" % t, 16)])
                 act(avg, R("sm", 16 * a, 16 * b), ACT.Identity, bias=63.75, scale=0.5)
             else:
-                me = ops[act(R("sm", 16 * a, 16 * b), got, ACT.Identity)]
-                me["ext"] = [("arr%d" % t, 16)]
-                me["deps"][sent] = True
+                for u, v in ((a, (a + b) // 2), ((a + b) // 2, b)):
+                    me = ops[act(R("sm", 16 * u, 16 * v), IND("XR", XW * t, XW * (t + 1), R("hl", u, v)), ACT.Identity)]
+                    me["ext"] = [("arr%d" % t, 16)] if u == a else []
+                    me["deps"][sent if u == a else len(ops) - 2] = True
                 mm(grp(R("b3", 0, 16 * n), [(R("I"), pi_), (R("I"), R("sm", 16 * a, 16 * b))]))
                 act(avg, R("b3", 0, 16 * n), ACT.Identity, bias=63.75, scale=0.5)
             scan(R("cum", a, b), R("one", 0, n), R("ask", a, b), ALU.mult, ALU.add, R("cum", a - 1, a) if a else 0.0)

@@ -5,99 +5,65 @@ import comms_topo
 ALU = AluOpType
 ACT = ActivationFunctionType
 NR, V_N, XW, RO = 8, 1536, 4096, 6
-TH4 = 72 * 4096
-C0 = TH4 - 2048
 PAR = {
     "L": [0, 8, 32],
-    "X": [0, 8, 16, 24, 32],
-    "XE": ["VVV", "VVG", "VGG", "VGG"],
-    "M": [0, 4, 8, 12, 16, 20, 24, 28, 32],
+    "LJ": [0, 4],
+    "X": [0, 8, 20, 32],
+    "M": [0, 8, 16, 24, 32],
     "N": [0, 4, 8, 12, 16, 20, 24, 28, 32],
-    "A": [0, 8, 16, 24, 32],
     "B": [0, 8, 16, 24, 32],
-    "BE": "SVVV",
-    "T": [0, 32],
-    "old": "D", "spp": True, "rec": "S", "k1": "S", "NE": "SSSSSSSS", "pre": True, "uso": False, "dd": 16,
-    "bias": {0: -800, 1: -800, 7: 4000, 8: 4000, 9: 4000, 10: 4000, 18: 4000, 21: 4000, 24: -800, 25: -4800, 26: -800, 27: -1600, 28: -800, 29: -800, 30: -800, 31: -800, 33: -300, 34: 800, 35: 4800, 36: 800, 37: 800, 45: -800, 46: -800, 47: -4800, 48: -4800, 49: -4800, 50: -800, 51: 4000, 53: -4000, 54: -3200, 56: 4000, 57: 3200, 58: -800, 59: -4000, 71: 4000, 72: 4000, 74: -2000, 75: -2800, 76: 1200, 77: -2800, 78: -4000, 80: 3700, 81: -300, 83: 800, 84: 800, 85: 800, 86: 800, 87: 800, 88: 800, 89: 800, 90: 800, 93: 800, 94: 800, 95: -4000, 96: -4000, 97: -4000, 98: -4000, 105: -300, 108: -300, 109: -4300, 110: 4000, 111: -300, 119: 4000, 120: 4000, 121: -800, 122: 3200, 124: 800, 128: -300, 129: -300, 130: -300, 131: -300, 132: -300, 143: -300, 144: -600, 145: -300, 146: -300, 147: -300, 159: -2000, 160: -2000, 161: -2000, 162: -2000, 164: 2000, 165: 2000, 166: 4000, 167: 4000, 169: 800, 170: 800, 171: 800, 172: 800, 175: -800, 176: -4800, 177: -800, 178: -800, 179: 800, 180: 800, 181: 800, 182: 800, 184: 4000, 186: -800, 187: -4800, 188: -4000, 189: -4000, 190: -4000, 192: 4000, 193: -6000, 194: -2000, 195: -2000, 196: -4000, 201: -800, 202: -800, 1020: -2000, 1021: 2000, 1024: -2000, 1025: -2000, 1026: -2000, 1027: -2000, 1034: 500, 1035: 800, 1036: 4800, 1037: 800, 1041: 2000, 1045: 2000, 1046: 2000, 1051: -4000, 1053: -300, 1055: -2000, 1056: -2000, 1057: -2000, 1058: -2000, 1059: 7700, 1060: 4000, 1061: 4000, 1062: 4000, 1063: -2000, 1064: -2000, 1065: -1200, 1066: -2000, 1072: 2000},
+    "D": [0, 8, 16],
+    "early": 1, "LE": [0, 16, 32], "XE": "SSSS",
+    "dead": "V", "ok": "V", "pick": "SV", "rec": "S", "sf": "V", "tries": 10, "swaps": 6000, "seed": 1,
 }
-PAR["bias"].update({8: 0, 40: 2000, 41: 2000, 49: -5100, 50: -1100, 51: 3700, 52: -300, 69: 4000, 70: 4000, 71: 6000, 81: -4300, 82: -4000, 100: -2000, 101: -6000, 135: -300, 136: -300, 137: -300, 138: -300, 178: -2800, 179: -3200, 180: 4800, 1026: 2000, 1027: 2000, 1028: 4000, 1029: 4000, 1030: -300, 1031: -300, 1036: 6800, 1037: 2800, 1038: 2000, 1039: 2000, 1045: 4800, 1046: 2800, 1047: 4800, 1048: 800, 1072: 0})
-PAR.update({"X": [0, 8, 20, 32], "XE": ["VVVVVVSG", "VVVVGGGG", "GGGGGGGG"]})
-PAR["bias"] = {3: -300, 4: -300, 5: -300, 6: -300, 7: 2000, 8: 2000, 9: 2000, 10: 2000, 14: 300, 15: -1700, 16: 4300, 18: 3700, 19: 4000, 20: 4000, 21: 4000, 24: -1600, 25: -1600, 26: 3200, 27: 3200, 28: -2000, 30: -800, 31: -800, 37: 4000, 39: -4000, 40: -4000, 41: -4000, 46: -4000, 47: -4000, 48: -4000, 50: 2000, 51: -6300, 52: -6300, 53: -6300, 54: -4300, 56: 4000, 57: 4000, 58: 5200, 59: 5200, 60: 1200, 61: 2000, 65: -4000, 66: -800, 68: 800, 69: 800, 70: 800, 71: 800, 75: -2000, 76: -1200, 77: 800, 78: -3200, 79: 800, 80: 800, 81: 800, 83: 2000, 84: 2000, 85: 2000, 86: 2000, 93: -600, 94: -300, 98: 4000, 102: 800, 103: 800, 104: 800, 109: -300, 111: 800, 116: 800, 117: 800, 118: -300, 120: -500, 121: -500, 122: 300, 125: -800, 126: 300, 128: -300, 129: 1600, 130: 800, 145: -2000, 147: 2000, 152: 4000, 153: 2000, 154: 2000, 155: 2000, 156: 2000, 160: 2000, 161: 2000, 162: 2000, 163: 2000, 189: -4000, 190: -4800, 191: -4500, 192: 300, 193: -3700, 194: 300, 211: -300, 212: -300, 213: -300, 214: -300, 217: -800, 218: -800, 219: -800, 220: -800, 1007: -6000, 1008: -2000, 1009: -2000, 1010: -2000, 1048: 3200, 1049: 4000, 1050: 4000, 1051: 4000, 1053: 4000, 1054: 8000, 1055: 8000, 1056: 6000, 1057: 8000, 1058: 4000, 1060: 2000, 1061: 2000, 1062: 2000, 1063: 2000}
-PAR["XE"] = ["VVVVVVSS", "VVVVVVVV", "VVVVVVVV"]
-SHIFT = ('0 0 0 -3 -3 -3 -3 20 20 0 20 0 0 0 3 -17 83 40 37 40 40 40 0 0 -36 -28 32 32 -20 0 -8 -8 -20 0 0 0 0 40 0 -40 -60 -60 -12 -12 8 8 -40 -40 -40 0 20 -63 -63 -63 -43 0 40 40 52 52 12 20 0 0 0 -80 -48 -20 8 8 8 8 0 0 0 -20 28 48 0 48 -32 -32 -40 -20 20 20 20 0 0 0 0 -20 -20 -6 -3 0 0 0 40 0 0 8 -32 -32 8 0 0 0 0 -3 0 28 0 0 0 0 8 8 5 8 -5 -5 3 0 0 -8 3 0 -3 16 8 0 0 0 0 0 0 0 0 0 0 0 0 0 0 -17 0 20 0 0 0 0 0 20 20 20 20 0 0 0 20 20 0 0 -20 -20 0 0 0 0 0 0 0 0 40 40 40 40 0 0 0 0 0 0 0 0 0 0 12 -28 -28 -25 3 -37 6 3 0 0 0 0 0 0 0 0 0 0 0 0 0 0 0 -3 -3 -3 -3 0 0 -8 -8 -8 -8', '0 0 0 0 0 0 0 -60 -20 -60 -60 -40 -40 0 0 0 0 0 0 0 8 8 8 8 0 -40 0 0 0 0 0 0 0 20 20 20 20 0 -40 -40 0 0 40 20 20 20 -60 0 32 40 40 40 0 40 80 80 60 80 40 0 20 20 20 20 0 -40 -40 0 0 0 -40 -40')
-PAR["XE"] = ["VVVVVVSS", "VVVVVVGG", "VVGGGGGG"]
-SHIFT = ('0 -3 17 11 33 44 13 28 28 -58 -23 0 81 -52 38 -17 3 2 -14 100 28 0 68 6 -45 0 83 40 8 27 -216 -115 23 6 12 8 70 116 0 -38 20 -126 0 -72 -20 -7 5 -3 -68 -75 -47 -82 45 -20 -72 -23 0 136 3 113 119 34 32 0 -16 -35 -57 44 -8 -43 -31 -33 -88 43 104 -9 -37 107 -54 71 -3 -1 39 8 40 86 23 72 -2 -56 -31 -32 91 28 -1 0 -11 115 -40 51 99 40 -17 -8 32 0 -7 16 -114 -22 2 44 16 -28 43 -42 0 31 -3 -43 0 -37 -110 0 27 -9 -169 45 29 -29 -11 115 12 -88 3 0 55 -110 -93 -59 -25 -230 -36 20 21 -38 26 -20 59 -52 -35 0 0 -9 51 117 48 77 140 37 -60 -12 -29 8 41 0 25 11 2 4 -32 -2 -39 -165 -43 20 20 43 83 3 0 -3 20 -107 -8 -8 -131 -114 -35 -3 6 -3 -75 19 -3 -1 -72 -9 0 -142 -40 -54 -7 -56 52 8 -23 -40 25 28 -55 -47 0 -37 0 25 36 160 -46 0 -20 -20 20 84 56', '-23 25 160 0 137 177 0 -60 11 0 -54 -17 -32 -60 -8 -24 -64 -68 -32 0 49 -15 -32 -75 45 8 8 25 -40 83 52 18 -53 -77 0 0 23 7 0 -29 2 -11 0 32 40 -20 -20 0 -20 0 60 40 0 30 149 45 17 77 -20 -28 12 23 40 -52 -48 -111 0 0 66 -3 -80 -20 -49 -17 -17')
-PAR["bias"] = {n + 1000 * q: 100 * int(v) for q in (0, 1) for n, v in enumerate(SHIFT[q].split())}
-SAME_WAR = True
-KEYS = []
 
 
 def cuts(k):
     return list(zip(PAR[k][:-1], PAR[k][1:]))
 
-SCRATCH = {
-    "X": ("sbuf", [128, XW], "bfloat16"), "XR": ("sbuf", [128, RO * XW], "bfloat16"),
-    "Ei": ("sbuf", [128, V_N], "int32"), "E": ("sbuf", [128, V_N + 64], "float32"),
-    "vi": ("sbuf", [128, 4], "int32"), "wi": ("sbuf", [128, 1], "int32"),
-    "vL": ("sbuf", [128, 8], "uint16"), "v128": ("sbuf", [128, 8], "float32"),
-    "c1h": ("sbuf", [128, 64], "float16"), "c1f": ("sbuf", [128, 64], "float32"),
-    "L1": ("sbuf", [128, 64], "uint16"), "pC": ("sbuf", [128, 32], "float32"), "sC": ("sbuf", [128, 32], "float32"),
-    "Xp": ("sbuf", [128, 512], "bfloat16"), "c2h": ("sbuf", [128, 512], "float16"),
-    "c128": ("sbuf", [128, 512], "bfloat16"),
-    "L2": ("sbuf", [128, 512], "uint16"), "Spp": ("sbuf", [128, 256], "float32"),
-    "dS": ("sbuf", [128, 32], "float16"),
-    "Xpb": ("sbuf", [128, XW], "bfloat16"), "m": ("sbuf", [128, XW], "bfloat16"),
-    "Gs": ("sbuf", [128, XW], "bfloat16"), "absd": ("sbuf", [128, XW], "bfloat16"),
-    "Fb": ("sbuf", [128, XW], "bfloat16"), "SO": ("sbuf", [128, XW], "bfloat16"),
-    "dead": ("sbuf", [128, 256], "bfloat16"), "lo": ("sbuf", [128, 256], "float32"),
-    "st": ("sbuf", [128, 256], "float32"), "subl": ("sbuf", [128, 32], "uint16"),
-    "nXs": ("sbuf", [128, 512], "bfloat16"), "ok": ("sbuf", [128, 256], "bfloat16"),
-    "I16": ("sbuf", [128, 128], "float16"), "n16": ("sbuf", [128, 32], "float16"),
-    "Z": ("sbuf", [128, 3 * 1536], "bfloat16"), "ns": ("sbuf", [128, 32], "bfloat16"),
-    "ha": ("sbuf", [128, 192], "int32"), "hl": ("sbuf", [128, 32], "uint16"),
-    "dd": ("sbuf", [128, 512], "bfloat16"), "ad": ("sbuf", [128, 512], "bfloat16"), "sm": ("sbuf", [128, 512], "bfloat16"),
-    "tf": ("sbuf", [128, 512], "float32"), "ask": ("sbuf", [128, 32], "bfloat16"), "cum": ("sbuf", [128, 32], "bfloat16"),
-    "idx": ("sbuf", [128, 32], "uint16"), "pr": ("sbuf", [128, 64], "float32"),
-    "U": ("sbuf", [128, 64], "float32"), "AB": ("sbuf", [128, 256], "float32"), "fm": ("sbuf", [128, 256], "float32"),
-    "lf": ("sbuf", [128, 16], "float32"), "off": ("sbuf", [128, 4], "uint16"),
-    "gi": ("sbuf", [128, 16], "int32"), "af": ("sbuf", [128, 40], "float32"), "thr": ("sbuf", [128, 2], "float32"),
-    "yvs": ("sbuf", [128, 8], "float32"),
-    "pi": ("sbuf", [128, 8], "int32"), "col": ("sbuf", [128, 32], "float32"),
-    "D1": ("sbuf", [128, 144], "float32"), "D16": ("sbuf", [128, 128], "float32"), "D8": ("sbuf", [128, 128], "float32"),
-    "cc": ("sbuf", [128, 64], "float32"), "lq": ("sbuf", [128, 64], "float32"),
-    "I": ("sbuf", [128, 128], "bfloat16"), "In": ("sbuf", [128, 128], "bfloat16"),
-    "W4": ("sbuf", [128, 144], "bfloat16"), "Wn": ("sbuf", [128, 144], "bfloat16"), "Ww": ("sbuf", [128, 144], "bfloat16"),
-    "Lo16": ("sbuf", [128, 144], "float16"), "Hi16": ("sbuf", [128, 144], "float16"),
-    "Lo32": ("sbuf", [128, 144], "float32"), "Hi32": ("sbuf", [128, 144], "float32"),
-    "RP": ("sbuf", [128, 144], "float16"), "RS": ("sbuf", [128, 144], "float16"),
-    "G0": ("sbuf", [128, 144], "float32"), "G1": ("sbuf", [128, 144], "float32"),
-    "P0": ("sbuf", [128, 144], "float32"), "P1": ("sbuf", [128, 144], "float32"),
-    "B16": ("sbuf", [128, 128], "bfloat16"), "B8": ("sbuf", [128, 128], "bfloat16"),
-    "TL": ("sbuf", [128, 128], "bfloat16"), "TL0": ("sbuf", [128, 128], "bfloat16"),
-    "Sel": ("sbuf", [128, 2048], "bfloat16"), "rs8": ("sbuf", [128, 2048], "bfloat16"),
-    "rsB": ("sbuf", [128, 256], "float32"), "c89": ("sbuf", [128, 128], "bfloat16"), "one": ("sbuf", [128, 128], "bfloat16"),
-    "IO": ("sbuf", [128, V_N], "float32"), "nC": ("sbuf", [128, 128], "float32"), "nC0": ("sbuf", [128, 128], "float32"),
-    "RL": ("sbuf", [128, 32], "uint16"), "lL": ("sbuf", [128, 32], "float32"), "mk": ("sbuf", [128, 16], "float32"),
-    "wb": ("sbuf", [128, 2], "bfloat16"),
-    "b0": ("psum", [128, 4, 8, 16], "float32"), "b1": ("psum", [128, 4, 8, 16], "float32"),
-    "b2": ("psum", [128, 512], "float32"), "b3": ("psum", [128, 512], "float32"),
-    "b4": ("psum", [128, 512], "float32"), "b5": ("psum", [128, 512], "float32"),
-    "b6": ("psum", [128, 512], "float32"), "b7": ("psum", [128, 64, 8], "float32"),
-}
+
+BF, HF, FL, I32, U16 = "bfloat16", "float16", "float32", "int32", "uint16"
+SCRATCH = {}
+for _dt, _list in (
+    (BF, "X:4096 XR:24576 c128:512 Xp:1024 Gs:3584 Wd:8704 dead:256 ok:256 nXs:512 ns:32 dd:512 sm:512 "
+         "I:128 In:128 Ia:128 W1:144 W14:144 Wn:144 Ww:144 B16:128 B8a:128 B8b:128 Sel:2048 big:2048 rs8:512 one:128 "
+         "cA:32 cB:32 wb:2"),
+    (HF, "c1h:64 c1e:64 c2h:512 c2e:512 gh:4 G0:144 G1:144 st:256 hT:32 hR:32 SF:32 ask:32 cum:32 I16:128 N16:128 I4k:128 n16:32 nn:128 on16:32 "
+         "Lo:144 Hi:144 LoK:144 HiK:144 HiS:144 RS:144 RX0:144 RX1:144 WJ0:144 WJ1:144 WJ2:144 WJ3:144 "
+         "WH0:144 WH1:144 WH2:144 WH3:144 Bn:128 TLq:128 Da0:128 Da1:128 Db:128"),
+    (FL, "E:1600 v128:8 c1f:64 De:64 NH:64 m12:64 base:64 m3:64 tf:128 U:64 AB:256 fm:256 lf:16 af:40 thr:2 yvs:8 "
+         "col:40 D1:144 D2:144 D16:128 D8:128 cc:64 lq:64 Es:1600 Ds:64 m1:64 P0:144 P1:144 IO:1536 lL:32 mk:64"),
+    (I32, "Ei:1536 vi:4 wi:1 ha:160 gi:16 pi:12"),
+    (U16, "vL:8 L1:96 L2s:224 subl:32 hl:32 idx:32 off:4"),
+):
+    for _w in _list.split():
+        SCRATCH[_w.split(":")[0]] = ("sbuf", [128, int(_w.split(":")[1])], _dt)
+SCRATCH.update({
+    "m": ("sbuf", [128, 4, 1024], BF), "Z": ("sbuf", [128, 8, 512], BF), "pc": ("sbuf", [128, 32, 16], BF),
+    "ad": ("sbuf", [128, 32, 16], BF), "L2p": ("sbuf", [128, 4, 64], U16),
+    "b0": ("psum", [128, 32, 16], FL), "b1": ("psum", [128, 32, 16], FL),
+    "b2": ("psum", [128, 512], FL), "b3": ("psum", [128, 512], FL), "b4": ("psum", [128, 8, 64], FL),
+    "b5": ("psum", [128, 512], FL), "b6": ("psum", [128, 512], FL), "b7": ("psum", [128, 64, 8], FL),
+})
 SEMAPHORES = (["cz", "ca", "cv", "cs", "cp", "cg", "ld0", "ld1", "ld2", "ld3", "st0", "st1", "st2", "st3", "st4"]
               + ["snt%d" % t for t in range(RO)] + ["arr%d" % t for t in range(RO)])
 COUNTER = {"V": "cv", "S": "cs", "P": "cp", "G": "cg"}
-TWO = ("bfloat16", "float16", "uint16")
-CM = {"v0": 64, "s0": 80, "g0": 200, "gat": 1.6, "sca": 3.8, "pe": 0.55, "pe0": 0, "x": 200, "same": 170, "tt": 2.0}
+TWO = (BF, HF, U16)
+CM = {"v0": 64, "s0": 80, "g0": 200, "gat": 1.6, "sca": 3.8, "pe": 0.55, "x": 200, "same": 170, "tt": 2.0}
 S_ = slice
+ALL = slice(None)
 
 
 def R(name, a=None, b=None, s=None):
     return (name, (S_(a, b, s),))
 
 
-def IND(name, a, b, lst):
-    return ("ind", R(name, a, b), lst)
+def Q(name, *idx):
+    return (name, idx)
+
+
+def IND(win, lst):
+    return ("ind", win, lst)
 
 
 def cols(ref):
@@ -118,7 +84,7 @@ def ap(T, x):
         return x
     if x[0] == "ind":
         return ap(T, x[1]).indirect(ap(T, x[2]))
-    return T[x[0]][(S_(None),) + x[1]]
+    return T[x[0]][(ALL,) + x[1]]
 
 
 def count(ref):
@@ -129,8 +95,9 @@ def build():
     ops = []
     hist = {}
     bank = {}
+    tag = ["pre"]
 
-    def add(eng, cost, emit, rd, wr, sig=None, lat=0, ext=()):
+    def add(eng, cost, emit, rd, wr, sig=None, lat=0):
         me = len(ops)
         deps = {}
         reads, writes = [], []
@@ -149,24 +116,22 @@ def build():
                 if SCRATCH[name][0] == "psum":
                     last = bank.setdefault(name, {})
                     for e, o in last.items():
-                        if o != me and (e != eng or eng == "P"):
+                        if o != me:
                             deps[o] = deps.get(o, False) or e != eng
-                    if eng in last and last[eng] != me and eng != "P":
-                        deps.setdefault(last[eng], False)
                     last[eng] = me
                     continue
                 mask = np.zeros(int(np.prod(SCRATCH[name][1][1:])), bool)
                 mask[cols(r)] = True
                 keep = []
                 for o, k, mk in hist.setdefault(name, []):
-                    hit = o != me and (k == "w" or kind == "w") and bool(np.any(mk & mask))
-                    if hit:
-                        deps[o] = deps.get(o, False) or (k == "w" and kind == "r") or SAME_WAR
+                    if o != me and (k == "w" or kind == "w") and bool(np.any(mk & mask)):
+                        deps[o] = True
                     if not (kind == "w" and o != me and not np.any(mk & ~mask)):
                         keep.append((o, k, mk))
                 keep.append((me, kind, mask))
                 hist[name] = keep
-        ops.append({"eng": eng, "cost": cost, "emit": emit, "deps": deps, "sig": sig, "lat": lat, "ext": ext})
+        ops.append({"eng": eng, "cost": cost, "emit": emit, "deps": deps, "sig": sig, "lat": lat, "ext": [],
+                    "name": tag[0] + ":" + (wr[0][1][0] if wr and wr[0][0] == "ind" else wr[0][0] if wr else "-")})
         return me
 
     def vcost(out, ins):
@@ -184,24 +149,26 @@ def build():
             return [g.vector.tensor_scalar(ap(T, out), ap(T, a), ap(T, s1), ap(T, s2), op0, op1)]
         return add("V", vcost(out, [a]), emit, [a, s1, s2], [out])
 
-    def tt(out, a, b, op, ext=()):
+    def tt(out, a, b, op):
         c = vcost(out, [a, b])
-        if a[0] != "ind":
+        if a[0] != "ind" and out[0] != "ind":
             c = CM["v0"] + count(a) * (1.0 if "psum" in (SCRATCH[a[0]][0], SCRATCH[b[0]][0]) else CM["tt"])
-        return add("V", c, lambda g, T: [g.vector.tensor_tensor(ap(T, out), ap(T, a), ap(T, b), op)], [a, b], [out], ext=ext)
+        return add("V", c, lambda g, T: [g.vector.tensor_tensor(ap(T, out), ap(T, a), ap(T, b), op)], [a, b], [out])
 
     def cp(out, a):
         return add("V", vcost(out, [a]), lambda g, T: [g.vector.tensor_copy(ap(T, out), ap(T, a))], [a], [out])
 
-    def scan(out, a, b, op0, op1, first=0.0):
+    def turn(out, a):
+        return add("V", vcost(out, [a]), lambda g, T: [g.vector.transpose(ap(T, out), ap(T, a))], [a], [out])
+
+    def scan(out, a, b, op0, op1):
         return add("V", vcost(out, [a, b]),
-                   lambda g, T: [g.vector.tensor_tensor_scan(ap(T, out), ap(T, a), ap(T, b), ap(T, first), op0, op1)],
-                   [a, b, first], [out])
+                   lambda g, T: [g.vector.tensor_tensor_scan(ap(T, out), ap(T, a), ap(T, b), 0.0, op0, op1)], [a, b], [out])
 
     def mset(out, val):
         return add("V", vcost(out, [out]), lambda g, T: [g.vector.memset(ap(T, out), val)], [], [out])
 
-    def act(out, a, func, bias=0.0, scale=1.0, acc=None):
+    def act(out, a, func=ACT.Identity, bias=0.0, scale=1.0, acc=None):
         def emit(g, T):
             if acc is not None:
                 return [g.scalar.activation(ap(T, out), ap(T, a), func, bias=ap(T, bias), scale=scale, accum_out=ap(T, acc))]
@@ -209,25 +176,18 @@ def build():
         c = CM["s0"] + count(a) * (CM["gat"] if a[0] == "ind" else 1.0) + (25 if acc else 0)
         return add("S", c, emit, [a, bias, scale], [out] + ([acc] if acc else []))
 
-    def mm(seq):
+    def mm(seq, start=True, stop=True):
         def emit(g, T):
-            res = []
-            for o, l, r, a, b in seq:
-                i = g.tensor.matmul(ap(T, o), ap(T, l), ap(T, r), a, b)
-                if b or (o, l, r, a, b) == seq[-1]:
-                    res.append(i)
-            return res
-        c = sum(CM["pe0"] + CM["pe"] * max(64, count(r)) * (4 if dtp(r) == "float32" else 1) for o, l, r, a, b in seq)
-        me = add("P", c, emit, [x for q in seq for x in q[1:3]], [q[0] for q in seq])
-        ops[me]["incs"] = sum(1 for q in seq if q[4] or q == seq[-1])
-        return me
-
-    def grp(out, pairs, start=True, stop=True):
-        return [(out, l, r, start and n == 0, stop and n == len(pairs) - 1) for n, (l, r) in enumerate(pairs)]
+            res = None
+            for n, (o, l, r) in enumerate(seq):
+                res = g.tensor.matmul(ap(T, o), ap(T, l), ap(T, r), start and n == 0, stop and n == len(seq) - 1)
+            return [res]
+        c = sum(CM["pe"] * max(64, count(r)) * (4 if dtp(r) == FL else 1) for o, l, r in seq)
+        return add("P", c, emit, [x for q in seq for x in q[1:3]], [q[0] for q in seq])
 
     def iota(out, pattern, base, cm):
         def emit(g, T):
-            if dtp(out) == "int32":
+            if dtp(out) == I32:
                 return [g.iota(ap(T, out), pattern, base, cm)]
             return [g.iota(ap(T, out), pattern, base, cm, allow_small_or_imprecise_dtypes=True)]
         return add("G", 160 + 2 * count(out), emit, [], [out])
@@ -240,8 +200,19 @@ def build():
     def dma(eng, sem, emit, rd, wr, nbytes):
         return add(eng, 60, emit, rd, wr, sig=(sem, 16), lat=2000 + nbytes / 250.0)
 
+    def sign(eng, out, a, bound, below):
+        if eng == "S":
+            return act(out, a, ACT.Sign, bias=bound if below else -bound, scale=-1.0 if below else 1.0)
+        return ts(out, a, bound, ALU.is_lt if below else ALU.is_gt, -0.5, ALU.add)
+
     def c_(n):
         return R("col", n, n + 1)
+
+    def mk(n):
+        return R("mk", n, n + 1)
+
+    A_ = 1.0 if PAR["dead"] == "S" else 0.5
+    B_ = 1.0 if PAR["ok"] == "S" else 0.5
 
     dma("Y", "ld0", lambda g, T: [g.sync.dma_start(T.vi[:], T.v0[:])], [], [R("vi")], 2048)
     dma("Y", "ld1", lambda g, T: [g.sync.dma_start(T.Ei[:], T.e0[:])], [], [R("Ei")], 786432)
@@ -250,92 +221,121 @@ def build():
 
     iota(R("pi", 0, 1), [[0, 1]], 0, 1)
     iota(R("D1"), [[1, 144]], 0, -1)
-    iota(R("D16"), [[16, 8], [0, 16]], 0, -1)
     iota(R("cc"), [[1, 64]], 0, 0)
+    iota(R("D2"), [[2, 72], [0, 2]], 0, -1)
+    iota(R("D16"), [[16, 8], [0, 16]], 0, -1)
     iota(R("D8"), [[8, 16], [0, 8]], 0, -1)
-    for n, k in ((1, 15), (2, 7), (3, 8), (4, 16)):
-        ts(R("pi", n, n + 1), R("pi", 0, 1), k, ALU.bitwise_and)
-    cp(R("col", 0, 4), R("pi", 1, 5))
-    r_, j_, hi_, kk_ = c_(0), c_(1), c_(2), c_(3)
-    ts(c_(4), hi_, 125.0, ALU.mult, 8.0, ALU.add)
-    ts(c_(5), hi_, -125.0, ALU.mult, 1008.0, ALU.add)
-    ts(c_(6), j_, -3.0, ALU.mult, c_(4), ALU.add)
-    ts(c_(7), j_, -3.0, ALU.mult, c_(5), ALU.add)
-    ts(R("RS"), R("D1"), 1.0, ALU.add, c_(7), ALU.is_equal)
-    ts(R("RP"), R("D1"), -7.0, ALU.add, c_(6), ALU.is_equal)
-    ts(R("Lo16"), R("D1"), c_(4), ALU.is_equal)
-    ts(R("Hi16"), R("D1"), c_(5), ALU.is_equal)
-    ts(c_(8), r_, -1.0, ALU.mult, 16.0, ALU.add)
-    ts(R("W4"), R("D1"), c_(8), ALU.is_equal, 4096.0, ALU.mult)
-    act(R("Wn"), R("W4"), ACT.Identity, scale=-1.0 / 131072)
-    cp(c_(9), R("wi"))
-    ts(R("Ww"), R("D1"), c_(8), ALU.is_equal, c_(9), ALU.mult)
+    for n, k in enumerate((15, 7, 8, 16, 3, 12, 14, 24)):
+        ts(R("pi", n + 1, n + 2), R("pi", 0, 1), k, ALU.bitwise_and)
+    cp(R("col", 0, 8), R("pi", 1, 9))
+    r_, j_, hi_, kk_, q3, q12, q14, q24 = [c_(n) for n in range(8)]
+    ts(c_(8), hi_, 125.0, ALU.mult, 8.0, ALU.add)
+    ts(c_(9), hi_, -125.0, ALU.mult, 1008.0, ALU.add)
+    ts(c_(10), j_, -3.0, ALU.mult, c_(9), ALU.add)
+    ts(R("RS"), R("D1"), 1.0, ALU.add, c_(10), ALU.is_equal)
+    ts(R("mk", 0, 4), R("cc", 0, 16, 4), q12, ALU.is_equal)
+    ts(R("mk", 4, 8), R("cc", 0, 8, 2), q14, ALU.is_equal)
+    ts(c_(11), q3, -4.0, ALU.mult, 14.0, ALU.add)
+    ts(c_(12), c_(11), r_, ALU.subtract)
+    for ih in (0, 1):
+        ts(R("RX%d" % ih), R("D2"), c_(12), ALU.is_equal, mk(1 - ih), ALU.mult)
+    for jq in range(4):
+        ts(R("WJ%d" % jq), R("D1"), 16.0 - 2 * jq, ALU.is_equal, mk(4 + jq), ALU.mult)
+    ts(R("Lo"), R("D1"), c_(8), ALU.is_equal)
+    ts(R("Hi"), R("D1"), c_(9), ALU.is_equal)
+    act(R("HiS"), R("Hi"), scale=A_ / 2048)
+    act(R("LoK"), R("Lo"), scale=2048 / A_)
+    act(R("HiK"), R("Hi"), scale=2048 / A_)
+    ts(c_(13), r_, -1.0, ALU.mult, 16.0, ALU.add)
+    ts(R("W1"), R("D1"), c_(13), ALU.is_equal)
+    act(R("Wn"), R("W1"), scale=-1.0)
+    act(R("W14"), R("W1"), scale=16384.0)
+    cp(c_(14), R("wi"))
+    act(R("Ww"), R("W1"), scale=c_(14))
     ts(R("I"), R("D1", 0, 128), 0.0, ALU.is_equal)
-    act(R("In"), R("I"), ACT.Identity, scale=-512.0)
-    ts(R("Lo32"), R("D1"), c_(4), ALU.is_equal)
-    ts(R("Hi32"), R("D1"), c_(5), ALU.is_equal)
-    ts(c_(10), kk_, 100.0, ALU.mult, 16.0, ALU.add)
-    ts(c_(11), kk_, -100.0, ALU.mult, 1600.0, ALU.add)
-    ts(R("G0"), R("D1"), c_(10), ALU.is_equal)
-    ts(R("G1"), R("D1"), c_(11), ALU.is_equal)
+    act(R("In"), R("I"), scale=-1.0)
+    act(R("Ia"), R("I"), scale=-256.0 / A_)
+    cp(R("I16"), R("I"))
+    ts(R("N16"), R("I"), -1.0, ALU.mult)
+    ts(R("I4k"), R("I"), 4096.0, ALU.mult)
+    ts(c_(15), kk_, 100.0, ALU.mult, 16.0, ALU.add)
+    ts(c_(16), kk_, -100.0, ALU.mult, 1600.0, ALU.add)
+    ts(R("G0"), R("D1"), c_(15), ALU.is_equal)
+    ts(R("G1"), R("D1"), c_(16), ALU.is_equal)
     ts(R("B16"), R("D16"), r_, ALU.add, 0.0, ALU.is_equal)
-    ts(R("B8"), R("D8"), j_, ALU.add, 0.0, ALU.is_equal)
-    ts(R("TL0"), R("D1", 0, 128), 0.0, ALU.is_lt, -1.0, ALU.mult)
-    tt(R("TL"), R("TL0"), R("B16"), ALU.mult)
-    mset(R("Fb", 0, 2048), 128.0)
-    add("G", CM["g0"] + 4096, lambda g, T: [g.affine_select(T.Sel[:], T.Fb[:, 0:2048], [[1, 16], [16, 8], [0, 16]],
-                                                            ALU.is_equal, 0.0, 0, -1)], [R("Fb", 0, 2048)], [R("Sel")])
+    ts(R("B8a"), R("D8"), j_, ALU.add, 0.0, ALU.is_equal)
+    act(R("B8b"), R("B8a"), scale=A_ / B_)
+    ts(R("Bn"), R("B16"), -1.0 / 512, ALU.mult)
+    ts(R("Db"), R("D1", 0, 128), 0.0, ALU.is_le, -1.0, ALU.mult)
+    tt(R("TLq"), R("Db"), R("Bn"), ALU.mult)
+    ts(c_(28), hi_, r_, ALU.add, 256.0, ALU.mult)
+    ts(c_(18), r_, -1.0, ALU.mult, 0.3125, ALU.add)
+    for kh in (0, 1):
+        ts(c_(29 + kh), c_(28), 1792.0 * kh - 8192, ALU.add)
+        act(R("Da%d" % kh), R("I"), scale=c_(29 + kh))
+    ts(R("Db"), R("I"), c_(18), ALU.mult)
+    ts(R("n16"), R("cc", 0, 32), 16.0, ALU.mult, r_, ALU.add)
+    mset(R("big"), 128.0 / B_)
+    add("G", CM["g0"] + 4096, lambda g, T: [g.affine_select(T.Sel[:], T.big[:], [[1, 16], [16, 8], [0, 16]],
+                                                            ALU.is_equal, 0.0, 0, -1)], [R("big")], [R("Sel")])
     mset(R("rs8"), 1.0)
     mset(R("rs8", 0, None, 8), 0.0)
-    mset(R("c89"), 28.5 / 32)
     mset(R("c128"), 128.0)
     mset(R("one"), 1.0)
-    mset(R("thr", 0, 1), 49.0)
+    mset(R("on16"), 1.0)
+    mset(R("cA"), -float(2 ** 25))
+    ts(c_(19), j_, -2048.0, ALU.mult, 7 * 2048.0, ALU.add)
+    ts(R("cB"), R("one", 0, 32), c_(19), ALU.mult)
+    mset(R("thr", 0, 1), -31.0 * A_)
     mset(R("E", V_N, V_N + 64), 0.0)
     iota(R("IO"), [[128, V_N]], 0, 0)
     iota(R("lq"), [[1, 2], [2, 32]], 0, 0)
-    iota(R("nC0"), [[1024, 4], [16, 32]], 0, 0)
-    act(R("nC"), R("nC0"), ACT.Identity, bias=r_)
-    ts(R("n16"), R("nC", 0, 32), 512.0, ALU.add)
-    cp(R("I16"), R("I"))
-    mset(R("Z", 0, 1536 * len(cuts("T"))), 0.0)
     iota(R("lL", 16, 20), [[1, 2], [32, 2]], 0, 0)
     ts(R("lL", 0, 4), R("cc", 0, 64, 16), r_, ALU.add)
     ts(R("lL", 4, 8), R("lL", 16, 20), r_, ALU.add, r_, ALU.add)
     ts(R("lL", 8, 16), R("lL", 0, 8), float(V_N), ALU.add, 128.0, ALU.mult)
-    for K in sorted(set(b - a for a, b in cuts("B"))):
-        n = 12 + K // 8
-        ts(c_(n), r_, 8.0 * K, ALU.mult, 7.0, ALU.add)
-        ts(R("RL", K, 2 * K), R("cc", 0, K), 8.0, ALU.mult, c_(n), ALU.add)
-    ts(c_(17), j_, -2048.0, ALU.mult, float(8 * 2048 - C0), ALU.add)
-    ts(R("mk", 0, 8), R("cc", 0, 8), j_, ALU.is_equal)
-    ts(R("mk", 8, 16), R("cc", 0, 8), j_, ALU.is_equal, float(-C0), ALU.mult)
     ts(R("lL", 24, 32), R("lL", 0, 8), float(2 ** 18), ALU.mult)
+    ts(R("mk", 8, 16), R("cc", 0, 8), j_, ALU.is_equal)
+    ts(R("mk", 16, 24), R("cc", 0, 8), j_, ALU.is_equal, 2048.0, ALU.mult)
+    ts(R("mk", 24, 28), R("cc", 0, 32, 8), q24, ALU.is_equal)
+    for n in range(4):
+        ts(R("WH%d" % n), R("D1"), 16.0 - 8 * n, ALU.is_equal, mk(24 + n), ALU.mult)
+    ts(c_(22), hi_, 1.0, ALU.mult, -8.0, ALU.add)
+    ts(c_(23), c_(22), j_, ALU.mult, 0.125, ALU.mult)
+    ts(R("nn", 0, 64), R("cc"), c_(22), ALU.mult, c_(23), ALU.add)
+    ts(R("nn", 64, 128), R("lq"), c_(22), ALU.mult, c_(23), ALU.add)
+    ts(R("mk", 44, 48), R("cc", 0, 4), -2.0, ALU.add, c_(22), ALU.mult)
+    ts(R("mk", 48, 52), R("mk", 44, 48), -128.0, ALU.mult)
+    ts(c_(24), hi_, -256.0, ALU.mult)
     cp(R("wb", 0, 1), R("wi"))
-    mm(grp(R("b3", 0, 1), [(R("B16"), R("wb", 0, 1))]))
-    ts(c_(18), R("b3", 0, 1), 128.0, ALU.mult)
-    ts(c_(19), j_, c_(4), ALU.add, -7.0, ALU.add)
-    ts(c_(20), j_, c_(5), ALU.add, -15.0, ALU.add)
+    mm([(R("b3", 0, 1), R("B16"), R("wb", 0, 1))])
+    ts(c_(25), R("b3", 0, 1), 128.0, ALU.mult)
+    ts(c_(26), j_, c_(8), ALU.add, -7.0, ALU.add)
+    ts(c_(27), j_, c_(9), ALU.add, -15.0, ALU.add)
     cp(R("vL", 0, 4), R("vi"))
     ts(R("v128", 0, 4), R("vi"), 128.0, ALU.mult)
     gcopy(R("E", 0, V_N), R("Ei"))
+    gcopy(R("Es", 0, V_N), R("Ei"))
+    mset(R("Es", V_N, V_N + 64), 0.0)
+    for a in (3584, 5120, 6656):
+        gcopy(R("Wd", a, a + 1536), R("big", 0, 1536))
 
     def W(name, o):
         return R(name, o, o + 128)
-    lolo, lohi, hilo, hihi = (8, "Lo"), (0, "Lo"), (16, "Hi"), (8, "Hi")
 
-    def sh(which, bits):
-        return W(which[1] + bits, which[0])
+    def move(src, dst, scaled=""):
+        return W(("Lo", "Hi")[src] + scaled, 8 + 8 * src - 8 * dst)
 
-    def send(t):
-        def emit(g, T):
-            return [("send", t)]
-        return add("G", 2200 if t else 4000, emit, [R("X")], [], sig=("snt%d" % t, 16), lat=11000)
+    Xw, Xs = R("X", 0, XW), R("X", 0, V_N)
+    key, tr, top, FB = [R("tf", 32 * n, 32 * n + 32) for n in range(4)]
+    pi_ = Q("pc", ALL, ALL)
 
-    f = {}
-    names = ["SF", "thK", "hp", "d1", "nh", "ds", "ix", "k1", "Rk", "k2", "FB", "key", "tr", "M", "d2", "t"]
-    for n, k in enumerate(names):
-        f[k] = R("tf", 32 * n, 32 * n + 32)
+    def h_(n):
+        return R("ha", 32 * n, 32 * n + 32)
+
+    def sub_list(src, k0, k1):
+        mm([(Q("b7", S_(k0, k1), ALL), move(1, h), R(src, 16 * k0 + h, 16 * k1, 2)) for h in (0, 1)])
+        ts(R("L2s", 7 * k0, 7 * k1), Q("b7", S_(k0, k1), S_(0, 7)), 2048.0, ALU.add)
 
     for t in range(RO):
         last = t == RO - 1
@@ -343,234 +343,212 @@ def build():
         vo = 4 * (t % 2)
         vn = 4 - vo
         vl = R("vL", vo, vo + 4)
-        EW = "Ei" if nat else "E"
+        Ew = R("Ei" if nat else "E", 0, V_N)
         reg = 1024 * (t % 4)
-        sent = send(t)
+        tag[0] = "%d.front" % t
+        sent = add("G", 2200 if t else 4000, lambda g, T, t=t: [("send", t)], [R("X")], [], sig=("snt%d" % t, 16), lat=11000)
         ops[sent]["round"] = t
 
-        def half(name, h):
-            return R(name, h, 64, 2) if nat else R(name, 32 * h, 32 * h + 32)
-        ts(R("c1h"), IND(EW, 0, V_N, vl), -2048.0, ALU.add)
-        mm(grp(R("b6", 0, 32), [(W("RS", 1 - h), half("c1h", h)) for h in (0, 1)])
-           + grp(R("b6", 32, 64), [(W("RP", 1 - h), half("c1h", h)) for h in (0, 1)]))
-        ts(R("L1"), R("b6", 0, 64), 2048.0, ALU.add)
-        mm(grp(R("b2", 0, 32), [(sh(lolo, "16"), half("c1h", 0)), (sh(lohi, "16"), half("c1h", 1))])
-           + grp(R("b2", 32, 64), [(sh(hilo, "16"), half("c1h", 0)), (sh(hihi, "16"), half("c1h", 1))]))
-        act(R("pC"), R("b2", 0, 32), ACT.Identity, bias=2048.0)
-        act(R("sC"), R("b2", 32, 64), ACT.Identity, bias=float(TH4))
-        where = {}
-        for c, (k0, k1) in enumerate(cuts("L")):
-            K = k1 - k0
-            ks = S_(k0, k1)
-            ts(R("c2h", 16 * k0, 16 * k1), IND(EW, 0, V_N, R("L1", k0, k1)), -2048.0, ALU.add)
-            ev, od = R("c2h", 16 * k0, 16 * k1, 2), R("c2h", 16 * k0 + 1, 16 * k1, 2)
-            mm(grp(("b7", (ks, S_(None))), [(sh(hilo, "16"), ev), (sh(hihi, "16"), od)]))
-            mm(grp(R("b4", 8 * k0, 8 * k1), [(sh(lolo, "16"), ev), (sh(lohi, "16"), od)]))
-            ts(R("L2", 16 * k0 + 8 * K, 16 * k0 + 15 * K), ("b7", (ks, S_(0, 7))), 2048.0, ALU.add)
-            ts(R("L2", 16 * k0, 16 * k0 + 8 * K), R("b4", 8 * k0, 8 * k1), 2048.0, ALU.add)
-            if PAR["spp"] or k1 == 32:
-                e = k0 if PAR["spp"] else 0
-                act(R("Spp", 8 * e, 8 * k1), ("b7", (S_(e, k1), S_(None))), ACT.Identity, bias=float(TH4))
-            for k in range(k0, k1):
-                where[k] = (16 * k0 + 8 * (k - k0), 16 * k0 + 8 * K + 7 * (k - k0))
-        for c, (k0, k1) in enumerate(cuts("X")):
-            act(R("Xp", 16 * k0, 16 * k1), IND("X", 0, XW, R("L1", 32 + k0, 32 + k1)), ACT.Identity)
-            for j, e in enumerate(PAR["XE"][c]):
-                dst, src = R("Xpb", 128 * k0 + j, 128 * k1, 8), R("Xp", 16 * k0, 16 * k1)
-                if e == "S":
-                    act(dst, src, ACT.Identity)
-                else:
-                    (gcopy if e == "G" else cp)(dst, src)
-        tt(R("U"), IND("IO", 0, V_N, vl), R("cc" if nat else "lq"), ALU.add)
+        def half(name, h, row=None):
+            s = S_(h, 64, 2) if nat else S_(32 * h, 32 * h + 32)
+            return Q(name, s) if row is None else Q(name, row, s)
+        ts(R("c1h"), IND(Ew, vl), -2048.0, ALU.add)
+        own = nat or not PAR["early"]
+        mm([(R("b5", 0, 32), W("RS", 1 - h), half("c1h", h)) for h in (0, 1) if own]
+           + [(R("b5", 32 + ih, 96, 2), W("RX%d" % ih, 2 - 2 * h), half("c1h", h)) for ih in (0, 1) for h in (0, 1)])
+        ts(R("L1", 0 if own else 32, 96), R("b5", 0 if own else 32, 96), 2048.0, ALU.add)
+        mm([(R("b6", 0, 32), move(1, h), half("c1h", h)) for h in (0, 1)])
+        act(FB, R("b6", 0, 32), bias=mk(16 + t), scale=mk(8 + t))
+        act(R("c1f"), R("c1h"), bias=2048.0)
+        for k0, k1 in cuts("L"):
+            ts(R("c2h", 16 * k0, 16 * k1), IND(Ew, R("L1", k0, k1)), -2048.0, ALU.add)
+            for j0, j1 in cuts("LJ"):
+                for jq in range(j0, j1):
+                    mm([(Q("b4", jq, S_(2 * k0, 2 * k1)), W("WJ%d" % jq, 16 - 2 * h - 4 * il),
+                         R("c2h", 16 * k0 + 2 * il + h, 16 * k1, 8)) for h in (0, 1) for il in range(4)])
+                ts(Q("L2p", S_(j0, j1), S_(2 * k0, 2 * k1)), Q("b4", S_(j0, j1), S_(2 * k0, 2 * k1)), 2048.0, ALU.add)
+            if own or PAR["early"] < 2:
+                sub_list("c2h", k0, k1)
+        for e, (k0, k1) in zip(PAR["XE"], cuts("X")):
+            (act if e == "S" else cp)(R("Xp", 32 * k0, 32 * k1), IND(Xw, R("L1", 32 + 2 * k0, 32 + 2 * k1)))
+        tag[0] = "%d.lead" % t
+        tt(R("U"), IND(R("IO", 0, V_N), vl), R("cc" if nat else "lq"), ALU.add)
+        lo_ = 0 if nat else 4
         for c in range(4):
             act(R("AB", 64 * c, 64 * c + 64), R("U"), ACT.Abs, bias=R("v128", vo + c, vo + c + 1), scale=-1.0)
-        lo_ = 0 if nat else 4
         for c in range(4):
             act(R("fm", 64 * c, 64 * c + 64), R("AB", 64 * c, 64 * c + 64), ACT.Relu,
                 bias=R("lL", 24 + lo_ + c, 25 + lo_ + c), scale=-float(2 ** 18), acc=R("lf", c, c + 1))
         tt(R("lf", 4, 8), R("lf", 0, 4), R("lL", 8 + lo_, 12 + lo_), ALU.min)
         tt(R("lf", 8, 12), R("lf", 4, 8), R("v128", vo, vo + 4), ALU.max)
         ts(R("off"), R("lf", 8, 12), 1.0 / 128, ALU.mult)
-        act(f["FB"], R("sC"), ACT.Identity, bias=R("mk", 8 + t, 9 + t), scale=R("mk", t, t + 1))
-        for a, b in cuts("M"):
-            o = where[a][0]
-            tt(R("m", 128 * a, 128 * b), IND("X", 0, XW, R("L2", o, o + 8 * (b - a))),
-               R("Xpb", 128 * a, 128 * b), ALU.min)
-        for c, (a, b) in enumerate(cuts("N")):
-            o = where[a][1]
-            src = IND("X", 0, XW, R("L2", o, o + 7 * (b - a)))
-            if PAR["NE"][c] == "S":
-                act(R("Gs", 112 * a, 112 * b), src, ACT.Identity)
-            else:
-                cp(R("Gs", 112 * a, 112 * b), src)
-        for c, (k0, k1) in enumerate(cuts("A")):
-            zm = R(("b5", "b6")[c % 2], 8 * k0, 8 * k1)
-            mm(grp(zm, [(W("W4", 16 - x), R("m", 128 * k0 + x, 128 * k1, 16)) for x in range(16)]))
-            ts(R("dead", 8 * k0, 8 * k1), zm, float(TH4), ALU.is_lt)
-            tt(R("lo", 8 * k0, 8 * k1), zm, R("Spp", 8 * k0, 8 * k1), ALU.min)
-            scan(R("st", 8 * k0, 8 * k1), R("dead", 8 * k0, 8 * k1), R("lo", 8 * k0, 8 * k1), ALU.mult, ALU.max)
-            ts(R("subl", k0, k1), R("st", 8 * k0 + 7, 8 * k1, 8), float(-C0), ALU.add, 0.0, ALU.max)
-            act(R("nXs", 16 * k0, 16 * k1), IND("X", 0, XW, R("subl", k0, k1)), ACT.Identity, scale=-1.0)
+        old, was = R("Wd", 8192, 8704), R("X", reg, reg + 512)
+        add("Y", 60, lambda g, T, was=was: [g.sync.dma_start(T.Wd[:, 8192:8704], ap(T, was))], [was], [old],
+            sig=("cz", 16 * (t + 1)), lat=3000)
+        add("G", 1800, lambda g, T: [g.dma_start(T.Wd[:, 8192:8704], T.c128[:], accum_op=ALU.add)], [old, R("c128")], [old],
+            sig=("ca", 16 * (t + 1)), lat=3000)
+        tag[0] = "%d.main" % t
+
+        def pairs(x, k0, k1):
+            h, jq, jl = x // 8, x % 8 // 2, x % 2
+            return Q("m", jq, S_(32 * k0 + 2 * h + jl, 32 * k1, 4))
+        for k0, k1 in cuts("N"):
+            act(R("Gs", 112 * k0, 112 * k1), IND(Xs, R("L2s", 7 * k0, 7 * k1)))
+        for c, (k0, k1) in enumerate(cuts("M")):
+            zm = R(("b5", "b6")[c % 2], 0, 8 * (k1 - k0))
+            for jq in range(4):
+                tt(Q("m", jq, S_(32 * k0, 32 * k1)), IND(Xw, Q("L2p", jq, S_(2 * k0, 2 * k1))),
+                   R("Xp", 32 * k0, 32 * k1), ALU.min)
+                mm([(zm, W("W1", 16 - x), pairs(x, k0, k1)) for x in (2 * jq, 2 * jq + 1, 2 * jq + 8, 2 * jq + 9)],
+                   jq == 0, jq == 3)
+            dead = R("dead", 8 * k0, 8 * k1)
+            sign(PAR["dead"], dead, zm, 71.5, True)
+            cand = R(zm[0], 256, 256 + 8 * (k1 - k0))
+            mm([(cand, move(1, h, "S"), R("c2h", 16 * k0 + h, 16 * k1, 2)) for h in (0, 1)] + [(cand, R("In"), dead)])
+            scan(R("st", 8 * k0, 8 * k1), dead, cand, ALU.min, ALU.max)
+            ts(R("subl", k0, k1), R("st", 8 * k0 + 7, 8 * k1, 8), 2048 / A_, ALU.mult)
+            act(R("nXs", 16 * k0, 16 * k1), IND(Xs, R("subl", k0, k1)), scale=-1.0)
         nd = [0, 0]
-
-        def h_(n, a=0, b=32):
-            return R("ha", 32 * n + a, 32 * n + b)
-
-        def f_(n, a, b):
-            return R("tf", f[n][1][0].start + a, f[n][1][0].start + b)
-
-        def names_records(p, a, b):
-            zb, n = 1536 * p, b - a
-            pi_ = R("Z", zb + 16 * a, zb + 16 * b)
-            mm(grp(R("b5", a, b), [(R("B8"), R(q, 8 * a + i, 8 * b, 8)) for q in ("dead", "ok") for i in range(8)]))
-            ts(R("ns", a, b), R("b5", a, b), R("thr", t % 2, t % 2 + 1), ALU.is_lt, -float(2 ** 24), ALU.mult)
-            ts(h_(0, a, b), R("b4", a, b), c_(18), ALU.subtract)
-            ts(h_(1, a, b), h_(0, a, b), XW - 1, ALU.bitwise_and)
-            ts(h_(2, a, b), h_(1, a, b), -4064.0, ALU.add)
-            ts(h_(3, a, b), h_(1, a, b), 4096.0, ALU.add)
-            tt(h_(4, a, b), h_(3, a, b), h_(2, a, b), ALU.mult)
-            ts(h_(5, a, b), h_(4, a, b), 5, ALU.arith_shift_right, XW - 1, ALU.bitwise_and)
-            cp(R("hl", a, b), h_(5, a, b))
-            mm(grp(R("b5", 32 + a, 32 + b), [(R("I"), R("ns", a, b))]
-                   + [(W("W4", 16 - x), R("Z", zb + 16 * a + x, zb + 16 * b, 16)) for x in range(16)]))
-            ts(f_("thK", a, b), R("b5", 32 + a, 32 + b), float(2 ** 23), ALU.is_lt, -1000.0, ALU.mult)
-            if b == 32:
-                ts(f["SF"], R("b5", 32, 64), float(2 ** 23), ALU.is_ge)
-                if PAR["k1"] == "V":
-                    ts(f["k1"], R("b5", 32, 64), -float(2 ** 23), ALU.add, 4.0, ALU.mult)
-                else:
-                    act(f["k1"], R("b5", 32, 64), ACT.Identity, bias=-float(2 ** 25), scale=4.0)
-            for u, v in ((a, b),) if n <= PAR["dd"] else ((a, (a + b) // 2), ((a + b) // 2, b)):
-                tt(R("dd", 16 * u, 16 * v), IND("X", 0, XW, R("hl", u, v)), R("Z", zb + 16 * u, zb + 16 * v), ALU.subtract)
-                act(R("ad", 16 * u, 16 * v), R("dd", 16 * u, 16 * v), ACT.Abs, bias=128.0)
-            mm(grp(R("b6", 64 + a, 64 + b), [(R("I"), R("c89", 0, n))]
-                   + [(W("Wn", 16 - x), R("ad", 16 * a + x, 16 * b, 16)) for x in range(16)]))
-            tt(R("ask", a, b), R("b6", 64 + a, 64 + b), f_("thK", a, b), ALU.is_lt)
-            old, was = R("Z", zb + 512 + 16 * a, zb + 512 + 16 * b), R("X", reg + 16 * a, reg + 16 * b)
-            if PAR["old"] == "S":
-                act(old, was, ACT.Identity, bias=128.0)
-            else:
-                add("Y", 60, lambda g, T: [g.sync.dma_start(ap(T, old), ap(T, was))], [was], [old],
-                    sig=("cz", 16 * (t + 1)), lat=3000)
-                add("G", 1800, lambda g, T: [g.dma_start(ap(T, old), T.c128[:], accum_op=ALU.add)], [old, R("c128")], [old],
-                    sig=("ca", 16 * (t + 1)), lat=3000)
-            got, avg = IND("XR", XW * t, XW * (t + 1), R("hl", a, b)), R("Z", zb + 1024 + 16 * a, zb + 1024 + 16 * b)
-            if PAR["rec"] == "V":
-                tt(R("sm", 16 * a, 16 * b), got, pi_, ALU.add, ext=[("arr%d" % t, 16)])
-                act(avg, R("sm", 16 * a, 16 * b), ACT.Identity, bias=63.75, scale=0.5)
-            else:
-                for u, v in ((a, (a + b) // 2), ((a + b) // 2, b)):
-                    me = ops[act(R("sm", 16 * u, 16 * v), IND("XR", XW * t, XW * (t + 1), R("hl", u, v)), ACT.Identity)]
-                    me["ext"] = [("arr%d" % t, 16)] if u == a else []
-                    me["deps"][sent if u == a else len(ops) - 2] = True
-                mm(grp(R("b3", 0, 16 * n), [(R("I"), pi_), (R("I"), R("sm", 16 * a, 16 * b))]))
-                act(avg, R("b3", 0, 16 * n), ACT.Identity, bias=63.75, scale=0.5)
-            scan(R("cum", a, b), R("one", 0, n), R("ask", a, b), ALU.mult, ALU.add, R("cum", a - 1, a) if a else 0.0)
-            ak = R("ask", a, b)
-            mm(grp(R("b5", 64 + a, 64 + b), [(R("TL"), ak), (R("In"), ak), (R("B16"), R("cum", a, b))])
-               + grp(R("b5", 96 + a, 96 + b), [(R("I16"), R("n16", a, b)), (R("In"), ak)]))
-            ts(f_("t", a, b), R("b5", 64 + a, 64 + b), -351.0, ALU.is_lt, 1024.0, ALU.mult)
-            tt(f_("ix", a, b), R("b5", 96 + a, 96 + b), f_("t", a, b), ALU.add)
-            cp(R("idx", a, b), f_("ix", a, b))
-
+        u, cnt = Q("b7", S_(0, 4), ALL), Q("b1", S_(0, 2), ALL)
+        K = Q("b0", S_(0, 2), ALL)
         for c, (k0, k1) in enumerate(cuts("B")):
-            K = k1 - k0
-            part = [p for p, (a, b) in enumerate(cuts("T")) if a <= k0 < b][0]
+            n = k1 - k0
             for a in range(k0, k1, 4):
                 bk = "b%d" % (nd[0] % 2)
                 nd[0] += 1
-                whole = (bk, (S_(None), S_(0, 7), S_(None)))
-                mm([(whole, R("I"), R("Gs", 112 * a, 112 * a + 448), True, False)])
-                mm([((bk, (S_(None), i, S_(None))), R("I"), R("nXs", 16 * a, 16 * a + 64), False, i == 6) for i in range(7)])
-                act(R("absd", 112 * a, 112 * a + 448), whole, ACT.Abs)
-            zd = ("b7", (S_(k0, k1), S_(None)))
-            mm([(zd, R("I"), R("c89", 0, 8 * K), True, False)]
-               + [(("b7", (S_(k0, k1), S_(0, 7))), W("Wn", 16 - x), R("absd", 112 * k0 + x, 112 * k1, 16), False, x == 15)
-                  for x in range(16)])
-            tt(R("ok", 8 * k0, 8 * k1), zd, R("dead", 8 * k0, 8 * k1), ALU.is_gt)
-            per = 64 // K
+                whole = Q(bk, S_(0, 28), ALL)
+                mm([(whole, R("I"), R("Gs", 112 * a, 112 * a + 448))], True, False)
+                mm([(Q(bk, S_(i, 28, 7), ALL), R("I"), R("nXs", 16 * a, 16 * a + 64)) for i in range(7)], False, True)
+                act(R("Wd", 112 * a, 112 * a + 448), whole, ACT.Abs)
+            zd = Q("b7", S_(k0, k1), ALL)
+            mm([(zd, R("Ia"), R("dead", 8 * k0, 8 * k1))]
+               + [(Q("b7", S_(k0, k1), S_(0, 7)), W("Wn", 16 - x), R("Wd", 112 * k0 + x, 112 * k1, 16)) for x in range(16)])
+            ok = R("ok", 8 * k0, 8 * k1)
+            sign(PAR["ok"], ok, zd, 227.5, False)
+            per = min(16, 64 // n)
             for x0 in range(0, 16, per):
                 bk = "b%d" % (2 + nd[1] % 2)
                 nd[1] += 1
                 xs = range(x0, x0 + per)
-                one = [(R(bk, 8 * K * (x - x0), 8 * K * (x - x0 + 1)), R("I"), R("m", 128 * k0 + x, 128 * k1, 16)) for x in xs]
-                two = [(R(bk, 8 * K * (x - x0), 8 * K * (x - x0 + 1)), W("Sel", 128 * x), R("ok", 8 * k0, 8 * k1)) for x in xs]
-                if PAR["pre"]:
-                    mm([q + (q is one[0], False) for q in one])
-                    mm([q + (False, q is two[-1]) for q in two])
-                else:
-                    mm([q for u, v in zip(one, two) for q in (u + (True, False), v + (False, True))])
-                o = 128 * k0 + 8 * K * x0
-                if PAR["BE"][c] == "S":
-                    act(R("Fb", o, o + 512), R(bk), ACT.Identity)
-                    if (x0 // per) % 2 == 0 and x0 + per < 16:
-                        continue
-                    xs = range(max(x0 - per, 0), x0 + per)
-                    o = 128 * k0 + 8 * K * xs[0]
-                    w = 8 * K * len(xs)
-                    scan(R("SO", o, o + w), R("rs8", 0, w), R("Fb", o, o + w), ALU.mult, ALU.max)
-                else:
-                    scan(R("SO", o, o + 512), R("rs8", 0, 512), R(bk), ALU.mult, ALU.max)
-                if k1 == 32 or PAR["uso"]:
-                    mm([(R("b4", k0, k1), W("Ww", 16 - x), R("SO", 128 * k0 + 8 * K * x + 7, 128 * k0 + 8 * K * (x + 1), 8),
-                         x == 0, x == 15) for x in xs])
-            zb = 1536 * part
-            act(R("Z", zb + 16 * k0, zb + 16 * k1), IND("SO", 128 * k0, 128 * k1, R("RL", K, 2 * K)), ACT.Identity)
-            a, b = cuts("T")[part]
-            if not PAR["uso"]:
-                e = min(b, PAR["B"][-2])
-                if k1 == e:
-                    mm(grp(R("b4", a, e), [(W("Ww", 16 - x), R("Z", zb + 16 * a + x, zb + 16 * e, 16)) for x in range(16)]))
-            if k1 == b:
-                names_records(part, a, b)
+                mm([(R(bk, 8 * n * (x - x0), 8 * n * (x - x0 + 1)), R("I"), pairs(x, k0, k1)) for x in xs], True, False)
+                mm([(R(bk, 8 * n * (x - x0), 8 * n * (x - x0 + 1)), W("Sel", 128 * x), ok) for x in xs], False, True)
+                scan(Q("Z", x0 // 2 + c, ALL), R("rs8"), R(bk), ALU.mult, ALU.max)
+                row = 2 * x0 + 8 * (c // 2)
+                gcopy(Q("pc", S_(row, row + 8), S_(k0 % 16, k0 % 16 + 8)), Q("Z", x0 // 2 + c, S_(7, 512, 8)))
+        tag[0] = "%d.hash" % t
+        for h in (0, 1):
+            gcopy(R("Wd", 4096 * h, 4096 * h + 4096, 16), Q("pc", S_(16 * h, 16 * h + 16), ALL))
+        for c in (0, 1):
+            mm([(u, W("Ww", 16 - 8 * c - y), Q("Z", S_(c, 8, 2), S_(8 * y + 7, 512, 64))) for y in range(8)], c == 0, c == 1)
+        ts(h_(0), u, c_(25), ALU.subtract)
+        ts(h_(1), h_(0), XW - 1, ALU.bitwise_and)
+        ts(h_(2), h_(1), 32.0, ALU.add)
+        tt(h_(3), h_(1), h_(2), ALU.mult)
+        ts(h_(4), h_(3), 5, ALU.arith_shift_right, XW - 1, ALU.bitwise_and)
+        cp(R("hl"), h_(4))
+        tag[0] = "%d.stand" % t
+        mm([(cnt, R("B8a"), R("dead", i, 256, 8)) for i in range(8)], True, False)
+        mm([(cnt, R("B8b"), R("ok", i, 256, 8)) for i in range(8)], False, True)
+        ts(R("ns"), cnt, R("thr", t % 2, t % 2 + 1), ALU.is_lt, -float(2 ** 25), ALU.mult)
         sub = R("st", 7, 256, 8)
-        tt(f["ds"], sub, R("sC"), ALU.subtract)
-        act(f["Rk"], sub, ACT.Identity, bias=c_(17))
-        tt(f["hp"], h_(5), R("pC"), ALU.subtract)
-        tt(f["nh"], R("nC", 32 * (t % 4), 32 * (t % 4) + 32), h_(5), ALU.subtract)
-        tt(f["d1"], f["hp"], f["SF"], ALU.mult)
-        tt(R("dS"), f["ds"], f["SF"], ALU.mult)
-        tt(f["k2"], f["k1"], f["Rk"], ALU.add)
-        tt(f["key"], f["k2"], f["FB"], ALU.max)
-        add("V", CM["v0"] + 32, lambda g, T: [g.vector.transpose(ap(T, f["tr"]), ap(T, f["key"]))], [f["key"]], [f["tr"]])
-        scan(f["M"], R("rs8", 0, 32), f["tr"], ALU.mult, ALU.max)
-        mo = f["M"][1][0].start
-        seq = []
-        for kk in (0, 1):
-            seq += grp(R("b2", kk, 4, 2), [(W("G%d" % kk, 16 - 16 * gp), R("tf", mo + 16 * gp + 7, mo + 16 * gp + 16, 8)) for gp in (0, 1)])
-        mm(seq)
-        cp(R("gi", 0, 4), R("b2", 0, 4))
+        mm([(K, R("I"), R("cA")), (K, R("I"), R("cB")), (K, R("I"), R("ns"))], True, False)
+        mm([(K, W("W14", 16 - x), Q("Z", S_(x // 8 * 4, x // 8 * 4 + 4), S_(x % 8 * 64 + 7, x % 8 * 64 + 64, 8))) for x in range(16)]
+           + [(K, move(h, h, "K"), sub) for h in (0, 1)], False, True)
+        ts(R("SF"), K, 0.0, ALU.is_ge)
+        tt(key, K, FB, ALU.max)
+        tag[0] = "%d.ask" % t
+        Y = Q("b1", S_(2, 4), ALL)
+        mm([(Y, R("I4k"), R("SF"))], True, False)
+        for x0, x1 in cuts("D"):
+            tt(R("dd", 32 * x0, 32 * x1), IND(Xw, R("hl", 2 * x0, 2 * x1)), R("Wd", 512 * x0, 512 * x1, 16), ALU.subtract)
+            act(Q("ad", S_(2 * x0, 2 * x1), ALL), R("dd", 32 * x0, 32 * x1), ACT.Abs, bias=128.0)
+            mm([(Y, W("W1", 16 - x), Q("ad", S_(2 * x0 + x % 8, 2 * x1, 8), ALL)) for x in range(x0, x1)], False, x1 == 16)
+        ts(R("ask"), Y, 4096 + 28.5, ALU.is_gt)
+        tag[0] = "%d.rec" % t
+        for a, b in ((0, 16), (16, 32)):
+            got = IND(R("XR", XW * t, XW * (t + 1)), R("hl", a, b))
+            if PAR["rec"] == "S":
+                me = ops[act(R("sm", 16 * a, 16 * b), got)]
+            else:
+                me = ops[tt(R("sm", 16 * a, 16 * b), got, R("Wd", 256 * a, 256 * b, 16), ALU.add)]
+            me["ext"] = [("arr%d" % t, 16)] if a == 0 else []
+            me["deps"][sent if a == 0 else len(ops) - 2] = True
+        if PAR["rec"] == "S":
+            mm([(Q("b0", ALL, ALL), R("I"), pi_), (Q("b0", ALL, ALL), R("I"), R("sm"))])
+        act(R("Wd", 1, 8192, 16), Q("b0", ALL, ALL) if PAR["rec"] == "S" else R("sm"), bias=63.75, scale=0.5)
+        tag[0] = "%d.go" % t
+        turn(tr, key)
+        scan(top, R("rs8", 0, 32), tr, ALU.mult, ALU.max)
+        cp(R("gi", 0, 4), R("tf", 64 + 7, 96, 8))
         ts(R("gi", 4, 8), R("gi", 0, 4), 2047, ALU.bitwise_and)
+        cp(R("gh"), R("gi", 4, 8))
+        mm([(R("b2", kk, 4, 2), W("G%d" % kk, 16 - 16 * gp), R("gh", 2 * gp, 2 * gp + 2)) for kk in (0, 1) for gp in (0, 1)])
         if not last:
-            cp(R("vL", vn, vn + 4), R("gi", 4, 8))
-            ts(R("v128", vn, vn + 4), R("gi", 4, 8), 128.0, ALU.mult)
-            mm(grp(R("b3", 0, 32), [(R("one"), R("ns"))]))
-            act(R("af", 0, 32), R("b3", 0, 32), ACT.Identity, scale=-1.0 / 2 ** 27, acc=R("af", 32, 33))
+            cp(R("vL", vn, vn + 4), R("b2", 0, 4))
+            act(R("v128", vn, vn + 4), R("b2", 0, 4), scale=128.0)
+            mm([(R("b3", 0, 32), R("one"), R("ns"))])
+            act(R("af", 0, 32), R("b3", 0, 32), scale=-1.0 / 2 ** 28, acc=R("af", 32, 33))
             cp(R("gi", 8, 9), R("af", 32, 33))
             ts(R("gi", 9, 10), R("gi", 8, 9), 7, ALU.bitwise_and)
-            ts(R("thr", 1 - t % 2, 2 - t % 2), R("gi", 9, 10), -1.0, ALU.mult, 49.0, ALU.add)
+            ts(R("thr", 1 - t % 2, 2 - t % 2), R("gi", 9, 10), -2.0 * A_, ALU.mult, -31.0 * A_, ALU.add)
         else:
-            ts(R("P0"), R("D1"), c_(19), ALU.is_equal)
-            ts(R("P1"), R("D1"), c_(20), ALU.is_equal)
-            cp(R("yvs", 0, 4), R("gi", 4, 8))
-            seq = []
-            for b in (0, 1):
-                seq += grp(R("b3", b, 4, 2), [(W("P%d" % b, 1 - h), R("yvs", 2 * h, 2 * h + 2)) for h in (0, 1)])
-            mm(seq)
-            act(R("yvs", 4, 8), R("b3", 0, 4), ACT.Identity)
+            ts(R("P0"), R("D1"), c_(26), ALU.is_equal)
+            ts(R("P1"), R("D1"), c_(27), ALU.is_equal)
+            cp(R("yvs", 0, 4), R("b2", 0, 4))
+            mm([(R("b3", b, 4, 2), W("P%d" % b, 1 - h), R("yvs", 2 * h, 2 * h + 2)) for b in (0, 1) for h in (0, 1)])
+            act(R("yvs", 4, 8), R("b3", 0, 4))
             dma("Y", "st0", lambda g, T: [g.sync.dma_start(T.yv[:], T.yvs[:, 4:8])], [R("yvs", 4, 8)], [], 2048)
-        pair = R("b4", 0, 64)
-        mm([(pair, R("I16"), R("c1h"), True, False)]
-           + [(half("b4", h), sh((lohi, hihi)[h], "16"), R("dS"), False, False) for h in (0, 1)])
-        mm([(half("b4", h), sh((lolo, hilo)[h], "32"), f["d1"], False, False) for h in (0, 1)])
-        tt(f["d2"], R("ask"), f["nh"], ALU.mult)
-        mm([(half("b4", h), sh((lolo, hilo)[h], "32"), f["d2"], False, h == 1) for h in (0, 1)])
-        ts(R("pr"), pair, 2048.0, ALU.add)
-        cp(IND("E", 0, V_N + 64, R("off")), R("pr"))
+        tag[0] = "%d.name" % t
+        ts(R("hT"), h_(4), -2048.0, ALU.add)
+        turn(R("hR"), R("hT"))
+
+        def hashed(bk):
+            return [(R(bk, 32 * kh + h, 32 * kh + 32, 2) if nat else R(bk, 32 * h + 16 * kh, 32 * h + 16 * kh + 16),
+                     W("WH%d" % (2 * h + kh), 16 - 16 * gp), R("hR", 16 * gp, 16 * gp + 16))
+                    for h in (0, 1) for kh in (0, 1) for gp in (0, 1)]
+        subs = [(R("b6", 0, 64), R("N16"), R("c1h"))] + [(half("b6", h), move(h, 1, "K"), sub) for h in (0, 1)]
+        mm([(half("b4", h, 0), move(h, d), R("SF")) for h in (0, 1) for d in (0, 1)])
+        if PAR["early"] and not last:
+            tag[0] = "%d.early" % t
+            mm(subs)
+            act(R("Ds"), R("b6", 0, 64), bias=c_(24))
+            tt(R("m1"), Q("b4", 0, ALL), R("Ds"), ALU.mult)
+            tt(IND(R("Es", 0, V_N + 64), R("off")), R("m1"), R("c1f"), ALU.add)
+            ts(R("c1e"), IND(R("Es", 0, V_N), R("vL", vn, vn + 4)), -2048.0, ALU.add)
+            mm([(R("b3", 0, 32), W("RS", 1 - h), R("c1e", 32 * h, 32 * h + 32)) for h in (0, 1)])
+            ts(R("L1", 0, 32), R("b3", 0, 32), 2048.0, ALU.add)
+            if PAR["early"] == 2:
+                for k0, k1 in cuts("LE"):
+                    ts(R("c2e", 16 * k0, 16 * k1), IND(R("Es", 0, V_N), R("L1", k0, k1)), -2048.0, ALU.add)
+                    sub_list("c2e", k0, k1)
+            tag[0] = "%d.name" % t
+        mm(subs, True, False)
+        mm(hashed("b6"), False, True)
+        act(R("De"), R("b6", 0, 64), bias=c_(24))
+        mm([(R("b5", 0, 64), R("I16"), R("nn", 0, 64) if nat else R("nn", 64, 128))] + hashed("b5"))
+        act(R("NH"), R("b5", 0, 64), bias=mk(48 + t % 4), scale=-1.0)
+        tt(R("m12"), Q("b4", 0, ALL), R("De"), ALU.mult)
+        tt(R("base"), R("m12"), R("c1f"), ALU.add)
+        mm([(half("b4", h, 1), move(h, 0), R("ask")) for h in (0, 1)])
+        tt(R("m3"), Q("b4", 1, ALL), R("NH"), ALU.mult)
+        tt(IND(R("E", 0, V_N + 64), R("off")), R("base"), R("m3"), ALU.add)
         if last:
             dma("Y", "st1", lambda g, T: [g.sync.dma_start(T.ye[:], T.E[:, 0:V_N])], [R("E", 0, V_N)], [], 786432)
-        for p, (a, b) in enumerate(cuts("T")):
-            act(R("X", reg + 16 * a, reg + 16 * b), IND("Z", 1536 * p, 1536 * (p + 1), R("idx", a, b)), ACT.Identity, bias=-128.0)
+        tag[0] = "%d.pick" % t
+        scan(R("cum"), R("on16"), R("ask"), ALU.mult, ALU.add)
+        ix = R("b2", 32, 64)
+        mm([(ix, R("I16"), R("n16")), (ix, R("Db"), R("ask")), (ix, R("TLq"), R("ask"))]
+           + [(R("b2", 32 + 16 * kh, 48 + 16 * kh), R("Da%d" % kh), R("ask", 16 * kh, 16 * kh + 16)) for kh in (0, 1)], True, False)
+        mm([(ix, R("Bn"), R("cum"))], False, True)
+        ts(R("idx"), ix, 8192 + 511 / 1024, ALU.add)
+        n = len(PAR["pick"])
+        for p, e in enumerate(PAR["pick"]):
+            a, b = 32 * p // n, 32 * (p + 1) // n
+            new, src = R("X", reg + 16 * a, reg + 16 * b), IND(R("Wd", 0, 8704), R("idx", a, b))
+            if e == "S":
+                act(new, src, bias=-128.0)
+            else:
+                ts(new, src, -128.0, ALU.add)
         if t == RO - 2:
             nx = 1024 * ((t + 1) % 4)
             dma("Y", "st2", lambda g, T, nx=nx: [g.sync.dma_start(T.yx[:, 0:nx], T.X[:, 0:nx])], [R("X", 0, nx)], [], 262144)
@@ -580,87 +558,6 @@ def build():
             dma("S", "st4", lambda g, T, reg=reg: [g.scalar.dma_start(T.yx[:, reg:reg + 512], T.X[:, reg:reg + 512])],
                 [R("X", reg, reg + 512)], [], 131072)
     return ops
-
-
-def schedule(ops):
-    n = len(ops)
-    succ = [[] for _ in range(n)]
-    for i, o in enumerate(ops):
-        for d in o["deps"]:
-            succ[d].append(i)
-
-    def gap(d, i):
-        if ops[d]["sig"] is not None:
-            return ops[d]["lat"]
-        if ops[d]["eng"] != ops[i]["eng"]:
-            return CM["x"]
-        return CM["same"] if ops[i]["deps"][d] else 0
-    bl = [0.0] * n
-    for i in range(n - 1, -1, -1):
-        bl[i] = ops[i]["cost"] + max([gap(i, s) + bl[s] for s in succ[i]] + [ops[i]["lat"]])
-    first = -1000
-    for i, o in enumerate(ops):
-        first = i if "round" in o else first
-        o["pos"] = i - first
-        bl[i] += PAR["bias"].get(i - first, 0) + (1e6 * (4 - i) if i < 4 else 0)
-    left = [len(o["deps"]) for o in ops]
-    ready = [0.0] * n
-    pool = {e: [] for e in "VSPGY"}
-    for i in range(n):
-        if left[i] == 0:
-            pool[ops[i]["eng"]].append(i)
-    free = {e: 0.0 for e in pool}
-    order, end = [], [0.0] * n
-    while len(order) < n:
-        best = None
-        for e in pool:
-            if pool[e]:
-                at = max(free[e], min(ready[i] for i in pool[e]))
-                if best is None or at < best[0]:
-                    best = (at, e)
-        at, e = best
-        now = [i for i in pool[e] if ready[i] <= at]
-        i = max(now, key=lambda q: bl[q])
-        soon = [q for q in pool[e] if at < ready[q] < at + min(0.5 * ops[i]["cost"], 250) and bl[q] > bl[i] + ops[i]["cost"]]
-        if soon:
-            i = max(soon, key=lambda q: bl[q])
-            at = ready[i]
-        pool[e].remove(i)
-        end[i] = at + ops[i]["cost"]
-        free[e] = end[i]
-        ops[i]["at"] = at
-        order.append(i)
-        for s in succ[i]:
-            ready[s] = max(ready[s], end[i] + gap(i, s))
-            left[s] -= 1
-            if left[s] == 0:
-                pool[ops[s]["eng"]].append(s)
-    return order
-
-
-def by_keys(ops, keys):
-    n = len(ops)
-    place, succ, left = [0] * n, [[] for _ in range(n)], [len(o["deps"]) for o in ops]
-    t, first = -1, 0
-    for i, o in enumerate(ops):
-        if "round" in o:
-            t, first = o["round"], i
-        tab = keys[0] if t < 0 else keys[1] if t == 0 else keys[3] if t == RO - 1 else keys[2]
-        place[i] = tab[min(i - first, len(tab) - 1)] + (keys[4] + keys[5] * t if t > 0 else 0)
-        o["at"] = place[i]
-        for d in o["deps"]:
-            succ[d].append(i)
-    pool = [i for i in range(n) if left[i] == 0]
-    order = []
-    while pool:
-        i = min(pool, key=lambda q: (place[q], q))
-        pool.remove(i)
-        order.append(i)
-        for s in succ[i]:
-            left[s] -= 1
-            if left[s] == 0:
-                pool.append(s)
-    return order
 
 
 def links(ops, cm):
@@ -688,29 +585,21 @@ def place(seq, before, cost, eng, start):
     return end
 
 
-def length(order, before, ops):
+def length(order, before, cost, eng, lat):
     free = {e: 0.0 for e in "VSPGY"}
-    end = [0.0] * len(ops)
+    end = [0.0] * len(cost)
     last = 0.0
     for i in order:
-        o = ops[i]
-        at = free[o["eng"]]
+        at = free[eng[i]]
         for d, g in before[i]:
             if end[d] + g > at:
                 at = end[d] + g
-        end[i] = free[o["eng"]] = at + o["cost"]
-        last = max(last, end[i] + o["lat"])
-    return last
+        end[i] = free[eng[i]] = at + cost[i]
+        last = max(last, end[i] + lat[i])
+    return last, end
 
 
-def improve(ops, tries, seed=1):
-    base = dict(CM)
-    views = []
-    for w, m in VIEWS:
-        CM.update(m)
-        o = build()
-        views.append((w, links(o, CM), o))
-        CM.update(base)
+def schedule(ops):
     n = len(ops)
     cost, eng, lat = [o["cost"] for o in ops], [o["eng"] for o in ops], [o["lat"] for o in ops]
     before = links(ops, CM)
@@ -720,13 +609,14 @@ def improve(ops, tries, seed=1):
     for i in range(n):
         for d, g in before[i]:
             after[d].append((i, g))
-    rng = np.random.RandomState(seed)
-    best = schedule(ops)
-    key = [o["at"] for o in ops]
-    top = sum(w * length(best, b, o) for w, b, o in views)
-    now = top
-    for it in range(tries):
-        shake = rng.normal(0, (30, 120, 400)[it % 3], n) * (rng.rand(n) < 0.3)
+    rest = [0.0] * n
+    for i in range(n - 1, -1, -1):
+        rest[i] = cost[i] + max([g + rest[s] for s, g in after[i]] + [lat[i]])
+    key = [-r for r in rest]
+    rng = np.random.RandomState(1)
+    best, top, now = None, 1e30, 1e30
+    for it in range(PAR["tries"]):
+        shake = rng.normal(0, (30, 120, 400)[it % 3], n) * (rng.rand(n) < 0.3) * (it > 0)
         k = [key[i] + shake[i] for i in range(n)]
         for i in range(n):
             for d, g in before[i]:
@@ -736,7 +626,7 @@ def improve(ops, tries, seed=1):
         end = place(sorted(range(n), key=lambda q: -end[q]), after, cost, eng, lat)
         end = place(sorted(range(n), key=lambda q: -end[q]), before, cost, eng, [0.0] * n)
         order = sorted(range(n), key=lambda q: (end[q] - cost[q], q))
-        v = sum(w * length(order, b, o) for w, b, o in views)
+        v = length(order, before, cost, eng, lat)[0]
         if v < now + 150:
             now, key = v, [end[q] - cost[q] for q in range(n)]
             if v < top:
@@ -746,13 +636,92 @@ def improve(ops, tries, seed=1):
     return best
 
 
-VIEWS = [(0.45, {}), (0.25, {"pe": 0.7, "gat": 1.3}), (0.3, {"x": 200, "same": 120, "gat": 1.7})]
-TRIES = 300
+def refine(ops):
+    n = len(ops)
+    eng = [o["eng"] for o in ops]
+    base, views = dict(CM), []
+    for w, m in VIEWS:
+        CM.update(m)
+        o = build()
+        views.append((w, links(o, CM), [q["cost"] for q in o], [q["lat"] for q in o]))
+        CM.update(base)
+    for v in views:
+        for i in (1, 2, 3):
+            v[1][i].append((i - 1, 0))
+    before, cost, lat = views[0][1:]
+    ids, rnd, seen = [], [], {}
+    for o in ops:
+        nm = o["name"] + o["eng"]
+        t = int(nm[0]) if nm[0].isdigit() else -1
+        seen[nm] = seen.get(nm, 0) + 1
+        ids.append((nm[1:], seen[nm]))
+        rnd.append(t)
+    schedule(ops)
+    at = [o["at"] for o in ops]
+    span = (max(at[i] for i in range(n) if rnd[i] == 4) - max(at[i] for i in range(n) if rnd[i] == 1)) / 3
+    shift = [max(t, 0) * span for t in rnd]
+    key = {}
+    for t in (5, 4, 0, -1, 2):
+        key.update({ids[i]: at[i] - shift[i] for i in range(n) if rnd[i] == t})
+
+    def weigh(key):
+        k = [key[ids[i]] + shift[i] for i in range(n)]
+        for i in range(n):
+            for d, g in before[i]:
+                if k[i] <= k[d]:
+                    k[i] = k[d] + 1e-3
+        order = sorted(range(n), key=lambda q: k[q])
+        res = [length(order, b, c, eng, l) for w, b, c, l in views]
+        return sum(v[0] * r[0] for v, r in zip(views, res)), order, k, res[0][1]
+
+    def chain(order, end):
+        prev, last = {}, {}
+        for i in order:
+            prev[i] = last.get(eng[i])
+            last[eng[i]] = i
+        i = max(range(n), key=lambda q: end[q] + lat[q])
+        res = []
+        while True:
+            start, p = end[i] - cost[i], prev[i]
+            if p is not None and abs(end[p] - start) < 1e-6:
+                res.append((p, i))
+                i = p
+                continue
+            x = [d for d, g in before[i] if abs(end[d] + g - start) < 1e-6]
+            if not x:
+                return res
+            i = x[0]
+    rng = np.random.RandomState(PAR["seed"])
+    now, order, k, end = weigh(key)
+    top, best = now, (order, end)
+    pairs = chain(order, end)
+    for it in range(PAR["swaps"]):
+        a, b = pairs[rng.randint(len(pairs))]
+        new = dict(key)
+        r = rng.rand()
+        if r < 0.4:
+            new[ids[b]] = k[a] - shift[b] - 1 - 300 * rng.rand() ** 3
+        elif r < 0.8:
+            new[ids[a]] = k[b] - shift[a] + 1 + 1500 * rng.rand() ** 3
+        else:
+            new[ids[rng.randint(n)]] += rng.normal(0, 600)
+        v, o2, k2, e2 = weigh(new)
+        if v < now - (125 * (1 - it / PAR["swaps"]) + 5) * np.log(rng.rand() + 1e-9):
+            key, k, now, order, end = new, k2, v, o2, e2
+            pairs = chain(order, end)
+            if v < top:
+                top, best = v, (o2, e2)
+    for i in range(n):
+        ops[i]["at"] = best[1][i] - cost[i]
+    return best[0]
+
+
+VIEWS = [(1.0, {})]
 
 
 def plan():
     ops = build()
-    order = schedule(ops)
+    order = refine(ops)
     cnt = {e: 0 for e in COUNTER}
     known = {e: {} for e in "VSPGY"}
     seen = {}
@@ -778,7 +747,7 @@ def plan():
             seen[s] = max(seen.get(s, 0), v)
         o["waits"] = waits
         if o["sig"] is None:
-            cnt[e] += o.get("incs", 1)
+            cnt[e] += 1
             o["done"] = (COUNTER[e], cnt[e])
         else:
             o["done"] = o["sig"]

import numpy as np
from concourse.mybir import AluOpType, ActivationFunctionType
import comms_topo

ALU = AluOpType
ACT = ActivationFunctionType
NR, V_N, XW, RO = 8, 1536, 4096, 6
PAR = {
    "L": [0, 8, 32],
    "LJ": [0, 4],
    "X": [0, 8, 20, 32],
    "M": [0, 8, 16, 24, 32],
    "N": [0, 4, 8, 12, 16, 20, 24, 28, 32],
    "B": [0, 8, 16, 24, 32],
    "D": [0, 8, 16],
    "early": 1, "LE": [0, 16, 32], "XE": "SSSS",
    "dead": "V", "ok": "V", "pick": "SV", "rec": "S", "sf": "V", "tries": 10, "swaps": 6000, "seed": 1,
}


def cuts(k):
    return list(zip(PAR[k][:-1], PAR[k][1:]))


BF, HF, FL, I32, U16 = "bfloat16", "float16", "float32", "int32", "uint16"
SCRATCH = {}
for _dt, _list in (
    (BF, "X:4096 XR:24576 c128:512 Xp:1024 Gs:3584 Wd:8704 dead:256 ok:256 nXs:512 ns:32 dd:512 sm:512 "
         "I:128 In:128 Ia:128 W1:144 W14:144 Wn:144 Ww:144 B16:128 B8a:128 B8b:128 Sel:2048 big:2048 rs8:512 one:128 "
         "cA:32 cB:32 wb:2"),
    (HF, "c1h:64 c1e:64 c2h:512 c2e:512 gh:4 G0:144 G1:144 st:256 hT:32 hR:32 SF:32 ask:32 cum:32 I16:128 N16:128 I4k:128 n16:32 nn:128 on16:32 "
         "Lo:144 Hi:144 LoK:144 HiK:144 HiS:144 RS:144 RX0:144 RX1:144 WJ0:144 WJ1:144 WJ2:144 WJ3:144 "
         "WH0:144 WH1:144 WH2:144 WH3:144 Bn:128 TLq:128 Da0:128 Da1:128 Db:128"),
    (FL, "E:1600 v128:8 c1f:64 De:64 NH:64 m12:64 base:64 m3:64 tf:128 U:64 AB:256 fm:256 lf:16 af:40 thr:2 yvs:8 "
         "col:40 D1:144 D2:144 D16:128 D8:128 cc:64 lq:64 Es:1600 Ds:64 m1:64 P0:144 P1:144 IO:1536 lL:32 mk:64"),
    (I32, "Ei:1536 vi:4 wi:1 ha:160 gi:16 pi:12"),
    (U16, "vL:8 L1:96 L2s:224 subl:32 hl:32 idx:32 off:4"),
):
    for _w in _list.split():
        SCRATCH[_w.split(":")[0]] = ("sbuf", [128, int(_w.split(":")[1])], _dt)
SCRATCH.update({
    "m": ("sbuf", [128, 4, 1024], BF), "Z": ("sbuf", [128, 8, 512], BF), "pc": ("sbuf", [128, 32, 16], BF),
    "ad": ("sbuf", [128, 32, 16], BF), "L2p": ("sbuf", [128, 4, 64], U16),
    "b0": ("psum", [128, 32, 16], FL), "b1": ("psum", [128, 32, 16], FL),
    "b2": ("psum", [128, 512], FL), "b3": ("psum", [128, 512], FL), "b4": ("psum", [128, 8, 64], FL),
    "b5": ("psum", [128, 512], FL), "b6": ("psum", [128, 512], FL), "b7": ("psum", [128, 64, 8], FL),
})
SEMAPHORES = (["cz", "ca", "cv", "cs", "cp", "cg", "ld0", "ld1", "ld2", "ld3", "st0", "st1", "st2", "st3", "st4"]
              + ["snt%d" % t for t in range(RO)] + ["arr%d" % t for t in range(RO)])
COUNTER = {"V": "cv", "S": "cs", "P": "cp", "G": "cg"}
TWO = (BF, HF, U16)
CM = {"v0": 64, "s0": 80, "g0": 200, "gat": 1.6, "sca": 3.8, "pe": 0.55, "x": 200, "same": 170, "tt": 2.0}
S_ = slice
ALL = slice(None)


def R(name, a=None, b=None, s=None):
    return (name, (S_(a, b, s),))


def Q(name, *idx):
    return (name, idx)


def IND(win, lst):
    return ("ind", win, lst)


def cols(ref):
    shape = SCRATCH[ref[0]][1][1:]
    return np.arange(int(np.prod(shape))).reshape(shape)[ref[1]].ravel()


def dtp(ref):
    return SCRATCH[ref[1][0] if ref[0] == "ind" else ref[0]][2]


def is_ref(x):
    return isinstance(x, tuple)


def ap(T, x):
    if not is_ref(x):
        return x
    if x[0] == "ind":
        return ap(T, x[1]).indirect(ap(T, x[2]))
    return T[x[0]][(ALL,) + x[1]]


def count(ref):
    return 16 * len(cols(ref[2])) if ref[0] == "ind" else len(cols(ref))


def build():
    ops = []
    hist = {}
    bank = {}
    tag = ["pre"]

    def add(eng, cost, emit, rd, wr, sig=None, lat=0):
        me = len(ops)
        deps = {}
        reads, writes = [], []
        for r in rd:
            if is_ref(r):
                reads += [r[1], r[2]] if r[0] == "ind" else [r]
        for w in wr:
            if w[0] == "ind":
                writes.append(w[1])
                reads.append(w[2])
            else:
                writes.append(w)
        for kind, refs in (("r", reads), ("w", writes)):
            for r in refs:
                name = r[0]
                if SCRATCH[name][0] == "psum":
                    last = bank.setdefault(name, {})
                    for e, o in last.items():
                        if o != me:
                            deps[o] = deps.get(o, False) or e != eng
                    last[eng] = me
                    continue
                mask = np.zeros(int(np.prod(SCRATCH[name][1][1:])), bool)
                mask[cols(r)] = True
                keep = []
                for o, k, mk in hist.setdefault(name, []):
                    if o != me and (k == "w" or kind == "w") and bool(np.any(mk & mask)):
                        deps[o] = True
                    if not (kind == "w" and o != me and not np.any(mk & ~mask)):
                        keep.append((o, k, mk))
                keep.append((me, kind, mask))
                hist[name] = keep
        ops.append({"eng": eng, "cost": cost, "emit": emit, "deps": deps, "sig": sig, "lat": lat, "ext": [],
                    "name": tag[0] + ":" + (wr[0][1][0] if wr and wr[0][0] == "ind" else wr[0][0] if wr else "-")})
        return me

    def vcost(out, ins):
        n = count(ins[0])
        if ins[0][0] == "ind":
            return CM["v0"] + CM["gat"] * n
        if out[0] == "ind":
            return CM["v0"] + CM["sca"] * n
        return CM["v0"] + n * (0.5 if all(dtp(x) in TWO for x in [out] + ins) else 1.0)

    def ts(out, a, s1, op0, s2=None, op1=None):
        def emit(g, T):
            if op1 is None:
                return [g.vector.tensor_scalar(ap(T, out), ap(T, a), ap(T, s1), None, op0)]
            return [g.vector.tensor_scalar(ap(T, out), ap(T, a), ap(T, s1), ap(T, s2), op0, op1)]
        return add("V", vcost(out, [a]), emit, [a, s1, s2], [out])

    def tt(out, a, b, op):
        c = vcost(out, [a, b])
        if a[0] != "ind" and out[0] != "ind":
            c = CM["v0"] + count(a) * (1.0 if "psum" in (SCRATCH[a[0]][0], SCRATCH[b[0]][0]) else CM["tt"])
        return add("V", c, lambda g, T: [g.vector.tensor_tensor(ap(T, out), ap(T, a), ap(T, b), op)], [a, b], [out])

    def cp(out, a):
        return add("V", vcost(out, [a]), lambda g, T: [g.vector.tensor_copy(ap(T, out), ap(T, a))], [a], [out])

    def turn(out, a):
        return add("V", vcost(out, [a]), lambda g, T: [g.vector.transpose(ap(T, out), ap(T, a))], [a], [out])

    def scan(out, a, b, op0, op1):
        return add("V", vcost(out, [a, b]),
                   lambda g, T: [g.vector.tensor_tensor_scan(ap(T, out), ap(T, a), ap(T, b), 0.0, op0, op1)], [a, b], [out])

    def mset(out, val):
        return add("V", vcost(out, [out]), lambda g, T: [g.vector.memset(ap(T, out), val)], [], [out])

    def act(out, a, func=ACT.Identity, bias=0.0, scale=1.0, acc=None):
        def emit(g, T):
            if acc is not None:
                return [g.scalar.activation(ap(T, out), ap(T, a), func, bias=ap(T, bias), scale=scale, accum_out=ap(T, acc))]
            return [g.scalar.activation(ap(T, out), ap(T, a), func, bias=ap(T, bias), scale=ap(T, scale))]
        c = CM["s0"] + count(a) * (CM["gat"] if a[0] == "ind" else 1.0) + (25 if acc else 0)
        return add("S", c, emit, [a, bias, scale], [out] + ([acc] if acc else []))

    def mm(seq, start=True, stop=True):
        def emit(g, T):
            res = None
            for n, (o, l, r) in enumerate(seq):
                res = g.tensor.matmul(ap(T, o), ap(T, l), ap(T, r), start and n == 0, stop and n == len(seq) - 1)
            return [res]
        c = sum(CM["pe"] * max(64, count(r)) * (4 if dtp(r) == FL else 1) for o, l, r in seq)
        return add("P", c, emit, [x for q in seq for x in q[1:3]], [q[0] for q in seq])

    def iota(out, pattern, base, cm):
        def emit(g, T):
            if dtp(out) == I32:
                return [g.iota(ap(T, out), pattern, base, cm)]
            return [g.iota(ap(T, out), pattern, base, cm, allow_small_or_imprecise_dtypes=True)]
        return add("G", 160 + 2 * count(out), emit, [], [out])

    def gcopy(out, a):
        n = count(a)
        return add("G", CM["g0"] + 2 * n,
                   lambda g, T: [g.affine_select(ap(T, out), ap(T, a), [[0, n]], ALU.is_gt, 0.0, 1, 0)], [a], [out])

    def dma(eng, sem, emit, rd, wr, nbytes):
        return add(eng, 60, emit, rd, wr, sig=(sem, 16), lat=2000 + nbytes / 250.0)

    def sign(eng, out, a, bound, below):
        if eng == "S":
            return act(out, a, ACT.Sign, bias=bound if below else -bound, scale=-1.0 if below else 1.0)
        return ts(out, a, bound, ALU.is_lt if below else ALU.is_gt, -0.5, ALU.add)

    def c_(n):
        return R("col", n, n + 1)

    def mk(n):
        return R("mk", n, n + 1)

    A_ = 1.0 if PAR["dead"] == "S" else 0.5
    B_ = 1.0 if PAR["ok"] == "S" else 0.5

    dma("Y", "ld0", lambda g, T: [g.sync.dma_start(T.vi[:], T.v0[:])], [], [R("vi")], 2048)
    dma("Y", "ld1", lambda g, T: [g.sync.dma_start(T.Ei[:], T.e0[:])], [], [R("Ei")], 786432)
    dma("Y", "ld2", lambda g, T: [g.sync.dma_start(T.X[:], T.x0[:])], [], [R("X")], 1835008)
    dma("Y", "ld3", lambda g, T: [g.sync.dma_start(T.wi[:], T.wt[:])], [], [R("wi")], 512)

    iota(R("pi", 0, 1), [[0, 1]], 0, 1)
    iota(R("D1"), [[1, 144]], 0, -1)
    iota(R("cc"), [[1, 64]], 0, 0)
    iota(R("D2"), [[2, 72], [0, 2]], 0, -1)
    iota(R("D16"), [[16, 8], [0, 16]], 0, -1)
    iota(R("D8"), [[8, 16], [0, 8]], 0, -1)
    for n, k in enumerate((15, 7, 8, 16, 3, 12, 14, 24)):
        ts(R("pi", n + 1, n + 2), R("pi", 0, 1), k, ALU.bitwise_and)
    cp(R("col", 0, 8), R("pi", 1, 9))
    r_, j_, hi_, kk_, q3, q12, q14, q24 = [c_(n) for n in range(8)]
    ts(c_(8), hi_, 125.0, ALU.mult, 8.0, ALU.add)
    ts(c_(9), hi_, -125.0, ALU.mult, 1008.0, ALU.add)
    ts(c_(10), j_, -3.0, ALU.mult, c_(9), ALU.add)
    ts(R("RS"), R("D1"), 1.0, ALU.add, c_(10), ALU.is_equal)
    ts(R("mk", 0, 4), R("cc", 0, 16, 4), q12, ALU.is_equal)
    ts(R("mk", 4, 8), R("cc", 0, 8, 2), q14, ALU.is_equal)
    ts(c_(11), q3, -4.0, ALU.mult, 14.0, ALU.add)
    ts(c_(12), c_(11), r_, ALU.subtract)
    for ih in (0, 1):
        ts(R("RX%d" % ih), R("D2"), c_(12), ALU.is_equal, mk(1 - ih), ALU.mult)
    for jq in range(4):
        ts(R("WJ%d" % jq), R("D1"), 16.0 - 2 * jq, ALU.is_equal, mk(4 + jq), ALU.mult)
    ts(R("Lo"), R("D1"), c_(8), ALU.is_equal)
    ts(R("Hi"), R("D1"), c_(9), ALU.is_equal)
    act(R("HiS"), R("Hi"), scale=A_ / 2048)
    act(R("LoK"), R("Lo"), scale=2048 / A_)
    act(R("HiK"), R("Hi"), scale=2048 / A_)
    ts(c_(13), r_, -1.0, ALU.mult, 16.0, ALU.add)
    ts(R("W1"), R("D1"), c_(13), ALU.is_equal)
    act(R("Wn"), R("W1"), scale=-1.0)
    act(R("W14"), R("W1"), scale=16384.0)
    cp(c_(14), R("wi"))
    act(R("Ww"), R("W1"), scale=c_(14))
    ts(R("I"), R("D1", 0, 128), 0.0, ALU.is_equal)
    act(R("In"), R("I"), scale=-1.0)
    act(R("Ia"), R("I"), scale=-256.0 / A_)
    cp(R("I16"), R("I"))
    ts(R("N16"), R("I"), -1.0, ALU.mult)
    ts(R("I4k"), R("I"), 4096.0, ALU.mult)
    ts(c_(15), kk_, 100.0, ALU.mult, 16.0, ALU.add)
    ts(c_(16), kk_, -100.0, ALU.mult, 1600.0, ALU.add)
    ts(R("G0"), R("D1"), c_(15), ALU.is_equal)
    ts(R("G1"), R("D1"), c_(16), ALU.is_equal)
    ts(R("B16"), R("D16"), r_, ALU.add, 0.0, ALU.is_equal)
    ts(R("B8a"), R("D8"), j_, ALU.add, 0.0, ALU.is_equal)
    act(R("B8b"), R("B8a"), scale=A_ / B_)
    ts(R("Bn"), R("B16"), -1.0 / 512, ALU.mult)
    ts(R("Db"), R("D1", 0, 128), 0.0, ALU.is_le, -1.0, ALU.mult)
    tt(R("TLq"), R("Db"), R("Bn"), ALU.mult)
    ts(c_(28), hi_, r_, ALU.add, 256.0, ALU.mult)
    ts(c_(18), r_, -1.0, ALU.mult, 0.3125, ALU.add)
    for kh in (0, 1):
        ts(c_(29 + kh), c_(28), 1792.0 * kh - 8192, ALU.add)
        act(R("Da%d" % kh), R("I"), scale=c_(29 + kh))
    ts(R("Db"), R("I"), c_(18), ALU.mult)
    ts(R("n16"), R("cc", 0, 32), 16.0, ALU.mult, r_, ALU.add)
    mset(R("big"), 128.0 / B_)
    add("G", CM["g0"] + 4096, lambda g, T: [g.affine_select(T.Sel[:], T.big[:], [[1, 16], [16, 8], [0, 16]],
                                                            ALU.is_equal, 0.0, 0, -1)], [R("big")], [R("Sel")])
    mset(R("rs8"), 1.0)
    mset(R("rs8", 0, None, 8), 0.0)
    mset(R("c128"), 128.0)
    mset(R("one"), 1.0)
    mset(R("on16"), 1.0)
    mset(R("cA"), -float(2 ** 25))
    ts(c_(19), j_, -2048.0, ALU.mult, 7 * 2048.0, ALU.add)
    ts(R("cB"), R("one", 0, 32), c_(19), ALU.mult)
    mset(R("thr", 0, 1), -31.0 * A_)
    mset(R("E", V_N, V_N + 64), 0.0)
    iota(R("IO"), [[128, V_N]], 0, 0)
    iota(R("lq"), [[1, 2], [2, 32]], 0, 0)
    iota(R("lL", 16, 20), [[1, 2], [32, 2]], 0, 0)
    ts(R("lL", 0, 4), R("cc", 0, 64, 16), r_, ALU.add)
    ts(R("lL", 4, 8), R("lL", 16, 20), r_, ALU.add, r_, ALU.add)
    ts(R("lL", 8, 16), R("lL", 0, 8), float(V_N), ALU.add, 128.0, ALU.mult)
    ts(R("lL", 24, 32), R("lL", 0, 8), float(2 ** 18), ALU.mult)
    ts(R("mk", 8, 16), R("cc", 0, 8), j_, ALU.is_equal)
    ts(R("mk", 16, 24), R("cc", 0, 8), j_, ALU.is_equal, 2048.0, ALU.mult)
    ts(R("mk", 24, 28), R("cc", 0, 32, 8), q24, ALU.is_equal)
    for n in range(4):
        ts(R("WH%d" % n), R("D1"), 16.0 - 8 * n, ALU.is_equal, mk(24 + n), ALU.mult)
    ts(c_(22), hi_, 1.0, ALU.mult, -8.0, ALU.add)
    ts(c_(23), c_(22), j_, ALU.mult, 0.125, ALU.mult)
    ts(R("nn", 0, 64), R("cc"), c_(22), ALU.mult, c_(23), ALU.add)
    ts(R("nn", 64, 128), R("lq"), c_(22), ALU.mult, c_(23), ALU.add)
    ts(R("mk", 44, 48), R("cc", 0, 4), -2.0, ALU.add, c_(22), ALU.mult)
    ts(R("mk", 48, 52), R("mk", 44, 48), -128.0, ALU.mult)
    ts(c_(24), hi_, -256.0, ALU.mult)
    cp(R("wb", 0, 1), R("wi"))
    mm([(R("b3", 0, 1), R("B16"), R("wb", 0, 1))])
    ts(c_(25), R("b3", 0, 1), 128.0, ALU.mult)
    ts(c_(26), j_, c_(8), ALU.add, -7.0, ALU.add)
    ts(c_(27), j_, c_(9), ALU.add, -15.0, ALU.add)
    cp(R("vL", 0, 4), R("vi"))
    ts(R("v128", 0, 4), R("vi"), 128.0, ALU.mult)
    gcopy(R("E", 0, V_N), R("Ei"))
    gcopy(R("Es", 0, V_N), R("Ei"))
    mset(R("Es", V_N, V_N + 64), 0.0)
    for a in (3584, 5120, 6656):
        gcopy(R("Wd", a, a + 1536), R("big", 0, 1536))

    def W(name, o):
        return R(name, o, o + 128)

    def move(src, dst, scaled=""):
        return W(("Lo", "Hi")[src] + scaled, 8 + 8 * src - 8 * dst)

    Xw, Xs = R("X", 0, XW), R("X", 0, V_N)
    key, tr, top, FB = [R("tf", 32 * n, 32 * n + 32) for n in range(4)]
    pi_ = Q("pc", ALL, ALL)

    def h_(n):
        return R("ha", 32 * n, 32 * n + 32)

    def sub_list(src, k0, k1):
        mm([(Q("b7", S_(k0, k1), ALL), move(1, h), R(src, 16 * k0 + h, 16 * k1, 2)) for h in (0, 1)])
        ts(R("L2s", 7 * k0, 7 * k1), Q("b7", S_(k0, k1), S_(0, 7)), 2048.0, ALU.add)

    for t in range(RO):
        last = t == RO - 1
        nat = t == 0
        vo = 4 * (t % 2)
        vn = 4 - vo
        vl = R("vL", vo, vo + 4)
        Ew = R("Ei" if nat else "E", 0, V_N)
        reg = 1024 * (t % 4)
        tag[0] = "%d.front" % t
        sent = add("G", 2200 if t else 4000, lambda g, T, t=t: [("send", t)], [R("X")], [], sig=("snt%d" % t, 16), lat=11000)
        ops[sent]["round"] = t

        def half(name, h, row=None):
            s = S_(h, 64, 2) if nat else S_(32 * h, 32 * h + 32)
            return Q(name, s) if row is None else Q(name, row, s)
        ts(R("c1h"), IND(Ew, vl), -2048.0, ALU.add)
        own = nat or not PAR["early"]
        mm([(R("b5", 0, 32), W("RS", 1 - h), half("c1h", h)) for h in (0, 1) if own]
           + [(R("b5", 32 + ih, 96, 2), W("RX%d" % ih, 2 - 2 * h), half("c1h", h)) for ih in (0, 1) for h in (0, 1)])
        ts(R("L1", 0 if own else 32, 96), R("b5", 0 if own else 32, 96), 2048.0, ALU.add)
        mm([(R("b6", 0, 32), move(1, h), half("c1h", h)) for h in (0, 1)])
        act(FB, R("b6", 0, 32), bias=mk(16 + t), scale=mk(8 + t))
        act(R("c1f"), R("c1h"), bias=2048.0)
        for k0, k1 in cuts("L"):
            ts(R("c2h", 16 * k0, 16 * k1), IND(Ew, R("L1", k0, k1)), -2048.0, ALU.add)
            for j0, j1 in cuts("LJ"):
                for jq in range(j0, j1):
                    mm([(Q("b4", jq, S_(2 * k0, 2 * k1)), W("WJ%d" % jq, 16 - 2 * h - 4 * il),
                         R("c2h", 16 * k0 + 2 * il + h, 16 * k1, 8)) for h in (0, 1) for il in range(4)])
                ts(Q("L2p", S_(j0, j1), S_(2 * k0, 2 * k1)), Q("b4", S_(j0, j1), S_(2 * k0, 2 * k1)), 2048.0, ALU.add)
            if own or PAR["early"] < 2:
                sub_list("c2h", k0, k1)
        for e, (k0, k1) in zip(PAR["XE"], cuts("X")):
            (act if e == "S" else cp)(R("Xp", 32 * k0, 32 * k1), IND(Xw, R("L1", 32 + 2 * k0, 32 + 2 * k1)))
        tag[0] = "%d.lead" % t
        tt(R("U"), IND(R("IO", 0, V_N), vl), R("cc" if nat else "lq"), ALU.add)
        lo_ = 0 if nat else 4
        for c in range(4):
            act(R("AB", 64 * c, 64 * c + 64), R("U"), ACT.Abs, bias=R("v128", vo + c, vo + c + 1), scale=-1.0)
        for c in range(4):
            act(R("fm", 64 * c, 64 * c + 64), R("AB", 64 * c, 64 * c + 64), ACT.Relu,
                bias=R("lL", 24 + lo_ + c, 25 + lo_ + c), scale=-float(2 ** 18), acc=R("lf", c, c + 1))
        tt(R("lf", 4, 8), R("lf", 0, 4), R("lL", 8 + lo_, 12 + lo_), ALU.min)
        tt(R("lf", 8, 12), R("lf", 4, 8), R("v128", vo, vo + 4), ALU.max)
        ts(R("off"), R("lf", 8, 12), 1.0 / 128, ALU.mult)
        old, was = R("Wd", 8192, 8704), R("X", reg, reg + 512)
        add("Y", 60, lambda g, T, was=was: [g.sync.dma_start(T.Wd[:, 8192:8704], ap(T, was))], [was], [old],
            sig=("cz", 16 * (t + 1)), lat=3000)
        add("G", 1800, lambda g, T: [g.dma_start(T.Wd[:, 8192:8704], T.c128[:], accum_op=ALU.add)], [old, R("c128")], [old],
            sig=("ca", 16 * (t + 1)), lat=3000)
        tag[0] = "%d.main" % t

        def pairs(x, k0, k1):
            h, jq, jl = x // 8, x % 8 // 2, x % 2
            return Q("m", jq, S_(32 * k0 + 2 * h + jl, 32 * k1, 4))
        for k0, k1 in cuts("N"):
            act(R("Gs", 112 * k0, 112 * k1), IND(Xs, R("L2s", 7 * k0, 7 * k1)))
        for c, (k0, k1) in enumerate(cuts("M")):
            zm = R(("b5", "b6")[c % 2], 0, 8 * (k1 - k0))
            for jq in range(4):
                tt(Q("m", jq, S_(32 * k0, 32 * k1)), IND(Xw, Q("L2p", jq, S_(2 * k0, 2 * k1))),
                   R("Xp", 32 * k0, 32 * k1), ALU.min)
                mm([(zm, W("W1", 16 - x), pairs(x, k0, k1)) for x in (2 * jq, 2 * jq + 1, 2 * jq + 8, 2 * jq + 9)],
                   jq == 0, jq == 3)
            dead = R("dead", 8 * k0, 8 * k1)
            sign(PAR["dead"], dead, zm, 71.5, True)
            cand = R(zm[0], 256, 256 + 8 * (k1 - k0))
            mm([(cand, move(1, h, "S"), R("c2h", 16 * k0 + h, 16 * k1, 2)) for h in (0, 1)] + [(cand, R("In"), dead)])
            scan(R("st", 8 * k0, 8 * k1), dead, cand, ALU.min, ALU.max)
            ts(R("subl", k0, k1), R("st", 8 * k0 + 7, 8 * k1, 8), 2048 / A_, ALU.mult)
            act(R("nXs", 16 * k0, 16 * k1), IND(Xs, R("subl", k0, k1)), scale=-1.0)
        nd = [0, 0]
        u, cnt = Q("b7", S_(0, 4), ALL), Q("b1", S_(0, 2), ALL)
        K = Q("b0", S_(0, 2), ALL)
        for c, (k0, k1) in enumerate(cuts("B")):
            n = k1 - k0
            for a in range(k0, k1, 4):
                bk = "b%d" % (nd[0] % 2)
                nd[0] += 1
                whole = Q(bk, S_(0, 28), ALL)
                mm([(whole, R("I"), R("Gs", 112 * a, 112 * a + 448))], True, False)
                mm([(Q(bk, S_(i, 28, 7), ALL), R("I"), R("nXs", 16 * a, 16 * a + 64)) for i in range(7)], False, True)
                act(R("Wd", 112 * a, 112 * a + 448), whole, ACT.Abs)
            zd = Q("b7", S_(k0, k1), ALL)
            mm([(zd, R("Ia"), R("dead", 8 * k0, 8 * k1))]
               + [(Q("b7", S_(k0, k1), S_(0, 7)), W("Wn", 16 - x), R("Wd", 112 * k0 + x, 112 * k1, 16)) for x in range(16)])
            ok = R("ok", 8 * k0, 8 * k1)
            sign(PAR["ok"], ok, zd, 227.5, False)
            per = min(16, 64 // n)
            for x0 in range(0, 16, per):
                bk = "b%d" % (2 + nd[1] % 2)
                nd[1] += 1
                xs = range(x0, x0 + per)
                mm([(R(bk, 8 * n * (x - x0), 8 * n * (x - x0 + 1)), R("I"), pairs(x, k0, k1)) for x in xs], True, False)
                mm([(R(bk, 8 * n * (x - x0), 8 * n * (x - x0 + 1)), W("Sel", 128 * x), ok) for x in xs], False, True)
                scan(Q("Z", x0 // 2 + c, ALL), R("rs8"), R(bk), ALU.mult, ALU.max)
                row = 2 * x0 + 8 * (c // 2)
                gcopy(Q("pc", S_(row, row + 8), S_(k0 % 16, k0 % 16 + 8)), Q("Z", x0 // 2 + c, S_(7, 512, 8)))
        tag[0] = "%d.hash" % t
        for h in (0, 1):
            gcopy(R("Wd", 4096 * h, 4096 * h + 4096, 16), Q("pc", S_(16 * h, 16 * h + 16), ALL))
        for c in (0, 1):
            mm([(u, W("Ww", 16 - 8 * c - y), Q("Z", S_(c, 8, 2), S_(8 * y + 7, 512, 64))) for y in range(8)], c == 0, c == 1)
        ts(h_(0), u, c_(25), ALU.subtract)
        ts(h_(1), h_(0), XW - 1, ALU.bitwise_and)
        ts(h_(2), h_(1), 32.0, ALU.add)
        tt(h_(3), h_(1), h_(2), ALU.mult)
        ts(h_(4), h_(3), 5, ALU.arith_shift_right, XW - 1, ALU.bitwise_and)
        cp(R("hl"), h_(4))
        tag[0] = "%d.stand" % t
        mm([(cnt, R("B8a"), R("dead", i, 256, 8)) for i in range(8)], True, False)
        mm([(cnt, R("B8b"), R("ok", i, 256, 8)) for i in range(8)], False, True)
        ts(R("ns"), cnt, R("thr", t % 2, t % 2 + 1), ALU.is_lt, -float(2 ** 25), ALU.mult)
        sub = R("st", 7, 256, 8)
        mm([(K, R("I"), R("cA")), (K, R("I"), R("cB")), (K, R("I"), R("ns"))], True, False)
        mm([(K, W("W14", 16 - x), Q("Z", S_(x // 8 * 4, x // 8 * 4 + 4), S_(x % 8 * 64 + 7, x % 8 * 64 + 64, 8))) for x in range(16)]
           + [(K, move(h, h, "K"), sub) for h in (0, 1)], False, True)
        ts(R("SF"), K, 0.0, ALU.is_ge)
        tt(key, K, FB, ALU.max)
        tag[0] = "%d.ask" % t
        Y = Q("b1", S_(2, 4), ALL)
        mm([(Y, R("I4k"), R("SF"))], True, False)
        for x0, x1 in cuts("D"):
            tt(R("dd", 32 * x0, 32 * x1), IND(Xw, R("hl", 2 * x0, 2 * x1)), R("Wd", 512 * x0, 512 * x1, 16), ALU.subtract)
            act(Q("ad", S_(2 * x0, 2 * x1), ALL), R("dd", 32 * x0, 32 * x1), ACT.Abs, bias=128.0)
            mm([(Y, W("W1", 16 - x), Q("ad", S_(2 * x0 + x % 8, 2 * x1, 8), ALL)) for x in range(x0, x1)], False, x1 == 16)
        ts(R("ask"), Y, 4096 + 28.5, ALU.is_gt)
        tag[0] = "%d.rec" % t
        for a, b in ((0, 16), (16, 32)):
            got = IND(R("XR", XW * t, XW * (t + 1)), R("hl", a, b))
            if PAR["rec"] == "S":
                me = ops[act(R("sm", 16 * a, 16 * b), got)]
            else:
                me = ops[tt(R("sm", 16 * a, 16 * b), got, R("Wd", 256 * a, 256 * b, 16), ALU.add)]
            me["ext"] = [("arr%d" % t, 16)] if a == 0 else []
            me["deps"][sent if a == 0 else len(ops) - 2] = True
        if PAR["rec"] == "S":
            mm([(Q("b0", ALL, ALL), R("I"), pi_), (Q("b0", ALL, ALL), R("I"), R("sm"))])
        act(R("Wd", 1, 8192, 16), Q("b0", ALL, ALL) if PAR["rec"] == "S" else R("sm"), bias=63.75, scale=0.5)
        tag[0] = "%d.go" % t
        turn(tr, key)
        scan(top, R("rs8", 0, 32), tr, ALU.mult, ALU.max)
        cp(R("gi", 0, 4), R("tf", 64 + 7, 96, 8))
        ts(R("gi", 4, 8), R("gi", 0, 4), 2047, ALU.bitwise_and)
        cp(R("gh"), R("gi", 4, 8))
        mm([(R("b2", kk, 4, 2), W("G%d" % kk, 16 - 16 * gp), R("gh", 2 * gp, 2 * gp + 2)) for kk in (0, 1) for gp in (0, 1)])
        if not last:
            cp(R("vL", vn, vn + 4), R("b2", 0, 4))
            act(R("v128", vn, vn + 4), R("b2", 0, 4), scale=128.0)
            mm([(R("b3", 0, 32), R("one"), R("ns"))])
            act(R("af", 0, 32), R("b3", 0, 32), scale=-1.0 / 2 ** 28, acc=R("af", 32, 33))
            cp(R("gi", 8, 9), R("af", 32, 33))
            ts(R("gi", 9, 10), R("gi", 8, 9), 7, ALU.bitwise_and)
            ts(R("thr", 1 - t % 2, 2 - t % 2), R("gi", 9, 10), -2.0 * A_, ALU.mult, -31.0 * A_, ALU.add)
        else:
            ts(R("P0"), R("D1"), c_(26), ALU.is_equal)
            ts(R("P1"), R("D1"), c_(27), ALU.is_equal)
            cp(R("yvs", 0, 4), R("b2", 0, 4))
            mm([(R("b3", b, 4, 2), W("P%d" % b, 1 - h), R("yvs", 2 * h, 2 * h + 2)) for b in (0, 1) for h in (0, 1)])
            act(R("yvs", 4, 8), R("b3", 0, 4))
            dma("Y", "st0", lambda g, T: [g.sync.dma_start(T.yv[:], T.yvs[:, 4:8])], [R("yvs", 4, 8)], [], 2048)
        tag[0] = "%d.name" % t
        ts(R("hT"), h_(4), -2048.0, ALU.add)
        turn(R("hR"), R("hT"))

        def hashed(bk):
            return [(R(bk, 32 * kh + h, 32 * kh + 32, 2) if nat else R(bk, 32 * h + 16 * kh, 32 * h + 16 * kh + 16),
                     W("WH%d" % (2 * h + kh), 16 - 16 * gp), R("hR", 16 * gp, 16 * gp + 16))
                    for h in (0, 1) for kh in (0, 1) for gp in (0, 1)]
        subs = [(R("b6", 0, 64), R("N16"), R("c1h"))] + [(half("b6", h), move(h, 1, "K"), sub) for h in (0, 1)]
        mm([(half("b4", h, 0), move(h, d), R("SF")) for h in (0, 1) for d in (0, 1)])
        if PAR["early"] and not last:
            tag[0] = "%d.early" % t
            mm(subs)
            act(R("Ds"), R("b6", 0, 64), bias=c_(24))
            tt(R("m1"), Q("b4", 0, ALL), R("Ds"), ALU.mult)
            tt(IND(R("Es", 0, V_N + 64), R("off")), R("m1"), R("c1f"), ALU.add)
            ts(R("c1e"), IND(R("Es", 0, V_N), R("vL", vn, vn + 4)), -2048.0, ALU.add)
            mm([(R("b3", 0, 32), W("RS", 1 - h), R("c1e", 32 * h, 32 * h + 32)) for h in (0, 1)])
            ts(R("L1", 0, 32), R("b3", 0, 32), 2048.0, ALU.add)
            if PAR["early"] == 2:
                for k0, k1 in cuts("LE"):
                    ts(R("c2e", 16 * k0, 16 * k1), IND(R("Es", 0, V_N), R("L1", k0, k1)), -2048.0, ALU.add)
                    sub_list("c2e", k0, k1)
            tag[0] = "%d.name" % t
        mm(subs, True, False)
        mm(hashed("b6"), False, True)
        act(R("De"), R("b6", 0, 64), bias=c_(24))
        mm([(R("b5", 0, 64), R("I16"), R("nn", 0, 64) if nat else R("nn", 64, 128))] + hashed("b5"))
        act(R("NH"), R("b5", 0, 64), bias=mk(48 + t % 4), scale=-1.0)
        tt(R("m12"), Q("b4", 0, ALL), R("De"), ALU.mult)
        tt(R("base"), R("m12"), R("c1f"), ALU.add)
        mm([(half("b4", h, 1), move(h, 0), R("ask")) for h in (0, 1)])
        tt(R("m3"), Q("b4", 1, ALL), R("NH"), ALU.mult)
        tt(IND(R("E", 0, V_N + 64), R("off")), R("base"), R("m3"), ALU.add)
        if last:
            dma("Y", "st1", lambda g, T: [g.sync.dma_start(T.ye[:], T.E[:, 0:V_N])], [R("E", 0, V_N)], [], 786432)
        tag[0] = "%d.pick" % t
        scan(R("cum"), R("on16"), R("ask"), ALU.mult, ALU.add)
        ix = R("b2", 32, 64)
        mm([(ix, R("I16"), R("n16")), (ix, R("Db"), R("ask")), (ix, R("TLq"), R("ask"))]
           + [(R("b2", 32 + 16 * kh, 48 + 16 * kh), R("Da%d" % kh), R("ask", 16 * kh, 16 * kh + 16)) for kh in (0, 1)], True, False)
        mm([(ix, R("Bn"), R("cum"))], False, True)
        ts(R("idx"), ix, 8192 + 511 / 1024, ALU.add)
        n = len(PAR["pick"])
        for p, e in enumerate(PAR["pick"]):
            a, b = 32 * p // n, 32 * (p + 1) // n
            new, src = R("X", reg + 16 * a, reg + 16 * b), IND(R("Wd", 0, 8704), R("idx", a, b))
            if e == "S":
                act(new, src, bias=-128.0)
            else:
                ts(new, src, -128.0, ALU.add)
        if t == RO - 2:
            nx = 1024 * ((t + 1) % 4)
            dma("Y", "st2", lambda g, T, nx=nx: [g.sync.dma_start(T.yx[:, 0:nx], T.X[:, 0:nx])], [R("X", 0, nx)], [], 262144)
            dma("Y", "st3", lambda g, T, nx=nx: [g.sync.dma_start(T.yx[:, nx + 512:XW], T.X[:, nx + 512:XW])],
                [R("X", nx + 512, XW)], [], 655360)
        if last:
            dma("S", "st4", lambda g, T, reg=reg: [g.scalar.dma_start(T.yx[:, reg:reg + 512], T.X[:, reg:reg + 512])],
                [R("X", reg, reg + 512)], [], 131072)
    return ops


def links(ops, cm):
    return [[(d, ops[d]["lat"] if ops[d]["sig"] is not None else cm["x"] if ops[d]["eng"] != o["eng"] else cm["same"] if raw else 0)
             for d, raw in o["deps"].items()] for o in ops]


def place(seq, before, cost, eng, start):
    end = [0.0] * len(cost)
    busy = {e: [] for e in "VSPGY"}
    for i in seq:
        at = start[i]
        for d, g in before[i]:
            if end[d] + g > at:
                at = end[d] + g
        row = busy[eng[i]]
        n = len(row)
        while n > 0 and row[n - 1][1] > at:
            n -= 1
        while n < len(row) and row[n][0] < at + cost[i]:
            at = max(at, row[n][1])
            n += 1
        row.insert(n, (at, at + cost[i]))
        end[i] = at + cost[i]
    return end


def length(order, before, cost, eng, lat):
    free = {e: 0.0 for e in "VSPGY"}
    end = [0.0] * len(cost)
    last = 0.0
    for i in order:
        at = free[eng[i]]
        for d, g in before[i]:
            if end[d] + g > at:
                at = end[d] + g
        end[i] = free[eng[i]] = at + cost[i]
        last = max(last, end[i] + lat[i])
    return last, end


def schedule(ops):
    n = len(ops)
    cost, eng, lat = [o["cost"] for o in ops], [o["eng"] for o in ops], [o["lat"] for o in ops]
    before = links(ops, CM)
    for i in (1, 2, 3):
        before[i].append((i - 1, 0))
    after = [[] for _ in range(n)]
    for i in range(n):
        for d, g in before[i]:
            after[d].append((i, g))
    rest = [0.0] * n
    for i in range(n - 1, -1, -1):
        rest[i] = cost[i] + max([g + rest[s] for s, g in after[i]] + [lat[i]])
    key = [-r for r in rest]
    rng = np.random.RandomState(1)
    best, top, now = None, 1e30, 1e30
    for it in range(PAR["tries"]):
        shake = rng.normal(0, (30, 120, 400)[it % 3], n) * (rng.rand(n) < 0.3) * (it > 0)
        k = [key[i] + shake[i] for i in range(n)]
        for i in range(n):
            for d, g in before[i]:
                if k[i] <= k[d]:
                    k[i] = k[d] + 1e-3
        end = place(sorted(range(n), key=lambda q: k[q]), before, cost, eng, [0.0] * n)
        end = place(sorted(range(n), key=lambda q: -end[q]), after, cost, eng, lat)
        end = place(sorted(range(n), key=lambda q: -end[q]), before, cost, eng, [0.0] * n)
        order = sorted(range(n), key=lambda q: (end[q] - cost[q], q))
        v = length(order, before, cost, eng, lat)[0]
        if v < now + 150:
            now, key = v, [end[q] - cost[q] for q in range(n)]
            if v < top:
                top, best = v, order
                for q in range(n):
                    ops[q]["at"] = key[q]
    return best


def refine(ops):
    n = len(ops)
    eng = [o["eng"] for o in ops]
    base, views = dict(CM), []
    for w, m in VIEWS:
        CM.update(m)
        o = build()
        views.append((w, links(o, CM), [q["cost"] for q in o], [q["lat"] for q in o]))
        CM.update(base)
    for v in views:
        for i in (1, 2, 3):
            v[1][i].append((i - 1, 0))
    before, cost, lat = views[0][1:]
    ids, rnd, seen = [], [], {}
    for o in ops:
        nm = o["name"] + o["eng"]
        t = int(nm[0]) if nm[0].isdigit() else -1
        seen[nm] = seen.get(nm, 0) + 1
        ids.append((nm[1:], seen[nm]))
        rnd.append(t)
    schedule(ops)
    at = [o["at"] for o in ops]
    span = (max(at[i] for i in range(n) if rnd[i] == 4) - max(at[i] for i in range(n) if rnd[i] == 1)) / 3
    shift = [max(t, 0) * span for t in rnd]
    key = {}
    for t in (5, 4, 0, -1, 2):
        key.update({ids[i]: at[i] - shift[i] for i in range(n) if rnd[i] == t})

    def weigh(key):
        k = [key[ids[i]] + shift[i] for i in range(n)]
        for i in range(n):
            for d, g in before[i]:
                if k[i] <= k[d]:
                    k[i] = k[d] + 1e-3
        order = sorted(range(n), key=lambda q: k[q])
        res = [length(order, b, c, eng, l) for w, b, c, l in views]
        return sum(v[0] * r[0] for v, r in zip(views, res)), order, k, res[0][1]

    def chain(order, end):
        prev, last = {}, {}
        for i in order:
            prev[i] = last.get(eng[i])
            last[eng[i]] = i
        i = max(range(n), key=lambda q: end[q] + lat[q])
        res = []
        while True:
            start, p = end[i] - cost[i], prev[i]
            if p is not None and abs(end[p] - start) < 1e-6:
                res.append((p, i))
                i = p
                continue
            x = [d for d, g in before[i] if abs(end[d] + g - start) < 1e-6]
            if not x:
                return res
            i = x[0]
    rng = np.random.RandomState(PAR["seed"])
    now, order, k, end = weigh(key)
    top, best = now, (order, end)
    pairs = chain(order, end)
    for it in range(PAR["swaps"]):
        a, b = pairs[rng.randint(len(pairs))]
        new = dict(key)
        r = rng.rand()
        if r < 0.4:
            new[ids[b]] = k[a] - shift[b] - 1 - 300 * rng.rand() ** 3
        elif r < 0.8:
            new[ids[a]] = k[b] - shift[a] + 1 + 1500 * rng.rand() ** 3
        else:
            new[ids[rng.randint(n)]] += rng.normal(0, 600)
        v, o2, k2, e2 = weigh(new)
        if v < now - (125 * (1 - it / PAR["swaps"]) + 5) * np.log(rng.rand() + 1e-9):
            key, k, now, order, end = new, k2, v, o2, e2
            pairs = chain(order, end)
            if v < top:
                top, best = v, (o2, e2)
    for i in range(n):
        ops[i]["at"] = best[1][i] - cost[i]
    return best[0]


VIEWS = [(1.0, {})]


def plan():
    ops = build()
    order = refine(ops)
    cnt = {e: 0 for e in COUNTER}
    known = {e: {} for e in "VSPGY"}
    seen = {}
    for i in order:
        o = ops[i]
        e = o["eng"]
        need = {}
        for d, raw in o["deps"].items():
            p = ops[d]
            if p["sig"] is None and p["eng"] == e and not raw:
                continue
            s, v = p["done"]
            if v > need.get(s, (0, None))[0]:
                need[s] = (v, d)
        waits = []
        for s, (v, d) in sorted(need.items(), key=lambda q: -ops[q[1][1]]["at"]):
            if known[e].get(s, 0) < v:
                waits.append((s, v))
                for s2, v2 in ops[d]["vc"].items():
                    known[e][s2] = max(known[e].get(s2, 0), v2)
        waits += list(o["ext"])
        for s, v in waits:
            seen[s] = max(seen.get(s, 0), v)
        o["waits"] = waits
        if o["sig"] is None:
            cnt[e] += 1
            o["done"] = (COUNTER[e], cnt[e])
        else:
            o["done"] = o["sig"]
        o["vc"] = dict(known[e])
        o["vc"][o["done"][0]] = o["done"][1]
    final = {}
    for o in ops:
        s, v = o["done"]
        final[s] = max(final.get(s, 0), v)
    tail = [(s, v) for s, v in final.items() if seen.get(s, 0) < v]
    return ops, order, tail


PLAN = []


def rank_program(g, core, T, topo):
    rank = T.rank_of(core)
    if rank is None:
        return
    if not PLAN:
        PLAN.append(plan())
    ops, order, tail = PLAN[0]
    queue = {"V": g.vector, "S": g.scalar, "P": g.tensor, "G": g, "Y": g.sync}
    for i in order:
        o = ops[i]
        for s, v in o["waits"]:
            queue[o["eng"]].wait_ge(T.sem[s], v * wide(s, core, T, topo))
        for ins in o["emit"](g, T):
            if isinstance(ins, tuple):
                t = ins[1]
                dst = T.cores[(rank - 1 - t % (NR - 1)) % NR]
                rid, pid, _ = topo.addr(dst)
                g.remote_dma(T.XR[:, XW * t:XW * (t + 1)], T.X[:], T.sem["arr%d" % t], T.sem["snt%d" % t],
                             pid, rid, topo.mask(core, dst))
            else:
                ins.then_inc(T.sem[o["done"][0]], 1 if o["sig"] is None else 16)
    for s, v in tail:
        g.wait_ge(T.sem[s], v * wide(s, core, T, topo))


def wide(s, core, T, topo):
    if s[:3] not in ("snt", "arr"):
        return 1
    t = int(s[3:])
    rank = T.rank_of(core)
    step = 1 + t % (NR - 1)
    if s[:3] == "snt":
        return len(topo.engines(core, T.cores[(rank - step) % NR])) // 16
    return len(topo.engines(T.cores[(rank + step) % NR], core)) // 16
